import numpy as np
import ml_dtypes


def mxq(x, axis, fmt="e4m3"):
    dtype, down = {"e4m3": (ml_dtypes.float8_e4m3fn, 7), "e5m2": (ml_dtypes.float8_e5m2, 14)}[fmt]
    v = np.moveaxis(np.asarray(x, np.float32).astype(ml_dtypes.bfloat16).astype(np.float64), axis, -1)
    blocks = v.reshape(v.shape[:-1] + (-1, 32))
    amax = np.abs(blocks).max(-1, keepdims=True)
    byte = np.maximum(np.where(amax > 0, np.frexp(amax)[1] - 1 + 127, 0) - down, 1)
    scale = np.exp2(byte - 127.0)
    codes = (blocks / scale).astype(np.float32).astype(dtype).astype(np.float64)
    return np.moveaxis((codes * scale).reshape(v.shape), -1, axis)


WIDE = False


def mx_kscale(k):
    if not WIDE:
        return np.ones(k)
    levels = np.array([24, -24, 12, -12, 0])
    if k % 512:
        return np.exp2(np.random.permutation(np.resize(levels, k // 32))).repeat(32)
    a = np.empty((k // 512, 16))
    for p in range(k // 512):
        a[p, :8] = np.random.permutation(np.resize(levels, 8))
        for g in range(8):
            far = levels[np.abs(levels - a[p, g]) >= 10]
            a[p, g + 8] = far[np.random.randint(len(far))]
    return np.exp2(a.ravel()).repeat(32)


def f64(x):
    return np.asarray(x).astype(np.float64)


def striped(idx):
    return np.tile(idx.reshape(-1, 16).T, (8, 1)).astype(np.uint16)


def unstriped(offs):
    return offs[:16].T.reshape(-1).astype(np.int64)


E2M1 = np.array([0.0, 0.5, 1.0, 1.5, 2.0, 3.0, 4.0, 6.0, -0.0, -0.5, -1.0, -1.5, -2.0, -3.0, -4.0, -6.0])


def pack_weight(w, fmt):
    k, n = w.shape
    w = f64(np.asarray(w, np.float32).astype(ml_dtypes.bfloat16)).reshape(k // 32, 32, n)
    amax = np.abs(w).max(1)
    if fmt == "e4m3":
        byte = np.frexp(amax)[1] - 1 + 127 - 7
    else:
        mant, ex = np.frexp(amax / 6.0)
        byte = np.where(mant > 0.5, ex, ex - 1) + 127
    byte = np.clip(np.where(amax > 0, byte, 1), 1, 254)
    scaled = (w * np.exp2(127.0 - byte)[:, None, :]).reshape(k, n).astype(np.float32)
    by_word = np.ascontiguousarray(scaled.reshape(k // 512, 128, 4, n).transpose(0, 1, 3, 2))
    if fmt == "e4m3":
        words = by_word.astype(ml_dtypes.float8_e4m3fn).view(np.uint8)
    else:
        c = by_word.astype(ml_dtypes.float4_e2m1fn).view(np.uint8) & 0xF
        words = (c[..., 0::2] | (c[..., 1::2] << 4)).reshape(k // 512, 128, 2 * n)
    return np.ascontiguousarray(words), np.ascontiguousarray(byte.astype(np.uint8).reshape(k // 512, 16, n))


def unpack_weight(words, scales, fmt):
    g, _, n = scales.shape
    words = np.ascontiguousarray(words).reshape(g, 128, n, -1)
    if fmt == "e4m3":
        vals = words.view(ml_dtypes.float8_e4m3fn).astype(np.float64)
    else:
        nib = np.empty((g, 128, n, 4), np.uint8)
        nib[..., 0::2] = words & 0xF
        nib[..., 1::2] = words >> 4
        vals = E2M1[nib]
    vals = vals * np.repeat(np.exp2(scales.astype(np.float64) - 127.0), 8, axis=1)[..., None]
    return vals.transpose(0, 1, 3, 2).reshape(g * 512, n)


def pack_table4(v):
    words, scales = pack_weight(v, "e2m1")
    g, t = words.shape[0] // 2, v.shape[1]
    return np.ascontiguousarray(words.reshape(g, 2, 128, t, 2).transpose(0, 2, 3, 1, 4).reshape(g, 128, t, 4)), scales


def unpack_table4(words, scales):
    g, _, t, _ = words.shape
    return unpack_weight(words.reshape(g, 128, t, 2, 2).transpose(0, 3, 1, 2, 4).reshape(2 * g, 128, 2 * t), scales, "e2m1")


def split(x):
    m, e = np.frexp(f64(x))
    hi = np.ldexp(np.trunc(16.0 * m) / 16.0, e)
    return hi, f64(x) - hi


K, L, N, T, J = 1024, 512, 512, 2048, 512


def setup_inputs():
    n = np.random.standard_normal
    s = mx_kscale(K)[:, None]
    s2 = mx_kscale(L)[:, None]
    p_tab = pack_table4(n((K, T)) * s)
    return {
        "tab_words": p_tab[0],
        "tab_scales": p_tab[1],
        "w": (n((K, N)) / np.sqrt(K) / s).astype(np.float32),
        "x": (n((L, J)) * s2).astype(np.float32),
        "wx": (n((L, N)) / np.sqrt(L) / s2).astype(np.float32),
        "iw0": (np.random.uniform(0.1, 0.6, J)).astype(np.float32),
        "iw1": (np.random.uniform(0.1, 0.6, J)).astype(np.float32),
        "iw2": (np.random.uniform(0.1, 0.6, J)).astype(np.float32),
        "res": (n((N, J))).astype(np.float32),
        "offs": striped(np.concatenate([np.random.permutation(T)[:J] for _ in range(3)])),
    }


def reference(tab_words, tab_scales, w, x, wx, iw0, iw1, iw2, res, offs):
    idx = unstriped(offs).reshape(3, J)
    tab_ = unpack_table4(tab_words, tab_scales)[:, idx]
    w_ = mxq(f64(w), 0, "e4m3")
    a0 = w_.T @ tab_[:, 0]
    a1 = w_.T @ tab_[:, 1]
    a2 = w_.T @ tab_[:, 2]
    x_ = mxq(f64(x), 0, "e4m3")
    wx_hi, wx_lo = split(wx)
    wx_hi_, wx_lo_ = mxq(wx_hi, 0, "e4m3"), mxq(wx_lo, 0, "e4m3")
    ax = wx_hi_.T @ x_ + wx_lo_.T @ x_
    return a0 * f64(iw0)[None, :] + a1 * f64(iw1)[None, :] + a2 * f64(iw2)[None, :] + ax + f64(res)

@@ -1,0 +1,229 @@
+from contextlib import ExitStack
+
+import concourse.mybir as mybir
+
+K, L, N, T, J = 1024, 512, 512, 2048, 512
+G = 3
+FLOPS = 2 * N * J * (G * K + 2 * L)
+
+F32 = mybir.dt.float32
+BF16 = mybir.dt.bfloat16
+I32 = mybir.dt.int32
+U32 = mybir.dt.uint32
+U16 = mybir.dt.uint16
+U8 = mybir.dt.uint8
+FP8X4 = mybir.dt.float8_e4m3fn_x4
+FP4X4 = mybir.dt.float4_e2m1fn_x4
+ALU = mybir.AluOpType
+COPY = mybir.ActivationFunctionType.Copy
+
+P = 128
+H = 256
+HI_MASK = -983056
+
+
+def tile_list_interp_hl_res_kernel(tc, tab_words, tab_scales, w, x, wx, iw0, iw1, iw2, res, offs, out):
+    nc = tc.nc
+    with ExitStack() as ctx:
+        keep = ctx.enter_context(tc.tile_pool(name="keep", bufs=1))
+        placed = ctx.enter_context(tc.tile_pool(name="placed", bufs=1))
+        psum = ctx.enter_context(tc.psum_pool(name="psum", bufs=1))
+
+        def sb(name, shape, dtype, tag=None):
+            return keep.tile(shape, dtype, name=name, tag=tag or name, align_bytes=64)
+
+        def at(name, shape, dtype, offset):
+            return placed.tile(shape, dtype, name=name, offset=offset, align_bytes=64)
+
+        offsets = keep.tile([P, G * J // 16], U16, name="offsets")
+        nc.sync.dma_start(offsets[:], offs)
+
+        def load_rows(raw, rows, c0, c1):
+            nc.sync.dma_start(raw[:, :, :], rows.rearrange("(p t) c -> p t c", t=4)[:, :, c0:c1])
+            return raw
+
+        def half(both, h):
+            return both[:, h * 4 * H : (h + 1) * 4 * H].rearrange("p (t c) -> p t c", t=4)
+
+        scale_tab = sb("scale_tab", [P, T], U8)
+        nc.gpsimd.memset(scale_tab[:].bitcast(I32), 0)
+        for q in range(4):
+            nc.sync.dma_start(scale_tab[32 * q : 32 * q + 8, :].bitcast(I32), tab_scales[:, 4 * q : 4 * q + 4, :].bitcast(I32))
+
+        ident = sb("ident", [P, P], F32)
+        for c0, c1, edge in ((0, 64, 8192), (64, 96, 24576), (96, 128, 26112)):
+            zeros = at("zeros%d" % c0, [P, c1 - c0], F32, edge - 64)
+            nc.gpsimd.memset(zeros[:], 0.0)
+            nc.gpsimd.affine_select(
+                out=ident[:, c0:c1], in_=zeros[:], compare_op=ALU.not_equal, fill=1.0,
+                base=-c0, pattern=[[-1, c1 - c0]], channel_multiplier=1,
+            )
+
+        w0_both = at("w0_raw", [P, 8 * H], F32, 0)
+        w0_raw = [load_rows(half(w0_both, 0), w[0:512, :], 0, H)]
+        word_tab = at("word_tab", [P, T], I32, 8192)
+        nc.sync.dma_start(word_tab[:], tab_words[0].rearrange("p t b -> p (t b)").bitcast(I32))
+        w0_raw.append(load_rows(half(w0_both, 1), w[0:512, :], H, N))
+        w1_both = at("w1_raw", [P, 8 * H], F32, 16384)
+        w1_raw = [load_rows(half(w1_both, h), w[512:1024, :], h * H, (h + 1) * H) for h in range(2)]
+        iw_rows = at("iw_rows", [P, P], F32, 26112)
+        nc.gpsimd.memset(iw_rows[:], 0.0)
+        for g, iw in enumerate((iw0, iw1, iw2)):
+            nc.gpsimd.dma_start(iw_rows[4 * g : 4 * g + 4, :], iw.rearrange("(c j) -> c j", c=4))
+
+        scales_p0 = sb("scales_p0", [P, G * J], U8)
+        nc.vector.tensor_copy(scales_p0[:], scale_tab[:].indirect(offsets[:]))
+        scales_p1 = at("scales_p1", [P, G * J], U8, 24576)
+        nc.vector.memset(scales_p1[:].bitcast(I32), 0)
+        nc.sync.dma_start(scales_p1[0:100, :].bitcast(I32), scales_p0[4:104, :].bitcast(I32))
+        tab_planes = (scales_p0, scales_p1)
+
+        def weave(name, raw_cols):
+            width = raw_cols.shape[2]
+            woven = sb(name, [P, width, 4], BF16)
+            nc.scalar.activation(
+                woven[:].rearrange("p (c i) t -> p c t i", i=4),
+                raw_cols.rearrange("p t (c i) -> p c t i", i=4),
+                COPY,
+            )
+            return woven
+
+        def quantize(woven, codes, plane):
+            nc.vector.quantize_mx(out=codes.bitcast(FP8X4), scales=plane, in_=woven[:].rearrange("p c t -> p (c t)"))
+
+        def gather(pairs, g, h):
+            c0 = (g * J + h * H) // 16
+            nc.vector.tensor_copy(pairs, word_tab[:].bitcast(U32).indirect(offsets[:, c0 : c0 + H // 16]))
+
+        def part(name, pairs):
+            width = pairs.shape[1]
+            parted = sb(name, [P, 2, 2 * width], U8)
+            nc.vector.tensor_copy(parted[:].bitcast(U16), pairs.bitcast(U16).rearrange("p (j d) -> p d j", d=2))
+            return parted
+
+        w_codes = [sb("w_codes%d" % a, [P, N], U32) for a in range(2)]
+        w_plane = [sb("w_plane%d" % a, [P, N], U8) for a in range(2)]
+
+        def quantize_w(a, woven):
+            for h in range(2):
+                quantize(woven[h], w_codes[a][:, h * H : (h + 1) * H], w_plane[a][:, h * H : (h + 1) * H])
+
+        words = {}
+        w0_woven = [weave("w0_woven%d" % h, w0_raw[h]) for h in range(2)]
+        pairs0 = at("pairs0", [P, G * H], U32, 26624 + 4096 - 1536)
+        for g in range(G):
+            gather(pairs0[:, g * H : (g + 1) * H], g, 0)
+        parted0 = part("parted0", pairs0[:])
+        for g in range(G):
+            words[g, 0] = parted0[:, :, 2 * g * H : 2 * (g + 1) * H]
+        wx_raw = [load_rows(at("wx_raw%d" % h, [P, 4, H], F32, 26624 + 4096 * h), wx, h * H, (h + 1) * H) for h in range(2)]
+        quantize_w(0, w0_woven)
+        x_both = at("x_raw", [P, 8 * H], F32, 0)
+        x_raw = [load_rows(half(x_both, h), x, h * H, (h + 1) * H) for h in range(2)]
+
+        def second_half(g, tag):
+            pairs = sb("pairs1_%d" % g, [P, H], U32, tag)
+            gather(pairs[:], g, 1)
+            words[g, 1] = part("parted1_%d" % g, pairs[:])[:]
+
+        w1_woven = [weave("w1_woven%d" % h, w1_raw[h]) for h in range(2)]
+        res_sb = at("res_sb", [P, 4, J], F32, 16384)
+        nc.sync.dma_start(res_sb[:], res.rearrange("(c p) j -> p c j", p=P))
+        second_half(0, "w0_woven1")
+        quantize_w(1, w1_woven)
+        second_half(1, "w1_woven0")
+        second_half(2, "w1_woven1")
+
+        iw_ps = psum.tile([P, P], F32, name="iw_ps", tag="turned3")
+        nc.tensor.transpose(iw_ps[:], iw_rows[:], ident[:])
+        iw_cols = sb("iw_cols", [P, 16], F32)
+        nc.scalar.activation(iw_cols[:], iw_ps[:, 0:16], COPY)
+
+        part_codes = [sb("part_codes%d" % s, [P, N], U32) for s in range(2)]
+        part_plane = [sb("part_plane%d" % s, [P, N], U8) for s in range(2)]
+        for h in range(2):
+            top = sb("top%d" % h, [P, H, 4], BF16)
+            wx_top = wx_raw[h][:].bitcast(BF16).rearrange("p t (c i e) -> p c t i e", i=4, e=2)[:, :, :, :, 1]
+            nc.scalar.copy(top[:].rearrange("p (c i) t -> p c t i", i=4), wx_top)
+            hi = sb("hi%d" % h, [P, H, 4], BF16)
+            nc.vector.tensor_scalar(
+                hi[:].rearrange("p c t -> p (c t)").bitcast(I32),
+                top[:].rearrange("p c t -> p (c t)").bitcast(I32),
+                HI_MASK, None, ALU.bitwise_and,
+            )
+            lo = sb("lo%d" % h, [P, H, 4], BF16)
+            nc.vector.tensor_tensor(lo[:], wx_raw[h][:].rearrange("p t c -> p c t"), hi[:], ALU.subtract)
+            cols = slice(h * H, (h + 1) * H)
+            quantize(hi, part_codes[0][:, cols], part_plane[0][:, cols])
+            quantize(lo, part_codes[1][:, cols], part_plane[1][:, cols])
+        x_codes = [sb("x_codes%d" % h, [P, H], U32) for h in range(2)]
+        x_plane = [sb("x_plane%d" % h, [P, H], U8) for h in range(2)]
+        for h in range(2):
+            quantize(weave("x_woven%d" % h, x_raw[h]), x_codes[h][:], x_plane[h][:])
+
+        used = []
+
+        def next_bank(name, shape):
+            used.append(name)
+            return psum.tile(shape, F32, name=name, tag="acc%d" % (len(used) % 4))
+
+        def look_up(jt):
+            h, u = divmod(jt, 2)
+            turned = psum.tile([P, 4, P], F32, name="turned%d" % jt, tag="turned%d" % jt)
+            for g in range(G):
+                bank = next_bank("a%d_%d" % (g, jt), [P, N])
+                s0 = g * J + jt * P
+                for a in range(2):
+                    nc.tensor.matmul_mx(
+                        out=bank[:],
+                        lhsT=words[g, h][:, a, 2 * u * P : 2 * (u + 1) * P].bitcast(FP4X4),
+                        lhsT_scale=tab_planes[a][:, s0 : s0 + P],
+                        rhs=w_codes[a][:].bitcast(FP8X4),
+                        rhs_scale=w_plane[a][:],
+                        start=(a == 0),
+                        stop=(a == 1),
+                    )
+                scaled = sb("scaled%d_%d" % (g, jt), [P, N], F32)
+                nc.scalar.activation(scaled[:], bank[:], COPY, scale=iw_cols[:, 4 * g + jt : 4 * g + jt + 1])
+                for c in range(4):
+                    nc.tensor.matmul(
+                        turned[:, c, :], scaled[:, c * P : (c + 1) * P], ident[:],
+                        start=(g == 0 and c == 0), stop=(g == G - 1 and c == 3), is_transpose=True,
+                    )
+            return turned
+
+        def skip_half(h):
+            own = sb("own%d" % h, [P, 4, H], F32)
+            for cp in range(2):
+                bank = next_bank("ax%d_%d" % (h, cp), [P, 2, H])
+                for e in range(2):
+                    c = 2 * cp + e
+                    for s in range(2):
+                        nc.tensor.matmul_mx(
+                            out=bank[:, e, :],
+                            lhsT=part_codes[s][:, c * P : (c + 1) * P].bitcast(FP8X4),
+                            lhsT_scale=part_plane[s][:, c * P : (c + 1) * P],
+                            rhs=x_codes[h][:].bitcast(FP8X4),
+                            rhs_scale=x_plane[h][:],
+                            start=(s == 0),
+                            stop=(s == 1),
+                        )
+                nc.vector.tensor_tensor(own[:, 2 * cp : 2 * cp + 2, :], bank[:], res_sb[:, 2 * cp : 2 * cp + 2, h * H : (h + 1) * H], ALU.add)
+            return own
+
+        out_rows = out.rearrange("(c p) j -> p c j", p=P)
+
+        def finish(jt, turned, own):
+            u = jt % 2
+            done = sb("done%d" % jt, [P, 4, P], F32)
+            nc.vector.tensor_tensor(done[:], turned[:], own[:, :, u * P : (u + 1) * P], ALU.add)
+            nc.sync.dma_start(out_rows[:, :, jt * P : (jt + 1) * P], done[:])
+
+        turned = [look_up(jt) for jt in range(3)]
+        own0 = skip_half(0)
+        finish(0, turned[0], own0)
+        finish(1, turned[1], own0)
+        turned.append(look_up(3))
+        own1 = skip_half(1)
+        finish(2, turned[2], own1)
+        finish(3, turned[3], own1)

@@ -45,8 +45,10 @@ def tile_list_interp_hl_res_kernel(tc, tab_words, tab_scales, w, x, wx, iw0, iw1
         def half(both, h):
             return both[:, h * 4 * H : (h + 1) * 4 * H].rearrange("p (t c) -> p t c", t=4)
 
+        w0_raw = [load_rows(at("w0_raw0", [P, 4, H], F32, 0), w[0:512, :], 0, H)[:]]
+
         scale_tab = sb("scale_tab", [P, T], U8)
-        nc.gpsimd.memset(scale_tab[:].bitcast(I32), 0)
+        nc.vector.memset(scale_tab[:].bitcast(I32), 0)
         for q in range(4):
             nc.sync.dma_start(scale_tab[32 * q : 32 * q + 8, :].bitcast(I32), tab_scales[:, 4 * q : 4 * q + 4, :].bitcast(I32))
 
@@ -59,11 +61,9 @@ def tile_list_interp_hl_res_kernel(tc, tab_words, tab_scales, w, x, wx, iw0, iw1
                 base=-c0, pattern=[[-1, c1 - c0]], channel_multiplier=1,
             )
 
-        w0_both = at("w0_raw", [P, 8 * H], F32, 0)
-        w0_raw = [load_rows(half(w0_both, 0), w[0:512, :], 0, H)]
+        w0_raw.append(load_rows(at("w0_raw1", [P, 4, H], F32, 4096), w[0:512, :], H, N)[:])
         word_tab = at("word_tab", [P, T], I32, 8192)
         nc.sync.dma_start(word_tab[:], tab_words[0].rearrange("p t b -> p (t b)").bitcast(I32))
-        w0_raw.append(load_rows(half(w0_both, 1), w[0:512, :], H, N))
         w1_both = at("w1_raw", [P, 8 * H], F32, 16384)
         w1_raw = [load_rows(half(w1_both, h), w[512:1024, :], h * H, (h + 1) * H) for h in range(2)]
         iw_rows = at("iw_rows", [P, P], F32, 26112)
@@ -78,117 +78,103 @@ def tile_list_interp_hl_res_kernel(tc, tab_words, tab_scales, w, x, wx, iw0, iw1
         nc.sync.dma_start(scales_p1[0:100, :].bitcast(I32), scales_p0[4:104, :].bitcast(I32))
         tab_planes = (scales_p0, scales_p1)
 
-        def weave(name, raw_cols):
-            width = raw_cols.shape[2]
-            woven = sb(name, [P, width, 4], BF16)
+        def weave(woven, raw_cols):
             nc.scalar.activation(
-                woven[:].rearrange("p (c i) t -> p c t i", i=4),
+                woven.rearrange("p (c i) t -> p c t i", i=4),
                 raw_cols.rearrange("p t (c i) -> p c t i", i=4),
                 COPY,
             )
-            return woven
 
         def quantize(woven, codes, plane):
-            nc.vector.quantize_mx(out=codes.bitcast(FP8X4), scales=plane, in_=woven[:].rearrange("p c t -> p (c t)"))
+            nc.vector.quantize_mx(out=codes.bitcast(FP8X4), scales=plane, in_=woven.rearrange("p c t -> p (c t)"))
 
-        def gather(pairs, g, h):
-            c0 = (g * J + h * H) // 16
-            nc.vector.tensor_copy(pairs, word_tab[:].bitcast(U32).indirect(offsets[:, c0 : c0 + H // 16]))
-
-        def part(name, pairs):
-            width = pairs.shape[1]
-            parted = sb(name, [P, 2, 2 * width], U8)
-            nc.vector.tensor_copy(parted[:].bitcast(U16), pairs.bitcast(U16).rearrange("p (j d) -> p d j", d=2))
+        def pick_words(pairs, h):
+            for g in range(G):
+                c0 = (g * J + h * H) // 16
+                nc.vector.tensor_copy(pairs[:, g * H : (g + 1) * H], word_tab[:].bitcast(U32).indirect(offsets[:, c0 : c0 + H // 16]))
+            parted = sb("parted%d" % h, [P, 2, 2 * G * H], U8)
+            nc.vector.tensor_copy(parted[:].bitcast(U16), pairs[:].bitcast(U16).rearrange("p (j d) -> p d j", d=2))
             return parted
 
         w_codes = [sb("w_codes%d" % a, [P, N], U32) for a in range(2)]
         w_plane = [sb("w_plane%d" % a, [P, N], U8) for a in range(2)]
-
-        def quantize_w(a, woven):
-            for h in range(2):
-                quantize(woven[h], w_codes[a][:, h * H : (h + 1) * H], w_plane[a][:, h * H : (h + 1) * H])
-
-        words = {}
-        w0_woven = [weave("w0_woven%d" % h, w0_raw[h]) for h in range(2)]
-        pairs0 = at("pairs0", [P, G * H], U32, 26624 + 4096 - 1536)
-        for g in range(G):
-            gather(pairs0[:, g * H : (g + 1) * H], g, 0)
-        parted0 = part("parted0", pairs0[:])
-        for g in range(G):
-            words[g, 0] = parted0[:, :, 2 * g * H : 2 * (g + 1) * H]
+        w_woven = [sb("w_woven%d" % a, [P, N, 4], BF16) for a in range(2)]
+        for h in range(2):
+            weave(w_woven[0][:, h * H : (h + 1) * H, :], w0_raw[h])
+        parted = [pick_words(at("pairs0", [P, G * H], U32, 26624 + 4096 - 1536), 0)]
         wx_raw = [load_rows(at("wx_raw%d" % h, [P, 4, H], F32, 26624 + 4096 * h), wx, h * H, (h + 1) * H) for h in range(2)]
-        quantize_w(0, w0_woven)
+        quantize(w_woven[0][:], w_codes[0][:], w_plane[0][:])
         x_both = at("x_raw", [P, 8 * H], F32, 0)
         x_raw = [load_rows(half(x_both, h), x, h * H, (h + 1) * H) for h in range(2)]
-
-        def second_half(g, tag):
-            pairs = sb("pairs1_%d" % g, [P, H], U32, tag)
-            gather(pairs[:], g, 1)
-            words[g, 1] = part("parted1_%d" % g, pairs[:])[:]
-
-        w1_woven = [weave("w1_woven%d" % h, w1_raw[h]) for h in range(2)]
+        for h in range(2):
+            weave(w_woven[1][:, h * H : (h + 1) * H, :], w1_raw[h])
         res_sb = at("res_sb", [P, 4, J], F32, 16384)
         nc.sync.dma_start(res_sb[:], res.rearrange("(c p) j -> p c j", p=P))
-        second_half(0, "w0_woven1")
-        quantize_w(1, w1_woven)
-        second_half(1, "w1_woven0")
-        second_half(2, "w1_woven1")
+        quantize(w_woven[1][:], w_codes[1][:], w_plane[1][:])
+        parted.append(pick_words(sb("pairs1", [P, G * H], U32, "w_woven1"), 1))
 
-        iw_ps = psum.tile([P, P], F32, name="iw_ps", tag="turned3")
+        iw_ps = psum.tile([P, P], F32, name="iw_ps", tag="turned2")
         nc.tensor.transpose(iw_ps[:], iw_rows[:], ident[:])
         iw_cols = sb("iw_cols", [P, 16], F32)
         nc.scalar.activation(iw_cols[:], iw_ps[:, 0:16], COPY)
 
-        part_codes = [sb("part_codes%d" % s, [P, N], U32) for s in range(2)]
-        part_plane = [sb("part_plane%d" % s, [P, N], U8) for s in range(2)]
+        part_codes = [sb("part_codes%d" % h, [P, 2 * H], U32) for h in range(2)]
+        part_plane = [sb("part_plane%d" % h, [P, 2 * H], U8) for h in range(2)]
         for h in range(2):
             top = sb("top%d" % h, [P, H, 4], BF16)
             wx_top = wx_raw[h][:].bitcast(BF16).rearrange("p t (c i e) -> p c t i e", i=4, e=2)[:, :, :, :, 1]
             nc.scalar.copy(top[:].rearrange("p (c i) t -> p c t i", i=4), wx_top)
-            hi = sb("hi%d" % h, [P, H, 4], BF16)
+            split = sb("split%d" % h, [P, 2 * H, 4], BF16)
+            hi, lo = split[:, 0:H, :], split[:, H : 2 * H, :]
             nc.vector.tensor_scalar(
-                hi[:].rearrange("p c t -> p (c t)").bitcast(I32),
+                hi.rearrange("p c t -> p (c t)").bitcast(I32),
                 top[:].rearrange("p c t -> p (c t)").bitcast(I32),
                 HI_MASK, None, ALU.bitwise_and,
             )
-            lo = sb("lo%d" % h, [P, H, 4], BF16)
-            nc.vector.tensor_tensor(lo[:], wx_raw[h][:].rearrange("p t c -> p c t"), hi[:], ALU.subtract)
-            cols = slice(h * H, (h + 1) * H)
-            quantize(hi, part_codes[0][:, cols], part_plane[0][:, cols])
-            quantize(lo, part_codes[1][:, cols], part_plane[1][:, cols])
+            nc.vector.tensor_tensor(lo, wx_raw[h][:].rearrange("p t c -> p c t"), hi, ALU.subtract)
+            quantize(split[:], part_codes[h][:], part_plane[h][:])
         x_codes = [sb("x_codes%d" % h, [P, H], U32) for h in range(2)]
         x_plane = [sb("x_plane%d" % h, [P, H], U8) for h in range(2)]
         for h in range(2):
-            quantize(weave("x_woven%d" % h, x_raw[h]), x_codes[h][:], x_plane[h][:])
+            x_woven = sb("x_woven%d" % h, [P, H, 4], BF16)
+            weave(x_woven[:], x_raw[h])
+            quantize(x_woven[:], x_codes[h][:], x_plane[h][:])
 
         used = []
 
         def next_bank(name, shape):
             used.append(name)
-            return psum.tile(shape, F32, name=name, tag="acc%d" % (len(used) % 4))
+            return psum.tile(shape, F32, name=name, tag="acc%d" % (len(used) % 5))
 
         def look_up(jt):
             h, u = divmod(jt, 2)
-            turned = psum.tile([P, 4, P], F32, name="turned%d" % jt, tag="turned%d" % jt)
+            turned = psum.tile([P, 4, P], F32, name="turned%d" % jt, tag="turned%d" % (jt % 3))
+            terms = []
             for g in range(G):
                 bank = next_bank("a%d_%d" % (g, jt), [P, N])
                 s0 = g * J + jt * P
                 for a in range(2):
                     nc.tensor.matmul_mx(
                         out=bank[:],
-                        lhsT=words[g, h][:, a, 2 * u * P : 2 * (u + 1) * P].bitcast(FP4X4),
+                        lhsT=parted[h][:, a, 2 * (g * H + u * P) : 2 * (g * H + (u + 1) * P)].bitcast(FP4X4),
                         lhsT_scale=tab_planes[a][:, s0 : s0 + P],
                         rhs=w_codes[a][:].bitcast(FP8X4),
                         rhs_scale=w_plane[a][:],
                         start=(a == 0),
                         stop=(a == 1),
                     )
-                scaled = sb("scaled%d_%d" % (g, jt), [P, N], F32)
-                nc.scalar.activation(scaled[:], bank[:], COPY, scale=iw_cols[:, 4 * g + jt : 4 * g + jt + 1])
+                weight = iw_cols[:, 4 * g + jt : 4 * g + jt + 1]
+                term = sb("term%d_%d" % (g, jt), [P, N], F32)
+                if h == 0 or g == 0:
+                    nc.scalar.activation(term[:], bank[:], COPY, scale=weight)
+                else:
+                    nc.vector.scalar_tensor_tensor(term[:], bank[:], weight, terms.pop()[:], ALU.mult, ALU.add)
+                terms.append(term)
+            for g, term in enumerate(terms):
                 for c in range(4):
                     nc.tensor.matmul(
-                        turned[:, c, :], scaled[:, c * P : (c + 1) * P], ident[:],
-                        start=(g == 0 and c == 0), stop=(g == G - 1 and c == 3), is_transpose=True,
+                        turned[:, c, :], term[:, c * P : (c + 1) * P], ident[:],
+                        start=(g == 0 and c == 0), stop=(g == len(terms) - 1 and c == 3), is_transpose=True,
                     )
             return turned
 
@@ -197,12 +183,12 @@ def tile_list_interp_hl_res_kernel(tc, tab_words, tab_scales, w, x, wx, iw0, iw1
             for cp in range(2):
                 bank = next_bank("ax%d_%d" % (h, cp), [P, 2, H])
                 for e in range(2):
-                    c = 2 * cp + e
                     for s in range(2):
+                        c0 = s * H + e * P
                         nc.tensor.matmul_mx(
                             out=bank[:, e, :],
-                            lhsT=part_codes[s][:, c * P : (c + 1) * P].bitcast(FP8X4),
-                            lhsT_scale=part_plane[s][:, c * P : (c + 1) * P],
+                            lhsT=part_codes[cp][:, c0 : c0 + P].bitcast(FP8X4),
+                            lhsT_scale=part_plane[cp][:, c0 : c0 + P],
                             rhs=x_codes[h][:].bitcast(FP8X4),
                             rhs_scale=x_plane[h][:],
                             start=(s == 0),

@@ -45,7 +45,7 @@ def tile_list_interp_hl_res_kernel(tc, tab_words, tab_scales, w, x, wx, iw0, iw1
         def half(both, h):
             return both[:, h * 4 * H : (h + 1) * 4 * H].rearrange("p (t c) -> p t c", t=4)
 
-        w0_raw = [load_rows(at("w0_raw0", [P, 4, H], F32, 0), w[0:512, :], 0, H)[:]]
+        w0_raw = [load_rows(at("w0_raw0", [P, 4, H], F32, 18432), w[0:512, :], 0, H)[:]]
 
         scale_tab = sb("scale_tab", [P, T], U8)
         nc.vector.memset(scale_tab[:].bitcast(I32), 0)
@@ -53,7 +53,7 @@ def tile_list_interp_hl_res_kernel(tc, tab_words, tab_scales, w, x, wx, iw0, iw1
             nc.sync.dma_start(scale_tab[32 * q : 32 * q + 8, :].bitcast(I32), tab_scales[:, 4 * q : 4 * q + 4, :].bitcast(I32))
 
         ident = sb("ident", [P, P], F32)
-        for c0, c1, edge in ((0, 64, 8192), (64, 96, 24576), (96, 128, 26112)):
+        for c0, c1, edge in ((0, 64, 24576 + 64), (64, 96, 8192), (96, 128, 36352)):
             zeros = at("zeros%d" % c0, [P, c1 - c0], F32, edge - 64)
             nc.gpsimd.memset(zeros[:], 0.0)
             nc.gpsimd.affine_select(
@@ -61,19 +61,19 @@ def tile_list_interp_hl_res_kernel(tc, tab_words, tab_scales, w, x, wx, iw0, iw1
                 base=-c0, pattern=[[-1, c1 - c0]], channel_multiplier=1,
             )
 
-        w0_raw.append(load_rows(at("w0_raw1", [P, 4, H], F32, 4096), w[0:512, :], H, N)[:])
+        w0_raw.append(load_rows(at("w0_raw1", [P, 4, H], F32, 24576), w[0:512, :], H, N)[:])
         word_tab = at("word_tab", [P, T], I32, 8192)
         nc.sync.dma_start(word_tab[:], tab_words[0].rearrange("p t b -> p (t b)").bitcast(I32))
-        w1_both = at("w1_raw", [P, 8 * H], F32, 16384)
+        w1_both = at("w1_raw", [P, 8 * H], F32, 0)
         w1_raw = [load_rows(half(w1_both, h), w[512:1024, :], h * H, (h + 1) * H) for h in range(2)]
-        iw_rows = at("iw_rows", [P, P], F32, 26112)
+        iw_rows = at("iw_rows", [P, P], F32, 36352)
         nc.gpsimd.memset(iw_rows[:], 0.0)
         for g, iw in enumerate((iw0, iw1, iw2)):
             nc.gpsimd.dma_start(iw_rows[4 * g : 4 * g + 4, :], iw.rearrange("(c j) -> c j", c=4))
 
         scales_p0 = sb("scales_p0", [P, G * J], U8)
         nc.vector.tensor_copy(scales_p0[:], scale_tab[:].indirect(offsets[:]))
-        scales_p1 = at("scales_p1", [P, G * J], U8, 24576)
+        scales_p1 = at("scales_p1", [P, G * J], U8, 34816)
         nc.vector.memset(scales_p1[:].bitcast(I32), 0)
         nc.sync.dma_start(scales_p1[0:100, :].bitcast(I32), scales_p0[4:104, :].bitcast(I32))
         tab_planes = (scales_p0, scales_p1)
@@ -101,28 +101,29 @@ def tile_list_interp_hl_res_kernel(tc, tab_words, tab_scales, w, x, wx, iw0, iw1
         w_woven = [sb("w_woven%d" % a, [P, N, 4], BF16) for a in range(2)]
         for h in range(2):
             weave(w_woven[0][:, h * H : (h + 1) * H, :], w0_raw[h])
-        parted = [pick_words(at("pairs0", [P, G * H], U32, 26624 + 4096 - 1536), 0)]
-        wx_raw = [load_rows(at("wx_raw%d" % h, [P, 4, H], F32, 26624 + 4096 * h), wx, h * H, (h + 1) * H) for h in range(2)]
-        quantize(w_woven[0][:], w_codes[0][:], w_plane[0][:])
-        x_both = at("x_raw", [P, 8 * H], F32, 0)
+        wx_both = at("wx_raw", [P, 8 * H], F32, 26624)
+        wx_raw = [load_rows(half(wx_both, h), wx, h * H, (h + 1) * H) for h in range(2)]
+        x_both = at("x_raw", [P, 8 * H], F32, 18432)
         x_raw = [load_rows(half(x_both, h), x, h * H, (h + 1) * H) for h in range(2)]
+        parted = [pick_words(sb("pairs0", [P, G * H], U32), 0)]
+        quantize(w_woven[0][:], w_codes[0][:], w_plane[0][:])
         for h in range(2):
             weave(w_woven[1][:, h * H : (h + 1) * H, :], w1_raw[h])
-        res_sb = at("res_sb", [P, 4, J], F32, 16384)
-        nc.sync.dma_start(res_sb[:], res.rearrange("(c p) j -> p c j", p=P))
         quantize(w_woven[1][:], w_codes[1][:], w_plane[1][:])
         parted.append(pick_words(sb("pairs1", [P, G * H], U32, "w_woven1"), 1))
+        res_sb = at("res_sb", [P, 4, J], F32, 8192)
+        nc.sync.dma_start(res_sb[:], res.rearrange("(c p) j -> p c j", p=P))
 
-        iw_ps = psum.tile([P, P], F32, name="iw_ps", tag="turned2")
+        iw_ps = psum.tile([P, P], F32, name="iw_ps", tag="bank7")
         nc.tensor.transpose(iw_ps[:], iw_rows[:], ident[:])
-        iw_cols = sb("iw_cols", [P, 16], F32)
+        iw_cols = at("iw_cols", [P, 16], F32, 0)
         nc.scalar.activation(iw_cols[:], iw_ps[:, 0:16], COPY)
 
         part_codes = [sb("part_codes%d" % h, [P, 2 * H], U32) for h in range(2)]
         part_plane = [sb("part_plane%d" % h, [P, 2 * H], U8) for h in range(2)]
         for h in range(2):
             top = sb("top%d" % h, [P, H, 4], BF16)
-            wx_top = wx_raw[h][:].bitcast(BF16).rearrange("p t (c i e) -> p c t i e", i=4, e=2)[:, :, :, :, 1]
+            wx_top = wx_raw[h].bitcast(BF16).rearrange("p t (c i e) -> p c t i e", i=4, e=2)[:, :, :, :, 1]
             nc.scalar.copy(top[:].rearrange("p (c i) t -> p c t i", i=4), wx_top)
             split = sb("split%d" % h, [P, 2 * H, 4], BF16)
             hi, lo = split[:, 0:H, :], split[:, H : 2 * H, :]
@@ -131,7 +132,7 @@ def tile_list_interp_hl_res_kernel(tc, tab_words, tab_scales, w, x, wx, iw0, iw1
                 top[:].rearrange("p c t -> p (c t)").bitcast(I32),
                 HI_MASK, None, ALU.bitwise_and,
             )
-            nc.vector.tensor_tensor(lo, wx_raw[h][:].rearrange("p t c -> p c t"), hi, ALU.subtract)
+            nc.vector.tensor_tensor(lo, wx_raw[h].rearrange("p t c -> p c t"), hi, ALU.subtract)
             quantize(split[:], part_codes[h][:], part_plane[h][:])
         x_codes = [sb("x_codes%d" % h, [P, H], U32) for h in range(2)]
         x_plane = [sb("x_plane%d" % h, [P, H], U8) for h in range(2)]
@@ -140,18 +141,14 @@ def tile_list_interp_hl_res_kernel(tc, tab_words, tab_scales, w, x, wx, iw0, iw1
             weave(x_woven[:], x_raw[h])
             quantize(x_woven[:], x_codes[h][:], x_plane[h][:])
 
-        used = []
-
-        def next_bank(name, shape):
-            used.append(name)
-            return psum.tile(shape, F32, name=name, tag="acc%d" % (len(used) % 5))
+        def bank_tile(name, shape, b):
+            return psum.tile(shape, F32, name=name, tag="bank%d" % b)
 
         def look_up(jt):
             h, u = divmod(jt, 2)
-            turned = psum.tile([P, 4, P], F32, name="turned%d" % jt, tag="turned%d" % (jt % 3))
             terms = []
             for g in range(G):
-                bank = next_bank("a%d_%d" % (g, jt), [P, N])
+                bank = bank_tile("a%d_%d" % (g, jt), [P, N], G * u + g)
                 s0 = g * J + jt * P
                 for a in range(2):
                     nc.tensor.matmul_mx(
@@ -164,12 +161,18 @@ def tile_list_interp_hl_res_kernel(tc, tab_words, tab_scales, w, x, wx, iw0, iw1
                         stop=(a == 1),
                     )
                 weight = iw_cols[:, 4 * g + jt : 4 * g + jt + 1]
-                term = sb("term%d_%d" % (g, jt), [P, N], F32)
-                if h == 0 or g == 0:
-                    nc.scalar.activation(term[:], bank[:], COPY, scale=weight)
-                else:
+                name = "term%d_%d" % (g, jt)
+                if g > 0:
+                    term = sb(name, [P, N], F32, "x_woven%d" % (1 - jt) if g == 1 and h == 0 else None)
                     nc.vector.scalar_tensor_tensor(term[:], bank[:], weight, terms.pop()[:], ALU.mult, ALU.add)
+                else:
+                    term = sb(name, [P, N], F32)
+                    nc.scalar.activation(term[:], bank[:], COPY, scale=weight)
                 terms.append(term)
+            return terms
+
+        def turn(jt, terms):
+            turned = bank_tile("turned%d" % jt, [P, 4, P], (6, 7, 1, 4)[jt])
             for g, term in enumerate(terms):
                 for c in range(4):
                     nc.tensor.matmul(
@@ -181,7 +184,7 @@ def tile_list_interp_hl_res_kernel(tc, tab_words, tab_scales, w, x, wx, iw0, iw1
         def skip_half(h):
             own = sb("own%d" % h, [P, 4, H], F32)
             for cp in range(2):
-                bank = next_bank("ax%d_%d" % (h, cp), [P, 2, H])
+                bank = bank_tile("ax%d_%d" % (h, cp), [P, 2, H], ((6, 7), (0, 3))[h][cp])
                 for e in range(2):
                     for s in range(2):
                         c0 = s * H + e * P
@@ -205,11 +208,12 @@ def tile_list_interp_hl_res_kernel(tc, tab_words, tab_scales, w, x, wx, iw0, iw1
             nc.vector.tensor_tensor(done[:], turned[:], own[:, :, u * P : (u + 1) * P], ALU.add)
             nc.sync.dma_start(out_rows[:, :, jt * P : (jt + 1) * P], done[:])
 
-        turned = [look_up(jt) for jt in range(3)]
-        own0 = skip_half(0)
-        finish(0, turned[0], own0)
-        finish(1, turned[1], own0)
-        turned.append(look_up(3))
-        own1 = skip_half(1)
-        finish(2, turned[2], own1)
-        finish(3, turned[3], own1)
+        terms = [look_up(0), look_up(1)]
+        own = skip_half(0)
+        terms.append(look_up(2))
+        for jt in range(2):
+            finish(jt, turn(jt, terms[jt]), own)
+        terms.append(look_up(3))
+        own = skip_half(1)
+        for jt in range(2, 4):
+            finish(jt, turn(jt, terms[jt]), own)

@@ -119,28 +119,6 @@ def tile_list_interp_hl_res_kernel(tc, tab_words, tab_scales, w, x, wx, iw0, iw1
         iw_cols = at("iw_cols", [P, 16], F32, 0)
         nc.scalar.activation(iw_cols[:], iw_ps[:, 0:16], COPY)
 
-        part_codes = [sb("part_codes%d" % h, [P, 2 * H], U32) for h in range(2)]
-        part_plane = [sb("part_plane%d" % h, [P, 2 * H], U8) for h in range(2)]
-        for h in range(2):
-            top = sb("top%d" % h, [P, H, 4], BF16)
-            wx_top = wx_raw[h].bitcast(BF16).rearrange("p t (c i e) -> p c t i e", i=4, e=2)[:, :, :, :, 1]
-            nc.scalar.copy(top[:].rearrange("p (c i) t -> p c t i", i=4), wx_top)
-            split = sb("split%d" % h, [P, 2 * H, 4], BF16)
-            hi, lo = split[:, 0:H, :], split[:, H : 2 * H, :]
-            nc.vector.tensor_scalar(
-                hi.rearrange("p c t -> p (c t)").bitcast(I32),
-                top[:].rearrange("p c t -> p (c t)").bitcast(I32),
-                HI_MASK, None, ALU.bitwise_and,
-            )
-            nc.vector.tensor_tensor(lo, wx_raw[h].rearrange("p t c -> p c t"), hi, ALU.subtract)
-            quantize(split[:], part_codes[h][:], part_plane[h][:])
-        x_codes = [sb("x_codes%d" % h, [P, H], U32) for h in range(2)]
-        x_plane = [sb("x_plane%d" % h, [P, H], U8) for h in range(2)]
-        for h in range(2):
-            x_woven = sb("x_woven%d" % h, [P, H, 4], BF16)
-            weave(x_woven[:], x_raw[h])
-            quantize(x_woven[:], x_codes[h][:], x_plane[h][:])
-
         def bank_tile(name, shape, b):
             return psum.tile(shape, F32, name=name, tag="bank%d" % b)
 
@@ -163,28 +141,77 @@ def tile_list_interp_hl_res_kernel(tc, tab_words, tab_scales, w, x, wx, iw0, iw1
                 weight = iw_cols[:, 4 * g + jt : 4 * g + jt + 1]
                 name = "term%d_%d" % (g, jt)
                 if g > 0:
-                    term = sb(name, [P, N], F32, "x_woven%d" % (1 - jt) if g == 1 and h == 0 else None)
+                    term = sb(name, [P, N], F32, ("split1", "x_woven1")[u] if g == 1 and h == 1 else None)
                     nc.vector.scalar_tensor_tensor(term[:], bank[:], weight, terms.pop()[:], ALU.mult, ALU.add)
                 else:
                     term = sb(name, [P, N], F32)
                     nc.scalar.activation(term[:], bank[:], COPY, scale=weight)
                 terms.append(term)
-            return terms
+            return terms[0]
 
-        def turn(jt, terms):
-            turned = bank_tile("turned%d" % jt, [P, 4, P], (6, 7, 1, 4)[jt])
-            for g, term in enumerate(terms):
-                for c in range(4):
-                    nc.tensor.matmul(
-                        turned[:, c, :], term[:, c * P : (c + 1) * P], ident[:],
-                        start=(g == 0 and c == 0), stop=(g == len(terms) - 1 and c == 3), is_transpose=True,
+        def turn(turned, term, first, last):
+            for c in range(4):
+                nc.tensor.matmul(
+                    turned[:, c, :], term[:, c * P : (c + 1) * P], ident[:],
+                    start=(first and c == 0), stop=(last and c == 3), is_transpose=True,
+                )
+
+        turned = []
+        for jt in range(2):
+            summed = look_up(jt)
+            turned.append(bank_tile("turned%d" % jt, [P, 4, P], 6 + jt))
+            turn(turned[jt], summed, True, False)
+
+        part_codes = [sb("part_codes%d" % h, [P, 2 * H], U32) for h in range(2)]
+        part_plane = [sb("part_plane%d" % h, [P, 2 * H], U8) for h in range(2)]
+        for h in range(2):
+            top = sb("top%d" % h, [P, H, 4], BF16)
+            wx_top = wx_raw[h].bitcast(BF16).rearrange("p t (c i e) -> p c t i e", i=4, e=2)[:, :, :, :, 1]
+            nc.scalar.copy(top[:].rearrange("p (c i) t -> p c t i", i=4), wx_top)
+            split = sb("split%d" % h, [P, 2 * H, 4], BF16)
+            hi, lo = split[:, 0:H, :], split[:, H : 2 * H, :]
+            nc.vector.tensor_scalar(
+                hi.rearrange("p c t -> p (c t)").bitcast(I32),
+                top[:].rearrange("p c t -> p (c t)").bitcast(I32),
+                HI_MASK, None, ALU.bitwise_and,
+            )
+            nc.vector.tensor_tensor(
+                lo.rearrange("p (c i) t -> p c t i", i=4),
+                wx_raw[h].rearrange("p t (c i) -> p c t i", i=4),
+                hi.rearrange("p (c i) t -> p c t i", i=4),
+                ALU.subtract,
+            )
+            quantize(split[:], part_codes[h][:], part_plane[h][:])
+        x_codes = [sb("x_codes%d" % h, [P, H], U32) for h in range(2)]
+        x_plane = [sb("x_plane%d" % h, [P, H], U8) for h in range(2)]
+        for h in range(2):
+            x_woven = sb("x_woven%d" % h, [P, H, 4], BF16)
+            weave(x_woven[:], x_raw[h])
+            quantize(x_woven[:], x_codes[h][:], x_plane[h][:])
+
+        late = [look_up(jt) for jt in range(2, 4)]
+
+        def skip_turned(jt):
+            bank = bank_tile("ax%d" % jt, [P, 2, H], G * jt)
+            for e in range(2):
+                for s in range(2):
+                    nc.tensor.matmul_mx(
+                        out=bank[:, e, :],
+                        lhsT=x_codes[0][:, jt * P : (jt + 1) * P].bitcast(FP8X4),
+                        lhsT_scale=x_plane[0][:, jt * P : (jt + 1) * P],
+                        rhs=part_codes[e][:, s * H : (s + 1) * H].bitcast(FP8X4),
+                        rhs_scale=part_plane[e][:, s * H : (s + 1) * H],
+                        start=(s == 0),
+                        stop=(s == 1),
                     )
-            return turned
+            own = sb("own%d" % jt, [P, N], F32)
+            nc.scalar.activation(own[:], bank[:].rearrange("p e c -> p (e c)"), COPY)
+            turn(turned[jt], own, False, True)
 
-        def skip_half(h):
-            own = sb("own%d" % h, [P, 4, H], F32)
+        def skip_upright():
+            own = sb("own_late", [P, 4, H], F32)
             for cp in range(2):
-                bank = bank_tile("ax%d_%d" % (h, cp), [P, 2, H], ((6, 7), (0, 3))[h][cp])
+                bank = bank_tile("ax_late%d" % cp, [P, 2, H], 1 + cp)
                 for e in range(2):
                     for s in range(2):
                         c0 = s * H + e * P
@@ -192,28 +219,28 @@ def tile_list_interp_hl_res_kernel(tc, tab_words, tab_scales, w, x, wx, iw0, iw1
                             out=bank[:, e, :],
                             lhsT=part_codes[cp][:, c0 : c0 + P].bitcast(FP8X4),
                             lhsT_scale=part_plane[cp][:, c0 : c0 + P],
-                            rhs=x_codes[h][:].bitcast(FP8X4),
-                            rhs_scale=x_plane[h][:],
+                            rhs=x_codes[1][:].bitcast(FP8X4),
+                            rhs_scale=x_plane[1][:],
                             start=(s == 0),
                             stop=(s == 1),
                         )
-                nc.vector.tensor_tensor(own[:, 2 * cp : 2 * cp + 2, :], bank[:], res_sb[:, 2 * cp : 2 * cp + 2, h * H : (h + 1) * H], ALU.add)
+                nc.vector.tensor_tensor(own[:, 2 * cp : 2 * cp + 2, :], bank[:], res_sb[:, 2 * cp : 2 * cp + 2, H:J], ALU.add)
             return own
 
         out_rows = out.rearrange("(c p) j -> p c j", p=P)
 
-        def finish(jt, turned, own):
-            u = jt % 2
+        def finish(jt, addend):
             done = sb("done%d" % jt, [P, 4, P], F32)
-            nc.vector.tensor_tensor(done[:], turned[:], own[:, :, u * P : (u + 1) * P], ALU.add)
+            nc.vector.tensor_tensor(done[:], turned[jt][:], addend, ALU.add)
             nc.sync.dma_start(out_rows[:, :, jt * P : (jt + 1) * P], done[:])
 
-        terms = [look_up(0), look_up(1)]
-        own = skip_half(0)
-        terms.append(look_up(2))
         for jt in range(2):
-            finish(jt, turn(jt, terms[jt]), own)
-        terms.append(look_up(3))
-        own = skip_half(1)
-        for jt in range(2, 4):
-            finish(jt, turn(jt, terms[jt]), own)
+            skip_turned(jt)
+        for u in range(2):
+            turned.append(bank_tile("turned%d" % (2 + u), [P, 4, P], 4 + u))
+            turn(turned[2 + u], late[u], True, True)
+        for jt in range(2):
+            finish(jt, res_sb[:, :, jt * P : (jt + 1) * P])
+        own_late = skip_upright()
+        for u in range(2):
+            finish(2 + u, own_late[:, :, u * P : (u + 1) * P])

@@ -45,15 +45,13 @@ def tile_list_interp_hl_res_kernel(tc, tab_words, tab_scales, w, x, wx, iw0, iw1
         def half(both, h):
             return both[:, h * 4 * H : (h + 1) * 4 * H].rearrange("p (t c) -> p t c", t=4)
 
-        w0_raw = [load_rows(at("w0_raw0", [P, 4, H], F32, 18432), w[0:512, :], 0, H)[:]]
-
         scale_tab = sb("scale_tab", [P, T], U8)
-        nc.vector.memset(scale_tab[:].bitcast(I32), 0)
+        nc.gpsimd.memset(scale_tab[:].bitcast(I32), 0)
         for q in range(4):
             nc.sync.dma_start(scale_tab[32 * q : 32 * q + 8, :].bitcast(I32), tab_scales[:, 4 * q : 4 * q + 4, :].bitcast(I32))
 
         ident = sb("ident", [P, P], F32)
-        for c0, c1, edge in ((0, 64, 24576 + 64), (64, 96, 8192), (96, 128, 36352)):
+        for c0, c1, edge in ((0, 64, 34816), (64, 96, 8192), (96, 128, 40448)):
             zeros = at("zeros%d" % c0, [P, c1 - c0], F32, edge - 64)
             nc.gpsimd.memset(zeros[:], 0.0)
             nc.gpsimd.affine_select(
@@ -61,19 +59,20 @@ def tile_list_interp_hl_res_kernel(tc, tab_words, tab_scales, w, x, wx, iw0, iw1
                 base=-c0, pattern=[[-1, c1 - c0]], channel_multiplier=1,
             )
 
-        w0_raw.append(load_rows(at("w0_raw1", [P, 4, H], F32, 24576), w[0:512, :], H, N)[:])
-        word_tab = at("word_tab", [P, T], I32, 8192)
+        w0_raw = [load_rows(at("w0_raw0", [P, 4, H], F32, 34816), w[0:512, :], 0, H)[:]]
+        word_tab = at("word_tab", [P, T], I32, 26624)
         nc.sync.dma_start(word_tab[:], tab_words[0].rearrange("p t b -> p (t b)").bitcast(I32))
+        w0_raw.append(load_rows(at("w0_raw1", [P, 4, H], F32, 8192), w[0:512, :], H, N)[:])
         w1_both = at("w1_raw", [P, 8 * H], F32, 0)
         w1_raw = [load_rows(half(w1_both, h), w[512:1024, :], h * H, (h + 1) * H) for h in range(2)]
-        iw_rows = at("iw_rows", [P, P], F32, 36352)
+        iw_rows = at("iw_rows", [P, P], F32, 40448)
         nc.gpsimd.memset(iw_rows[:], 0.0)
         for g, iw in enumerate((iw0, iw1, iw2)):
             nc.gpsimd.dma_start(iw_rows[4 * g : 4 * g + 4, :], iw.rearrange("(c j) -> c j", c=4))
 
         scales_p0 = sb("scales_p0", [P, G * J], U8)
         nc.vector.tensor_copy(scales_p0[:], scale_tab[:].indirect(offsets[:]))
-        scales_p1 = at("scales_p1", [P, G * J], U8, 34816)
+        scales_p1 = at("scales_p1", [P, G * J], U8, 38912)
         nc.vector.memset(scales_p1[:].bitcast(I32), 0)
         nc.sync.dma_start(scales_p1[0:100, :].bitcast(I32), scales_p0[4:104, :].bitcast(I32))
         tab_planes = (scales_p0, scales_p1)
@@ -101,17 +100,16 @@ def tile_list_interp_hl_res_kernel(tc, tab_words, tab_scales, w, x, wx, iw0, iw1
         w_woven = [sb("w_woven%d" % a, [P, N, 4], BF16) for a in range(2)]
         for h in range(2):
             weave(w_woven[0][:, h * H : (h + 1) * H, :], w0_raw[h])
-        wx_both = at("wx_raw", [P, 8 * H], F32, 26624)
-        wx_raw = [load_rows(half(wx_both, h), wx, h * H, (h + 1) * H) for h in range(2)]
-        x_both = at("x_raw", [P, 8 * H], F32, 18432)
-        x_raw = [load_rows(half(x_both, h), x, h * H, (h + 1) * H) for h in range(2)]
+        skip_raw = at("skip_raw", [P, 16 * H], F32, 10240)
+        wx_raw = [load_rows(half(skip_raw, h), wx, h * H, (h + 1) * H) for h in range(2)]
+        x_raw = [load_rows(half(skip_raw, 2 + h), x, h * H, (h + 1) * H) for h in range(2)]
         parted = [pick_words(sb("pairs0", [P, G * H], U32), 0)]
         quantize(w_woven[0][:], w_codes[0][:], w_plane[0][:])
         for h in range(2):
             weave(w_woven[1][:, h * H : (h + 1) * H, :], w1_raw[h])
         quantize(w_woven[1][:], w_codes[1][:], w_plane[1][:])
-        parted.append(pick_words(sb("pairs1", [P, G * H], U32, "w_woven1"), 1))
-        res_sb = at("res_sb", [P, 4, J], F32, 8192)
+        parted.append(pick_words(sb("pairs1", [P, G * H], U32, "w_woven0"), 1))
+        res_sb = at("res_sb", [P, 4, J], F32, 26624)
         nc.sync.dma_start(res_sb[:], res.rearrange("(c p) j -> p c j", p=P))
 
         iw_ps = psum.tile([P, P], F32, name="iw_ps", tag="bank7")

@@ -20,6 +20,7 @@ COPY = mybir.ActivationFunctionType.Copy
 P = 128
 H = 256
 HI_MASK = -983056
+MX_BANKS = 4
 
 
 def tile_list_interp_hl_res_kernel(tc, tab_words, tab_scales, w, x, wx, iw0, iw1, iw2, res, offs, out):
@@ -29,52 +30,55 @@ def tile_list_interp_hl_res_kernel(tc, tab_words, tab_scales, w, x, wx, iw0, iw1
         placed = ctx.enter_context(tc.tile_pool(name="placed", bufs=1))
         psum = ctx.enter_context(tc.psum_pool(name="psum", bufs=1))
 
-        def sb(name, shape, dtype, tag=None):
-            return keep.tile(shape, dtype, name=name, tag=tag or name, align_bytes=64)
+        def sb(name, shape, dtype):
+            return keep.tile(shape, dtype, name=name, align_bytes=64)
 
         def at(name, shape, dtype, offset):
             return placed.tile(shape, dtype, name=name, offset=offset, align_bytes=64)
 
-        offsets = keep.tile([P, G * J // 16], U16, name="offsets")
-        nc.sync.dma_start(offsets[:], offs)
-
         def load_rows(raw, rows, c0, c1):
-            nc.sync.dma_start(raw[:, :, :], rows.rearrange("(p t) c -> p t c", t=4)[:, :, c0:c1])
+            nc.sync.dma_start(raw, rows.rearrange("(p t) c -> p t c", t=4)[:, :, c0:c1])
             return raw
 
-        def half(both, h):
-            return both[:, h * 4 * H : (h + 1) * 4 * H].rearrange("p (t c) -> p t c", t=4)
+        offsets = keep.tile([P, G * J // 16], U16, name="offsets")
+        nc.sync.dma_start(offsets[:], offs)
+        w_raw = [load_rows(sb("w_raw0", [P, 4, H], F32)[:], w[0:512, :], 0, H)]
 
-        scale_tab = sb("scale_tab", [P, T], U8)
+        scale_tab = at("scale_tab", [P, T], U8, 55808)
         nc.gpsimd.memset(scale_tab[:].bitcast(I32), 0)
         for q in range(4):
-            nc.sync.dma_start(scale_tab[32 * q : 32 * q + 8, :].bitcast(I32), tab_scales[:, 4 * q : 4 * q + 4, :].bitcast(I32))
+            nc.sync.dma_start(scale_tab[32 * q : 32 * q + 4, :].bitcast(I32), tab_scales[0, 4 * q : 4 * q + 4, :].bitcast(I32))
+        nc.sync.dma_start(scale_tab[4:P:8, :].bitcast(I32), tab_scales[1].bitcast(I32))
 
         ident = sb("ident", [P, P], F32)
-        for c0, c1, edge in ((0, 64, 34816), (64, 96, 8192), (96, 128, 40448)):
-            zeros = at("zeros%d" % c0, [P, c1 - c0], F32, edge - 64)
-            nc.gpsimd.memset(zeros[:], 0.0)
+        pieces = ((0, 32, 4096 - 64), (32, 64, 20992 - 64), (64, 128, 29184))
+        for c0, c1, edge in pieces:
+            zeros = at("zeros%d" % c0, [P, c1 - c0], F32, edge)
+            nc.vector.memset(zeros[:], 0.0)
             nc.gpsimd.affine_select(
                 out=ident[:, c0:c1], in_=zeros[:], compare_op=ALU.not_equal, fill=1.0,
                 base=-c0, pattern=[[-1, c1 - c0]], channel_multiplier=1,
             )
 
-        w0_raw = [load_rows(at("w0_raw0", [P, 4, H], F32, 34816), w[0:512, :], 0, H)[:]]
-        word_tab = at("word_tab", [P, T], I32, 26624)
+        word_tab = at("word_tab", [P, T], I32, 4096)
         nc.sync.dma_start(word_tab[:], tab_words[0].rearrange("p t b -> p (t b)").bitcast(I32))
-        w0_raw.append(load_rows(at("w0_raw1", [P, 4, H], F32, 8192), w[0:512, :], H, N)[:])
-        w1_both = at("w1_raw", [P, 8 * H], F32, 0)
-        w1_raw = [load_rows(half(w1_both, h), w[512:1024, :], h * H, (h + 1) * H) for h in range(2)]
-        iw_rows = at("iw_rows", [P, P], F32, 40448)
-        nc.gpsimd.memset(iw_rows[:], 0.0)
+        iw_rows = at("iw_rows", [P, P], F32, 4096 - 512)
+        nc.vector.memset(iw_rows[:], 0.0)
         for g, iw in enumerate((iw0, iw1, iw2)):
-            nc.gpsimd.dma_start(iw_rows[4 * g : 4 * g + 4, :], iw.rearrange("(c j) -> c j", c=4))
+            nc.sync.dma_start(iw_rows[4 * g : 4 * g + 4, :], iw.rearrange("(c j) -> c j", c=4))
+        w_raw.append(load_rows(at("w_raw1", [P, 4, H], F32, 16896)[:], w[0:512, :], H, N))
+        w1_raw = at("w1_raw", [P, 8 * H], F32, 20992)
+        for h in range(2):
+            cols = w1_raw[:, h * 4 * H : (h + 1) * 4 * H].rearrange("p (t c) -> p t c", t=4)
+            w_raw.append(load_rows(cols, w[512:1024, :], h * H, (h + 1) * H))
 
-        scales_p0 = sb("scales_p0", [P, G * J], U8)
+        scales_p1 = sb("scales_p1", [P, G * J], U8)
+        nc.gpsimd.memset(scales_p1[:].bitcast(I32), 0)
+
+        scales_p0 = at("scales_p0", [P, G * J], U8, 29184)
         nc.vector.tensor_copy(scales_p0[:], scale_tab[:].indirect(offsets[:]))
-        scales_p1 = at("scales_p1", [P, G * J], U8, 38912)
-        nc.vector.memset(scales_p1[:].bitcast(I32), 0)
-        nc.sync.dma_start(scales_p1[0:100, :].bitcast(I32), scales_p0[4:104, :].bitcast(I32))
+        for q in range(4):
+            nc.sync.dma_start(scales_p1[32 * q : 32 * q + 4, :].bitcast(I32), scales_p0[32 * q + 4 : 32 * q + 32 : 8, :].bitcast(I32))
         tab_planes = (scales_p0, scales_p1)
 
         def weave(woven, raw_cols):
@@ -87,65 +91,87 @@ def tile_list_interp_hl_res_kernel(tc, tab_words, tab_scales, w, x, wx, iw0, iw1
         def quantize(woven, codes, plane):
             nc.vector.quantize_mx(out=codes.bitcast(FP8X4), scales=plane, in_=woven.rearrange("p c t -> p (c t)"))
 
-        def pick_words(pairs, h):
-            for g in range(G):
-                c0 = (g * J + h * H) // 16
-                nc.vector.tensor_copy(pairs[:, g * H : (g + 1) * H], word_tab[:].bitcast(U32).indirect(offsets[:, c0 : c0 + H // 16]))
-            parted = sb("parted%d" % h, [P, 2, 2 * G * H], U8)
+        def pick_words(pairs, g, h):
+            c0 = (g * J + h * H) // 16
+            nc.vector.tensor_copy(pairs, word_tab[:].bitcast(U32).indirect(offsets[:, c0 : c0 + H // 16]))
+
+        def part_words(parted, pairs):
             nc.vector.tensor_copy(parted[:].bitcast(U16), pairs[:].bitcast(U16).rearrange("p (j d) -> p d j", d=2))
-            return parted
-
-        w_codes = [sb("w_codes%d" % a, [P, N], U32) for a in range(2)]
-        w_plane = [sb("w_plane%d" % a, [P, N], U8) for a in range(2)]
-        w_woven = [sb("w_woven%d" % a, [P, N, 4], BF16) for a in range(2)]
-        for h in range(2):
-            weave(w_woven[0][:, h * H : (h + 1) * H, :], w0_raw[h])
-        skip_raw = at("skip_raw", [P, 16 * H], F32, 10240)
-        wx_raw = [load_rows(half(skip_raw, h), wx, h * H, (h + 1) * H) for h in range(2)]
-        x_raw = [load_rows(half(skip_raw, 2 + h), x, h * H, (h + 1) * H) for h in range(2)]
-        parted = [pick_words(sb("pairs0", [P, G * H], U32), 0)]
-        quantize(w_woven[0][:], w_codes[0][:], w_plane[0][:])
-        for h in range(2):
-            weave(w_woven[1][:, h * H : (h + 1) * H, :], w1_raw[h])
-        quantize(w_woven[1][:], w_codes[1][:], w_plane[1][:])
-        parted.append(pick_words(sb("pairs1", [P, G * H], U32, "w_woven0"), 1))
-        res_sb = at("res_sb", [P, 4, J], F32, 26624)
-        nc.sync.dma_start(res_sb[:], res.rearrange("(c p) j -> p c j", p=P))
-
-        iw_ps = psum.tile([P, P], F32, name="iw_ps", tag="bank7")
-        nc.tensor.transpose(iw_ps[:], iw_rows[:], ident[:])
-        iw_cols = at("iw_cols", [P, 16], F32, 0)
-        nc.scalar.activation(iw_cols[:], iw_ps[:, 0:16], COPY)
 
         def bank_tile(name, shape, b):
             return psum.tile(shape, F32, name=name, tag="bank%d" % b)
 
-        def look_up(jt):
+        iw_ps = bank_tile("iw_ps", [P, P], 7)
+        nc.tensor.transpose(iw_ps[:], iw_rows[:], ident[:])
+        iw_cols = sb("iw_cols", [P, 16], F32)
+
+        w_codes = [sb("w_codes%d" % a, [P, N], U32) for a in range(2)]
+        w_plane = [at("w_plane0", [P, N], U8, 56320), sb("w_plane1", [P, N], U8)]
+        w_woven = [at("w_woven%d" % i, [P, H, 4], BF16, 30720 + 2048 * i) for i in range(4)]
+
+        def quantize_w(i):
+            a, h = divmod(i, 2)
+            quantize(w_woven[i][:], w_codes[a][:, h * H : (h + 1) * H], w_plane[a][:, h * H : (h + 1) * H])
+
+        for i in range(4):
+            weave(w_woven[i][:], w_raw[i])
+        nc.scalar.activation(iw_cols[:], iw_ps[:, 0:16], COPY)
+        pairs = [sb("pairs0", [P, H], U32), at("pairs1", [P, H], U32, 35840), at("pairs2", [P, H], U32, 37888)]
+        parted = [sb("parted0", [P, 2, 2 * H], U8), at("parted1", [P, 2, 2 * H], U8, 36864), sb("parted2", [P, 2, 2 * H], U8)]
+        quantize_w(0)
+        pick_words(pairs[0][:], 0, 0)
+        part_words(parted[0], pairs[0])
+        quantize_w(1)
+        quantize_w(2)
+        pick_words(pairs[1][:], 1, 0)
+        quantize_w(3)
+        pick_words(pairs[2][:], 2, 0)
+        part_words(parted[1], pairs[1])
+        part_words(parted[2], pairs[2])
+        wx_raw = [load_rows(at("wx_raw%d" % h, [P, 4, H], F32, 52224 + 4608 * h)[:], wx, h * H, (h + 1) * H) for h in range(2)]
+        x_raw = load_rows(at("x_raw", [P, 4, J], F32, 20992)[:], x, 0, J)
+        pairs_late = at("pairs_late", [P, G * H], U32, 33792)
+        for g in range(G):
+            pick_words(pairs_late[:, g * H : (g + 1) * H], g, 1)
+        parted_late = sb("parted_late", [P, 2, 2 * G * H], U8)
+        part_words(parted_late, pairs_late)
+        res_sb = at("res_sb", [P, 4, J], F32, 4096)
+        nc.sync.dma_start(res_sb[:], res.rearrange("(c p) j -> p c j", p=P))
+
+        iw_col = lambda g, jt: iw_cols[:, 4 * g + jt : 4 * g + jt + 1]
+
+        def look_up(g, jt, b):
             h, u = divmod(jt, 2)
-            terms = []
-            for g in range(G):
-                bank = bank_tile("a%d_%d" % (g, jt), [P, N], G * u + g)
-                s0 = g * J + jt * P
-                for a in range(2):
-                    nc.tensor.matmul_mx(
-                        out=bank[:],
-                        lhsT=parted[h][:, a, 2 * (g * H + u * P) : 2 * (g * H + (u + 1) * P)].bitcast(FP4X4),
-                        lhsT_scale=tab_planes[a][:, s0 : s0 + P],
-                        rhs=w_codes[a][:].bitcast(FP8X4),
-                        rhs_scale=w_plane[a][:],
-                        start=(a == 0),
-                        stop=(a == 1),
-                    )
-                weight = iw_cols[:, 4 * g + jt : 4 * g + jt + 1]
-                name = "term%d_%d" % (g, jt)
-                if g > 0:
-                    term = sb(name, [P, N], F32, ("split1", "x_woven1")[u] if g == 1 and h == 1 else None)
-                    nc.vector.scalar_tensor_tensor(term[:], bank[:], weight, terms.pop()[:], ALU.mult, ALU.add)
+            bank = bank_tile("a%d_%d" % (g, jt), [P, N], b)
+            s0 = g * J + jt * P
+            passes = (0, 1) if (g, h) == (0, 0) else (1, 0)
+            for a in passes:
+                if h == 0:
+                    words = parted[g][:, a, 2 * u * P : 2 * (u + 1) * P]
                 else:
-                    term = sb(name, [P, N], F32)
-                    nc.scalar.activation(term[:], bank[:], COPY, scale=weight)
-                terms.append(term)
-            return terms[0]
+                    words = parted_late[:, a, 2 * (g * H + u * P) : 2 * (g * H + (u + 1) * P)]
+                nc.tensor.matmul_mx(
+                    out=bank[:],
+                    lhsT=words.bitcast(FP4X4),
+                    lhsT_scale=tab_planes[a][:, s0 : s0 + P],
+                    rhs=w_codes[a][:].bitcast(FP8X4),
+                    rhs_scale=w_plane[a][:],
+                    start=(a == passes[0]),
+                    stop=(a == passes[1]),
+                )
+            return bank
+
+        def scaled(g, jt, b):
+            bank = look_up(g, jt, b)
+            term = sb("term%d_%d" % (g, jt), [P, N], F32)
+            nc.scalar.activation(term[:], bank[:], COPY, scale=iw_col(g, jt))
+            return term
+
+        def added(g, jt, b, earlier):
+            bank = look_up(g, jt, b)
+            term = sb("term%d_%d" % (g, jt), [P, N], F32)
+            nc.vector.scalar_tensor_tensor(term[:], bank[:], iw_col(g, jt), earlier[:], ALU.mult, ALU.add)
+            return term
 
         def turn(turned, term, first, last):
             for c in range(4):
@@ -154,91 +180,91 @@ def tile_list_interp_hl_res_kernel(tc, tab_words, tab_scales, w, x, wx, iw0, iw1
                     start=(first and c == 0), stop=(last and c == 3), is_transpose=True,
                 )
 
-        turned = []
-        for jt in range(2):
-            summed = look_up(jt)
-            turned.append(bank_tile("turned%d" % jt, [P, 4, P], 6 + jt))
-            turn(turned[jt], summed, True, False)
-
-        part_codes = [sb("part_codes%d" % h, [P, 2 * H], U32) for h in range(2)]
-        part_plane = [sb("part_plane%d" % h, [P, 2 * H], U8) for h in range(2)]
-        for h in range(2):
+        def top_half(h):
             top = sb("top%d" % h, [P, H, 4], BF16)
-            wx_top = wx_raw[h].bitcast(BF16).rearrange("p t (c i e) -> p c t i e", i=4, e=2)[:, :, :, :, 1]
-            nc.scalar.copy(top[:].rearrange("p (c i) t -> p c t i", i=4), wx_top)
+            upper = wx_raw[h].bitcast(BF16).rearrange("p t (c i e) -> p c t i e", i=4, e=2)[:, :, :, :, 1]
+            nc.scalar.copy(top[:].rearrange("p (c i) t -> p c t i", i=4), upper)
+            return top
+
+        def mask_half(h, top):
             split = sb("split%d" % h, [P, 2 * H, 4], BF16)
-            hi, lo = split[:, 0:H, :], split[:, H : 2 * H, :]
             nc.vector.tensor_scalar(
-                hi.rearrange("p c t -> p (c t)").bitcast(I32),
+                split[:, 0:H, :].rearrange("p c t -> p (c t)").bitcast(I32),
                 top[:].rearrange("p c t -> p (c t)").bitcast(I32),
                 HI_MASK, None, ALU.bitwise_and,
             )
+            return split
+
+        def rest_half(h, split):
             nc.vector.tensor_tensor(
-                lo.rearrange("p (c i) t -> p c t i", i=4),
+                split[:, H : 2 * H, :].rearrange("p (c i) t -> p c t i", i=4),
                 wx_raw[h].rearrange("p t (c i) -> p c t i", i=4),
-                hi.rearrange("p (c i) t -> p c t i", i=4),
+                split[:, 0:H, :].rearrange("p (c i) t -> p c t i", i=4),
                 ALU.subtract,
             )
-            quantize(split[:], part_codes[h][:], part_plane[h][:])
+
+        part_codes = [sb("part_codes%d" % h, [P, 2 * H], U32) for h in range(2)]
+        part_plane = [sb("part_plane%d" % h, [P, 2 * H], U8) for h in range(2)]
         x_codes = [sb("x_codes%d" % h, [P, H], U32) for h in range(2)]
         x_plane = [sb("x_plane%d" % h, [P, H], U8) for h in range(2)]
-        for h in range(2):
-            x_woven = sb("x_woven%d" % h, [P, H, 4], BF16)
-            weave(x_woven[:], x_raw[h])
-            quantize(x_woven[:], x_codes[h][:], x_plane[h][:])
+        x_woven = [at("x_woven%d" % h, [P, H, 4], BF16, 36864 + 2048 * h) for h in range(2)]
+        own = [sb("own%d" % h, [P, 4, H], F32) for h in range(2)]
+        out_rows = out.rearrange("(c p) j -> p c j", p=P)
 
-        late = [look_up(jt) for jt in range(2, 4)]
-
-        def skip_turned(jt):
-            bank = bank_tile("ax%d" % jt, [P, 2, H], G * jt)
+        def skip(h, cp, b):
+            bank = bank_tile("ax%d_%d" % (h, cp), [P, 2, H], b)
             for e in range(2):
                 for s in range(2):
+                    c0 = s * H + e * P
                     nc.tensor.matmul_mx(
                         out=bank[:, e, :],
-                        lhsT=x_codes[0][:, jt * P : (jt + 1) * P].bitcast(FP8X4),
-                        lhsT_scale=x_plane[0][:, jt * P : (jt + 1) * P],
-                        rhs=part_codes[e][:, s * H : (s + 1) * H].bitcast(FP8X4),
-                        rhs_scale=part_plane[e][:, s * H : (s + 1) * H],
+                        lhsT=part_codes[cp][:, c0 : c0 + P].bitcast(FP8X4),
+                        lhsT_scale=part_plane[cp][:, c0 : c0 + P],
+                        rhs=x_codes[h][:].bitcast(FP8X4),
+                        rhs_scale=x_plane[h][:],
                         start=(s == 0),
                         stop=(s == 1),
                     )
-            own = sb("own%d" % jt, [P, N], F32)
-            nc.scalar.activation(own[:], bank[:].rearrange("p e c -> p (e c)"), COPY)
-            turn(turned[jt], own, False, True)
+            nc.vector.tensor_tensor(own[h][:, 2 * cp : 2 * cp + 2, :], bank[:], res_sb[:, 2 * cp : 2 * cp + 2, h * H : (h + 1) * H], ALU.add)
 
-        def skip_upright():
-            own = sb("own_late", [P, 4, H], F32)
-            for cp in range(2):
-                bank = bank_tile("ax_late%d" % cp, [P, 2, H], 1 + cp)
-                for e in range(2):
-                    for s in range(2):
-                        c0 = s * H + e * P
-                        nc.tensor.matmul_mx(
-                            out=bank[:, e, :],
-                            lhsT=part_codes[cp][:, c0 : c0 + P].bitcast(FP8X4),
-                            lhsT_scale=part_plane[cp][:, c0 : c0 + P],
-                            rhs=x_codes[1][:].bitcast(FP8X4),
-                            rhs_scale=x_plane[1][:],
-                            start=(s == 0),
-                            stop=(s == 1),
-                        )
-                nc.vector.tensor_tensor(own[:, 2 * cp : 2 * cp + 2, :], bank[:], res_sb[:, 2 * cp : 2 * cp + 2, H:J], ALU.add)
-            return own
-
-        out_rows = out.rearrange("(c p) j -> p c j", p=P)
-
-        def finish(jt, addend):
+        def finish(jt, turned):
+            h, u = divmod(jt, 2)
             done = sb("done%d" % jt, [P, 4, P], F32)
-            nc.vector.tensor_tensor(done[:], turned[jt][:], addend, ALU.add)
+            nc.vector.tensor_tensor(done[:], turned[:], own[h][:, :, u * P : (u + 1) * P], ALU.add)
             nc.sync.dma_start(out_rows[:, :, jt * P : (jt + 1) * P], done[:])
 
-        for jt in range(2):
-            skip_turned(jt)
+        tops = [top_half(h) for h in range(2)]
+        first = [scaled(0, u, u) for u in range(2)]
+        second = [scaled(1, u, 2 + u) for u in range(2)]
+        splits = [mask_half(h, tops[h]) for h in range(2)]
+        for h in range(2):
+            rest_half(h, splits[h])
+        turned = [bank_tile("turned%d" % u, [P, 4, P], 4 + u) for u in range(2)]
+        for h in range(2):
+            weave(x_woven[h][:], x_raw[:, :, h * H : (h + 1) * H])
+        third = [scaled(2, u, u) for u in range(2)]
+        late = [[scaled(0, 2, 2), scaled(1, 2, 3)]]
         for u in range(2):
-            turned.append(bank_tile("turned%d" % (2 + u), [P, 4, P], 4 + u))
-            turn(turned[2 + u], late[u], True, True)
-        for jt in range(2):
-            finish(jt, res_sb[:, :, jt * P : (jt + 1) * P])
-        own_late = skip_upright()
+            turn(turned[u], first[u], True, False)
+            turn(turned[u], second[u], False, False)
+        late.append([scaled(0, 3, 0), scaled(1, 3, 1)])
         for u in range(2):
-            finish(2 + u, own_late[:, :, u * P : (u + 1) * P])
+            turn(turned[u], third[u], False, True)
+        quantize(splits[0][:], part_codes[0][:], part_plane[0][:])
+        quantize(x_woven[0][:], x_codes[0][:], x_plane[0][:])
+        quantize(splits[1][:], part_codes[1][:], part_plane[1][:])
+        quantize(x_woven[1][:], x_codes[1][:], x_plane[1][:])
+        for u in range(2):
+            late[u][1] = added(2, 2 + u, 2 + u, late[u][1])
+        skip(0, 0, 6)
+        skip(0, 1, 7)
+        skip(1, 0, 0)
+        skip(1, 1, 1)
+        for u in range(2):
+            finish(u, turned[u])
+        for u in range(2):
+            turned.append(bank_tile("turned%d" % (2 + u), [P, 4, P], 6 + u))
+            turn(turned[2 + u], late[u][0], True, False)
+            turn(turned[2 + u], late[u][1], False, True)
+        for u in range(2):
+            finish(2 + u, turned[2 + u])

@@ -48,7 +48,7 @@ def tile_list_interp_hl_res_kernel(tc, tab_words, tab_scales, w, x, wx, iw0, iw1
         nc.gpsimd.memset(scale_tab[:].bitcast(I32), 0)
         for q in range(4):
             nc.sync.dma_start(scale_tab[32 * q : 32 * q + 4, :].bitcast(I32), tab_scales[0, 4 * q : 4 * q + 4, :].bitcast(I32))
-        nc.sync.dma_start(scale_tab[4:P:8, :].bitcast(I32), tab_scales[1].bitcast(I32))
+        nc.sync.dma_start(scale_tab[8:24, :].bitcast(I32), tab_scales[1].bitcast(I32))
 
         ident = sb("ident", [P, P], F32)
         pieces = ((0, 32, 4096 - 64), (32, 64, 20992 - 64), (64, 128, 29184))
@@ -78,7 +78,7 @@ def tile_list_interp_hl_res_kernel(tc, tab_words, tab_scales, w, x, wx, iw0, iw1
         scales_p0 = at("scales_p0", [P, G * J], U8, 29184)
         nc.vector.tensor_copy(scales_p0[:], scale_tab[:].indirect(offsets[:]))
         for q in range(4):
-            nc.sync.dma_start(scales_p1[32 * q : 32 * q + 4, :].bitcast(I32), scales_p0[32 * q + 4 : 32 * q + 32 : 8, :].bitcast(I32))
+            nc.sync.dma_start(scales_p1[32 * q : 32 * q + 4, :].bitcast(I32), scales_p0[8 + 4 * q : 12 + 4 * q, :].bitcast(I32))
         tab_planes = (scales_p0, scales_p1)
 
         def weave(woven, raw_cols):
@@ -161,9 +161,10 @@ def tile_list_interp_hl_res_kernel(tc, tab_words, tab_scales, w, x, wx, iw0, iw1
                 )
             return bank
 
-        def scaled(g, jt, b):
+        def scaled(g, jt, b, offset=None):
             bank = look_up(g, jt, b)
-            term = sb("term%d_%d" % (g, jt), [P, N], F32)
+            name = "term%d_%d" % (g, jt)
+            term = sb(name, [P, N], F32) if offset is None else at(name, [P, N], F32, offset)
             nc.scalar.activation(term[:], bank[:], COPY, scale=iw_col(g, jt))
             return term
 
@@ -207,8 +208,10 @@ def tile_list_interp_hl_res_kernel(tc, tab_words, tab_scales, w, x, wx, iw0, iw1
         part_plane = [sb("part_plane%d" % h, [P, 2 * H], U8) for h in range(2)]
         x_codes = [sb("x_codes%d" % h, [P, H], U32) for h in range(2)]
         x_plane = [sb("x_plane%d" % h, [P, H], U8) for h in range(2)]
-        x_woven = [at("x_woven%d" % h, [P, H, 4], BF16, 36864 + 2048 * h) for h in range(2)]
-        own = [sb("own%d" % h, [P, 4, H], F32) for h in range(2)]
+        x_woven = [at("x_woven%d" % h, [P, H, 4], BF16, 36864 - 1024 + 2048 * h) for h in range(2)]
+        own = sb("own", [P, 4, H], F32)
+        early = sb("early", [P, 4, H], F32)
+        early_res = sb("early_res", [P, 4, H], F32)
         out_rows = out.rearrange("(c p) j -> p c j", p=P)
 
         def skip(h, cp, b):
@@ -225,13 +228,17 @@ def tile_list_interp_hl_res_kernel(tc, tab_words, tab_scales, w, x, wx, iw0, iw1
                         start=(s == 0),
                         stop=(s == 1),
                     )
-            nc.vector.tensor_tensor(own[h][:, 2 * cp : 2 * cp + 2, :], bank[:], res_sb[:, 2 * cp : 2 * cp + 2, h * H : (h + 1) * H], ALU.add)
+            return bank
 
-        def finish(jt, turned):
-            h, u = divmod(jt, 2)
-            done = sb("done%d" % jt, [P, 4, P], F32)
-            nc.vector.tensor_tensor(done[:], turned[:], own[h][:, :, u * P : (u + 1) * P], ALU.add)
-            nc.sync.dma_start(out_rows[:, :, jt * P : (jt + 1) * P], done[:])
+        def finish_early(cp, bank):
+            done = at("done_early%d" % cp, [P, 2, H], F32, 61440 - 1024 + 2048 * cp)
+            nc.vector.tensor_tensor(done[:], bank[:], early_res[:, 2 * cp : 2 * cp + 2, :], ALU.add)
+            nc.sync.dma_start(out_rows[:, 2 * cp : 2 * cp + 2, 0:H], done[:])
+
+        def finish_late(u, turned):
+            done = sb("done_late%d" % u, [P, 4, P], F32)
+            nc.vector.tensor_tensor(done[:], turned[:], own[:, :, u * P : (u + 1) * P], ALU.add)
+            nc.sync.dma_start(out_rows[:, :, H + u * P : H + (u + 1) * P], done[:])
 
         tops = [top_half(h) for h in range(2)]
         first = [scaled(0, u, u) for u in range(2)]
@@ -240,31 +247,35 @@ def tile_list_interp_hl_res_kernel(tc, tab_words, tab_scales, w, x, wx, iw0, iw1
         for h in range(2):
             rest_half(h, splits[h])
         turned = [bank_tile("turned%d" % u, [P, 4, P], 4 + u) for u in range(2)]
-        for h in range(2):
+        for h in (1, 0):
             weave(x_woven[h][:], x_raw[:, :, h * H : (h + 1) * H])
         third = [scaled(2, u, u) for u in range(2)]
         late = [[scaled(0, 2, 2), scaled(1, 2, 3)]]
         for u in range(2):
             turn(turned[u], first[u], True, False)
             turn(turned[u], second[u], False, False)
-        late.append([scaled(0, 3, 0), scaled(1, 3, 1)])
         for u in range(2):
             turn(turned[u], third[u], False, True)
+        for u in range(2):
+            cols = slice(u * P, (u + 1) * P)
+            nc.scalar.activation(early[:, :, cols], turned[u][:], COPY)
+            nc.gpsimd.tensor_tensor(early_res[:, :, cols], early[:, :, cols], res_sb[:, :, cols], ALU.add)
+        late.append([scaled(0, 3, 0, 61440), scaled(1, 3, 1)])
         quantize(splits[0][:], part_codes[0][:], part_plane[0][:])
-        quantize(x_woven[0][:], x_codes[0][:], x_plane[0][:])
-        quantize(splits[1][:], part_codes[1][:], part_plane[1][:])
         quantize(x_woven[1][:], x_codes[1][:], x_plane[1][:])
+        quantize(splits[1][:], part_codes[1][:], part_plane[1][:])
+        quantize(x_woven[0][:], x_codes[0][:], x_plane[0][:])
+        late[0][0] = added(2, 2, 2, late[0][0])
+        for cp in range(2):
+            bank = skip(1, cp, 6 + cp)
+            nc.vector.tensor_tensor(own[:, 2 * cp : 2 * cp + 2, :], bank[:], res_sb[:, 2 * cp : 2 * cp + 2, H:J], ALU.add)
+        late[1][0] = added(2, 3, 3, late[1][0])
+        ax_early = [skip(0, cp, 4 + cp) for cp in range(2)]
         for u in range(2):
-            late[u][1] = added(2, 2 + u, 2 + u, late[u][1])
-        skip(0, 0, 6)
-        skip(0, 1, 7)
-        skip(1, 0, 0)
-        skip(1, 1, 1)
-        for u in range(2):
-            finish(u, turned[u])
-        for u in range(2):
-            turned.append(bank_tile("turned%d" % (2 + u), [P, 4, P], 6 + u))
-            turn(turned[2 + u], late[u][0], True, False)
-            turn(turned[2 + u], late[u][1], False, True)
-        for u in range(2):
-            finish(2 + u, turned[2 + u])
+            turned.append(bank_tile("turned%d" % (2 + u), [P, 4, P], 2 - 2 * u))
+            turn(turned[2 + u], late[u][1], True, False)
+            turn(turned[2 + u], late[u][0], False, True)
+        finish_late(0, turned[2])
+        for cp in range(2):
+            finish_early(cp, ax_early[cp])
+        finish_late(1, turned[3])

@@ -235,10 +235,10 @@ def tile_list_interp_hl_res_kernel(tc, tab_words, tab_scales, w, x, wx, iw0, iw1
             nc.vector.tensor_tensor(done[:], bank[:], early_res[:, 2 * cp : 2 * cp + 2, :], ALU.add)
             nc.sync.dma_start(out_rows[:, 2 * cp : 2 * cp + 2, 0:H], done[:])
 
-        def finish_late(u, turned):
-            done = sb("done_late%d" % u, [P, 4, P], F32)
-            nc.vector.tensor_tensor(done[:], turned[:], own[:, :, u * P : (u + 1) * P], ALU.add)
-            nc.sync.dma_start(out_rows[:, :, H + u * P : H + (u + 1) * P], done[:])
+        def finish_late(u, turned, c0, c1):
+            done = sb("done_late%d_%d" % (u, c0), [P, c1 - c0, P], F32)
+            nc.vector.tensor_tensor(done[:], turned[:, c0:c1, :], own[:, c0:c1, u * P : (u + 1) * P], ALU.add)
+            nc.sync.dma_start(out_rows[:, c0:c1, H + u * P : H + (u + 1) * P], done[:])
 
         tops = [top_half(h) for h in range(2)]
         first = [scaled(0, u, u) for u in range(2)]
@@ -249,13 +249,11 @@ def tile_list_interp_hl_res_kernel(tc, tab_words, tab_scales, w, x, wx, iw0, iw1
         turned = [bank_tile("turned%d" % u, [P, 4, P], 4 + u) for u in range(2)]
         for h in (1, 0):
             weave(x_woven[h][:], x_raw[:, :, h * H : (h + 1) * H])
-        third = [scaled(2, u, u) for u in range(2)]
+        second = [added(2, u, u, second[u]) for u in range(2)]
         late = [[scaled(0, 2, 2), scaled(1, 2, 3)]]
         for u in range(2):
             turn(turned[u], first[u], True, False)
-            turn(turned[u], second[u], False, False)
-        for u in range(2):
-            turn(turned[u], third[u], False, True)
+            turn(turned[u], second[u], False, True)
         for u in range(2):
             cols = slice(u * P, (u + 1) * P)
             nc.scalar.activation(early[:, :, cols], turned[u][:], COPY)
@@ -275,7 +273,8 @@ def tile_list_interp_hl_res_kernel(tc, tab_words, tab_scales, w, x, wx, iw0, iw1
             turned.append(bank_tile("turned%d" % (2 + u), [P, 4, P], 2 - 2 * u))
             turn(turned[2 + u], late[u][1], True, False)
             turn(turned[2 + u], late[u][0], False, True)
-        finish_late(0, turned[2])
+        finish_late(0, turned[2], 0, 4)
         for cp in range(2):
             finish_early(cp, ax_early[cp])
-        finish_late(1, turned[3])
+        finish_late(1, turned[3], 0, 2)
+        finish_late(1, turned[3], 2, 4)

@@ -42,7 +42,6 @@ def tile_list_interp_hl_res_kernel(tc, tab_words, tab_scales, w, x, wx, iw0, iw1
 
         offsets = keep.tile([P, G * J // 16], U16, name="offsets")
         nc.sync.dma_start(offsets[:], offs)
-        w_raw = [load_rows(sb("w_raw0", [P, 4, H], F32)[:], w[0:512, :], 0, H)]
 
         scale_tab = at("scale_tab", [P, T], U8, 55808)
         nc.gpsimd.memset(scale_tab[:].bitcast(I32), 0)
@@ -51,18 +50,18 @@ def tile_list_interp_hl_res_kernel(tc, tab_words, tab_scales, w, x, wx, iw0, iw1
         nc.sync.dma_start(scale_tab[8:24, :].bitcast(I32), tab_scales[1].bitcast(I32))
 
         ident = sb("ident", [P, P], F32)
-        pieces = ((0, 32, 4096 - 64), (32, 64, 20992 - 64), (64, 128, 29184))
-        for c0, c1, edge in pieces:
-            zeros = at("zeros%d" % c0, [P, c1 - c0], F32, edge)
+        for i, edge in enumerate((4096, 12352, 20992, 73728)):
+            zeros = at("zeros%d" % i, [P, 32], F32, edge - 64)
             nc.vector.memset(zeros[:], 0.0)
             nc.gpsimd.affine_select(
-                out=ident[:, c0:c1], in_=zeros[:], compare_op=ALU.not_equal, fill=1.0,
-                base=-c0, pattern=[[-1, c1 - c0]], channel_multiplier=1,
+                out=ident[:, 32 * i : 32 * (i + 1)], in_=zeros[:], compare_op=ALU.not_equal, fill=1.0,
+                base=-32 * i, pattern=[[-1, 32]], channel_multiplier=1,
             )
 
+        w_raw = [load_rows(at("w_raw0", [P, 4, H], F32, 0)[:], w[0:512, :], 0, H)]
         word_tab = at("word_tab", [P, T], I32, 4096)
         nc.sync.dma_start(word_tab[:], tab_words[0].rearrange("p t b -> p (t b)").bitcast(I32))
-        iw_rows = at("iw_rows", [P, P], F32, 4096 - 512)
+        iw_rows = at("iw_rows", [P, P], F32, 12288)
         nc.vector.memset(iw_rows[:], 0.0)
         for g, iw in enumerate((iw0, iw1, iw2)):
             nc.sync.dma_start(iw_rows[4 * g : 4 * g + 4, :], iw.rearrange("(c j) -> c j", c=4))
@@ -71,11 +70,12 @@ def tile_list_interp_hl_res_kernel(tc, tab_words, tab_scales, w, x, wx, iw0, iw1
         for h in range(2):
             cols = w1_raw[:, h * 4 * H : (h + 1) * 4 * H].rearrange("p (t c) -> p t c", t=4)
             w_raw.append(load_rows(cols, w[512:1024, :], h * H, (h + 1) * H))
+        wx_raw = [load_rows(at("wx_raw0", [P, 4, H], F32, 69632)[:], wx, 0, H)]
 
         scales_p1 = sb("scales_p1", [P, G * J], U8)
         nc.gpsimd.memset(scales_p1[:].bitcast(I32), 0)
 
-        scales_p0 = at("scales_p0", [P, G * J], U8, 29184)
+        scales_p0 = at("scales_p0", [P, G * J], U8, 73728)
         nc.vector.tensor_copy(scales_p0[:], scale_tab[:].indirect(offsets[:]))
         for q in range(4):
             nc.sync.dma_start(scales_p1[32 * q : 32 * q + 4, :].bitcast(I32), scales_p0[8 + 4 * q : 12 + 4 * q, :].bitcast(I32))
@@ -116,21 +116,21 @@ def tile_list_interp_hl_res_kernel(tc, tab_words, tab_scales, w, x, wx, iw0, iw1
         for i in range(4):
             weave(w_woven[i][:], w_raw[i])
         nc.scalar.activation(iw_cols[:], iw_ps[:, 0:16], COPY)
-        pairs = [sb("pairs0", [P, H], U32), at("pairs1", [P, H], U32, 35840), at("pairs2", [P, H], U32, 37888)]
-        parted = [sb("parted0", [P, 2, 2 * H], U8), at("parted1", [P, 2, 2 * H], U8, 36864), sb("parted2", [P, 2, 2 * H], U8)]
+        pairs = [sb("pairs0", [P, H], U32), sb("pairs1", [P, H], U32), at("pairs2", [P, H], U32, 33792)]
+        parted = [sb("parted0", [P, 2, 2 * H], U8), at("parted1", [P, 2, 2 * H], U8, 32768), at("parted2", [P, 2, 2 * H], U8, 34816)]
         quantize_w(0)
         pick_words(pairs[0][:], 0, 0)
+        pick_words(pairs[1][:], 1, 0)
         part_words(parted[0], pairs[0])
         quantize_w(1)
-        quantize_w(2)
-        pick_words(pairs[1][:], 1, 0)
-        quantize_w(3)
-        pick_words(pairs[2][:], 2, 0)
         part_words(parted[1], pairs[1])
+        pick_words(pairs[2][:], 2, 0)
+        quantize_w(2)
         part_words(parted[2], pairs[2])
-        wx_raw = [load_rows(at("wx_raw%d" % h, [P, 4, H], F32, 52224 + 4608 * h)[:], wx, h * H, (h + 1) * H) for h in range(2)]
-        x_raw = load_rows(at("x_raw", [P, 4, J], F32, 20992)[:], x, 0, J)
-        pairs_late = at("pairs_late", [P, G * H], U32, 33792)
+        quantize_w(3)
+        wx_raw.append(load_rows(at("wx_raw1", [P, 4, H], F32, 56832)[:], wx, H, N))
+        x_raw = load_rows(at("x_raw", [P, 4, J], F32, 48128)[:], x, 0, J)
+        pairs_late = at("pairs_late", [P, G * H], U32, 36864)
         for g in range(G):
             pick_words(pairs_late[:, g * H : (g + 1) * H], g, 1)
         parted_late = sb("parted_late", [P, 2, 2 * G * H], U8)
@@ -188,7 +188,7 @@ def tile_list_interp_hl_res_kernel(tc, tab_words, tab_scales, w, x, wx, iw0, iw1
             return top
 
         def mask_half(h, top):
-            split = sb("split%d" % h, [P, 2 * H, 4], BF16)
+            split = at("split%d" % h, [P, 2 * H, 4], BF16, 77824 + 4096 * h)
             nc.vector.tensor_scalar(
                 split[:, 0:H, :].rearrange("p c t -> p (c t)").bitcast(I32),
                 top[:].rearrange("p c t -> p (c t)").bitcast(I32),
@@ -208,7 +208,7 @@ def tile_list_interp_hl_res_kernel(tc, tab_words, tab_scales, w, x, wx, iw0, iw1
         part_plane = [sb("part_plane%d" % h, [P, 2 * H], U8) for h in range(2)]
         x_codes = [sb("x_codes%d" % h, [P, H], U32) for h in range(2)]
         x_plane = [sb("x_plane%d" % h, [P, H], U8) for h in range(2)]
-        x_woven = [at("x_woven%d" % h, [P, H, 4], BF16, 36864 - 1024 + 2048 * h) for h in range(2)]
+        x_woven = [at("x_woven%d" % h, [P, H, 4], BF16, 34816 - 2048 * h) for h in range(2)]
         own = sb("own", [P, 4, H], F32)
         early = sb("early", [P, 4, H], F32)
         early_res = sb("early_res", [P, 4, H], F32)
@@ -242,14 +242,15 @@ def tile_list_interp_hl_res_kernel(tc, tab_words, tab_scales, w, x, wx, iw0, iw1
 
         tops = [top_half(h) for h in range(2)]
         first = [scaled(0, u, u) for u in range(2)]
-        second = [scaled(1, u, 2 + u) for u in range(2)]
-        splits = [mask_half(h, tops[h]) for h in range(2)]
-        for h in range(2):
-            rest_half(h, splits[h])
+        second = [scaled(1, u, 2 + u, 81920 + 2048 * u) for u in range(2)]
+        splits = [mask_half(0, tops[0])]
+        rest_half(0, splits[0])
         turned = [bank_tile("turned%d" % u, [P, 4, P], 4 + u) for u in range(2)]
         for h in (1, 0):
             weave(x_woven[h][:], x_raw[:, :, h * H : (h + 1) * H])
         second = [added(2, u, u, second[u]) for u in range(2)]
+        splits.append(mask_half(1, tops[1]))
+        rest_half(1, splits[1])
         late = [[scaled(0, 2, 2), scaled(1, 2, 3)]]
         for u in range(2):
             turn(turned[u], first[u], True, False)
@@ -263,14 +264,14 @@ def tile_list_interp_hl_res_kernel(tc, tab_words, tab_scales, w, x, wx, iw0, iw1
         quantize(x_woven[1][:], x_codes[1][:], x_plane[1][:])
         quantize(splits[1][:], part_codes[1][:], part_plane[1][:])
         quantize(x_woven[0][:], x_codes[0][:], x_plane[0][:])
-        late[0][0] = added(2, 2, 2, late[0][0])
+        late[0][0] = added(2, 2, 6, late[0][0])
         for cp in range(2):
-            bank = skip(1, cp, 6 + cp)
+            bank = skip(1, cp, 2 + cp)
             nc.vector.tensor_tensor(own[:, 2 * cp : 2 * cp + 2, :], bank[:], res_sb[:, 2 * cp : 2 * cp + 2, H:J], ALU.add)
-        late[1][0] = added(2, 3, 3, late[1][0])
+        late[1][0] = added(2, 3, 7, late[1][0])
         ax_early = [skip(0, cp, 4 + cp) for cp in range(2)]
         for u in range(2):
-            turned.append(bank_tile("turned%d" % (2 + u), [P, 4, P], 2 - 2 * u))
+            turned.append(bank_tile("turned%d" % (2 + u), [P, 4, P], 6 - 6 * u))
             turn(turned[2 + u], late[u][1], True, False)
             turn(turned[2 + u], late[u][0], False, True)
         finish_late(0, turned[2], 0, 4)

@@ -183,12 +183,15 @@ def tile_list_interp_hl_res_kernel(tc, tab_words, tab_scales, w, x, wx, iw0, iw1
 
         def top_half(h):
             top = sb("top%d" % h, [P, H, 4], BF16)
-            upper = wx_raw[h].bitcast(BF16).rearrange("p t (c i e) -> p c t i e", i=4, e=2)[:, :, :, :, 1]
-            nc.scalar.copy(top[:].rearrange("p (c i) t -> p c t i", i=4), upper)
+            if h == 0:
+                upper = wx_raw[h].bitcast(BF16).rearrange("p t (c i e) -> p c t i e", i=4, e=2)[:, :, :, :, 1]
+                nc.scalar.copy(top[:].rearrange("p (c i) t -> p c t i", i=4), upper)
+            else:
+                nc.gpsimd.tensor_copy(top[:], wx_raw[h].bitcast(BF16).rearrange("p t (c e) -> p c t e", e=2)[:, :, :, 1])
             return top
 
         def mask_half(h, top):
-            split = at("split%d" % h, [P, 2 * H, 4], BF16, 77824 + 4096 * h)
+            split = sb("split%d" % h, [P, 2 * H, 4], BF16)
             nc.vector.tensor_scalar(
                 split[:, 0:H, :].rearrange("p c t -> p (c t)").bitcast(I32),
                 top[:].rearrange("p c t -> p (c t)").bitcast(I32),
@@ -242,19 +245,18 @@ def tile_list_interp_hl_res_kernel(tc, tab_words, tab_scales, w, x, wx, iw0, iw1
 
         tops = [top_half(h) for h in range(2)]
         first = [scaled(0, u, u) for u in range(2)]
-        second = [scaled(1, u, 2 + u, 81920 + 2048 * u) for u in range(2)]
-        splits = [mask_half(0, tops[0])]
-        rest_half(0, splits[0])
+        second = [scaled(1, u, 2 + u) for u in range(2)]
+        third = [scaled(2, u, u) for u in range(2)]
+        splits = [mask_half(h, tops[h]) for h in range(2)]
+        for h in range(2):
+            rest_half(h, splits[h])
         turned = [bank_tile("turned%d" % u, [P, 4, P], 4 + u) for u in range(2)]
         for h in (1, 0):
             weave(x_woven[h][:], x_raw[:, :, h * H : (h + 1) * H])
-        second = [added(2, u, u, second[u]) for u in range(2)]
-        splits.append(mask_half(1, tops[1]))
-        rest_half(1, splits[1])
         late = [[scaled(0, 2, 2), scaled(1, 2, 3)]]
-        for u in range(2):
-            turn(turned[u], first[u], True, False)
-            turn(turned[u], second[u], False, True)
+        for i, terms in enumerate((first, second, third)):
+            for u in range(2):
+                turn(turned[u], terms[u], i == 0, i == 2)
         for u in range(2):
             cols = slice(u * P, (u + 1) * P)
             nc.scalar.activation(early[:, :, cols], turned[u][:], COPY)

@@ -81,12 +81,11 @@ def tile_list_interp_hl_res_kernel(tc, tab_words, tab_scales, w, x, wx, iw0, iw1
             nc.sync.dma_start(scales_p1[32 * q : 32 * q + 4, :].bitcast(I32), scales_p0[8 + 4 * q : 12 + 4 * q, :].bitcast(I32))
         tab_planes = (scales_p0, scales_p1)
 
+        def by_lines(woven, raw_cols):
+            return woven.rearrange("p (c i) t -> p c t i", i=4), raw_cols.rearrange("p t (c i) -> p c t i", i=4)
+
         def weave(woven, raw_cols):
-            nc.scalar.activation(
-                woven.rearrange("p (c i) t -> p c t i", i=4),
-                raw_cols.rearrange("p t (c i) -> p c t i", i=4),
-                COPY,
-            )
+            nc.scalar.activation(*by_lines(woven, raw_cols), COPY)
 
         def quantize(woven, codes, plane):
             nc.vector.quantize_mx(out=codes.bitcast(FP8X4), scales=plane, in_=woven.rearrange("p c t -> p (c t)"))
@@ -106,15 +105,16 @@ def tile_list_interp_hl_res_kernel(tc, tab_words, tab_scales, w, x, wx, iw0, iw1
         iw_cols = sb("iw_cols", [P, 16], F32)
 
         w_codes = [sb("w_codes%d" % a, [P, N], U32) for a in range(2)]
-        w_plane = [at("w_plane0", [P, N], U8, 56320), sb("w_plane1", [P, N], U8)]
+        w_plane = [at("w_plane0", [P, N], U8, 56832), sb("w_plane1", [P, N], U8)]
         w_woven = [at("w_woven%d" % i, [P, H, 4], BF16, 30720 + 2048 * i) for i in range(4)]
 
         def quantize_w(i):
             a, h = divmod(i, 2)
             quantize(w_woven[i][:], w_codes[a][:, h * H : (h + 1) * H], w_plane[a][:, h * H : (h + 1) * H])
 
-        for i in range(4):
+        for i in range(3):
             weave(w_woven[i][:], w_raw[i])
+        weave(w_woven[3][:, 0:P, :], w_raw[3][:, :, 0:P])
         nc.scalar.activation(iw_cols[:], iw_ps[:, 0:16], COPY)
         pairs = [sb("pairs0", [P, H], U32), sb("pairs1", [P, H], U32), at("pairs2", [P, H], U32, 33792)]
         parted = [sb("parted0", [P, 2, 2 * H], U8), at("parted1", [P, 2, 2 * H], U8, 32768), at("parted2", [P, 2, 2 * H], U8, 34816)]
@@ -126,9 +126,10 @@ def tile_list_interp_hl_res_kernel(tc, tab_words, tab_scales, w, x, wx, iw0, iw1
         part_words(parted[1], pairs[1])
         pick_words(pairs[2][:], 2, 0)
         quantize_w(2)
+        nc.vector.tensor_copy(*by_lines(w_woven[3][:, P:H, :], w_raw[3][:, :, P:H]))
         part_words(parted[2], pairs[2])
         quantize_w(3)
-        wx_raw.append(load_rows(at("wx_raw1", [P, 4, H], F32, 56832)[:], wx, H, N))
+        wx_raw.append(load_rows(at("wx_raw1", [P, 4, H], F32, 57344)[:], wx, H, N))
         x_raw = load_rows(at("x_raw", [P, 4, J], F32, 48128)[:], x, 0, J)
         pairs_late = at("pairs_late", [P, G * H], U32, 36864)
         for g in range(G):
@@ -144,7 +145,7 @@ def tile_list_interp_hl_res_kernel(tc, tab_words, tab_scales, w, x, wx, iw0, iw1
             h, u = divmod(jt, 2)
             bank = bank_tile("a%d_%d" % (g, jt), [P, N], b)
             s0 = g * J + jt * P
-            passes = (0, 1) if (g, h) == (0, 0) else (1, 0)
+            passes = (0, 1) if g < 2 and h == 0 else (1, 0)
             for a in passes:
                 if h == 0:
                     words = parted[g][:, a, 2 * u * P : 2 * (u + 1) * P]
@@ -213,7 +214,7 @@ def tile_list_interp_hl_res_kernel(tc, tab_words, tab_scales, w, x, wx, iw0, iw1
         x_plane = [sb("x_plane%d" % h, [P, H], U8) for h in range(2)]
         x_woven = [at("x_woven%d" % h, [P, H, 4], BF16, 34816 - 2048 * h) for h in range(2)]
         own = sb("own", [P, 4, H], F32)
-        early = sb("early", [P, 4, H], F32)
+        early = at("early", [P, 4, H], F32, 44544)
         early_res = sb("early_res", [P, 4, H], F32)
         out_rows = out.rearrange("(c p) j -> p c j", p=P)
 
@@ -234,7 +235,7 @@ def tile_list_interp_hl_res_kernel(tc, tab_words, tab_scales, w, x, wx, iw0, iw1
             return bank
 
         def finish_early(cp, bank):
-            done = at("done_early%d" % cp, [P, 2, H], F32, 61440 - 1024 + 2048 * cp)
+            done = at("done_early%d" % cp, [P, 2, H], F32, 54784 + 8192 * cp)
             nc.vector.tensor_tensor(done[:], bank[:], early_res[:, 2 * cp : 2 * cp + 2, :], ALU.add)
             nc.sync.dma_start(out_rows[:, 2 * cp : 2 * cp + 2, 0:H], done[:])
 
@@ -246,14 +247,14 @@ def tile_list_interp_hl_res_kernel(tc, tab_words, tab_scales, w, x, wx, iw0, iw1
         tops = [top_half(h) for h in range(2)]
         first = [scaled(0, u, u) for u in range(2)]
         second = [scaled(1, u, 2 + u) for u in range(2)]
-        third = [scaled(2, u, u) for u in range(2)]
+        third = [scaled(2, u, 6 + u) for u in range(2)]
         splits = [mask_half(h, tops[h]) for h in range(2)]
         for h in range(2):
             rest_half(h, splits[h])
         turned = [bank_tile("turned%d" % u, [P, 4, P], 4 + u) for u in range(2)]
         for h in (1, 0):
             weave(x_woven[h][:], x_raw[:, :, h * H : (h + 1) * H])
-        late = [[scaled(0, 2, 2), scaled(1, 2, 3)]]
+        late = [[scaled(0, 2, 2, 48640), scaled(1, 2, 3, 50688)]]
         for i, terms in enumerate((first, second, third)):
             for u in range(2):
                 turn(turned[u], terms[u], i == 0, i == 2)
@@ -261,7 +262,7 @@ def tile_list_interp_hl_res_kernel(tc, tab_words, tab_scales, w, x, wx, iw0, iw1
             cols = slice(u * P, (u + 1) * P)
             nc.scalar.activation(early[:, :, cols], turned[u][:], COPY)
             nc.gpsimd.tensor_tensor(early_res[:, :, cols], early[:, :, cols], res_sb[:, :, cols], ALU.add)
-        late.append([scaled(0, 3, 0, 61440), scaled(1, 3, 1)])
+        late.append([scaled(0, 3, 0, 54784), scaled(1, 3, 1, 52736)])
         quantize(splits[0][:], part_codes[0][:], part_plane[0][:])
         quantize(x_woven[1][:], x_codes[1][:], x_plane[1][:])
         quantize(splits[1][:], part_codes[1][:], part_plane[1][:])

@@ -1,6 +1,7 @@
 from contextlib import ExitStack
 
 import concourse.mybir as mybir
+from concourse.masks import make_identity
 
 K, L, N, T, J = 1024, 512, 512, 2048, 512
 G = 3
@@ -42,6 +43,7 @@ def tile_list_interp_hl_res_kernel(tc, tab_words, tab_scales, w, x, wx, iw0, iw1
 
         offsets = keep.tile([P, G * J // 16], U16, name="offsets")
         nc.sync.dma_start(offsets[:], offs)
+        w_head = load_rows(sb("w_head", [P, 4, P], F32)[:], w[0:512, :], 0, P)
 
         scale_tab = at("scale_tab", [P, T], U8, 55808)
         nc.gpsimd.memset(scale_tab[:].bitcast(I32), 0)
@@ -50,15 +52,9 @@ def tile_list_interp_hl_res_kernel(tc, tab_words, tab_scales, w, x, wx, iw0, iw1
         nc.sync.dma_start(scale_tab[8:24, :].bitcast(I32), tab_scales[1].bitcast(I32))
 
         ident = sb("ident", [P, P], F32)
-        for i, edge in enumerate((4096, 12352, 20992, 73728)):
-            zeros = at("zeros%d" % i, [P, 32], F32, edge - 64)
-            nc.vector.memset(zeros[:], 0.0)
-            nc.gpsimd.affine_select(
-                out=ident[:, 32 * i : 32 * (i + 1)], in_=zeros[:], compare_op=ALU.not_equal, fill=1.0,
-                base=-32 * i, pattern=[[-1, 32]], channel_multiplier=1,
-            )
+        make_identity(nc, ident[:])
 
-        w_raw = [load_rows(at("w_raw0", [P, 4, H], F32, 0)[:], w[0:512, :], 0, H)]
+        w_raw = [load_rows(sb("w_raw0", [P, 4, P], F32)[:], w[0:512, :], P, H)]
         word_tab = at("word_tab", [P, T], I32, 4096)
         nc.sync.dma_start(word_tab[:], tab_words[0].rearrange("p t b -> p (t b)").bitcast(I32))
         iw_rows = at("iw_rows", [P, P], F32, 12288)
@@ -112,7 +108,9 @@ def tile_list_interp_hl_res_kernel(tc, tab_words, tab_scales, w, x, wx, iw0, iw1
             a, h = divmod(i, 2)
             quantize(w_woven[i][:], w_codes[a][:, h * H : (h + 1) * H], w_plane[a][:, h * H : (h + 1) * H])
 
-        for i in range(3):
+        weave(w_woven[0][:, 0:P, :], w_head)
+        weave(w_woven[0][:, P:H, :], w_raw[0])
+        for i in range(1, 3):
             weave(w_woven[i][:], w_raw[i])
         weave(w_woven[3][:, 0:P, :], w_raw[3][:, :, 0:P])
         nc.scalar.activation(iw_cols[:], iw_ps[:, 0:16], COPY)

@@ -91,7 +91,7 @@ def tile_list_interp_hl_res_kernel(tc, tab_words, tab_scales, w, x, wx, iw0, iw1
             nc.vector.tensor_copy(pairs, word_tab[:].bitcast(U32).indirect(offsets[:, c0 : c0 + H // 16]))
 
         def part_words(parted, pairs):
-            nc.vector.tensor_copy(parted[:].bitcast(U16), pairs[:].bitcast(U16).rearrange("p (j d) -> p d j", d=2))
+            nc.vector.tensor_copy(parted[:].bitcast(U16), pairs.bitcast(U16).rearrange("p (j d) -> p d j", d=2))
 
         def bank_tile(name, shape, b):
             return psum.tile(shape, F32, name=name, tag="bank%d" % b)
@@ -119,21 +119,22 @@ def tile_list_interp_hl_res_kernel(tc, tab_words, tab_scales, w, x, wx, iw0, iw1
         quantize_w(0)
         pick_words(pairs[0][:], 0, 0)
         pick_words(pairs[1][:], 1, 0)
-        part_words(parted[0], pairs[0])
+        part_words(parted[0], pairs[0][:])
         quantize_w(1)
-        part_words(parted[1], pairs[1])
+        part_words(parted[1], pairs[1][:])
         pick_words(pairs[2][:], 2, 0)
         quantize_w(2)
         nc.vector.tensor_copy(*by_lines(w_woven[3][:, P:H, :], w_raw[3][:, :, P:H]))
-        part_words(parted[2], pairs[2])
+        part_words(parted[2], pairs[2][:])
         quantize_w(3)
         wx_raw.append(load_rows(at("wx_raw1", [P, 4, H], F32, 57344)[:], wx, H, N))
         x_raw = load_rows(at("x_raw", [P, 4, J], F32, 48128)[:], x, 0, J)
         pairs_late = at("pairs_late", [P, G * H], U32, 36864)
         for g in range(G):
             pick_words(pairs_late[:, g * H : (g + 1) * H], g, 1)
-        parted_late = sb("parted_late", [P, 2, 2 * G * H], U8)
-        part_words(parted_late, pairs_late)
+        parted_late = [sb("parted_late0", [P, 2, 4 * H], U8), sb("parted_late1", [P, 2, 2 * H], U8)]
+        part_words(parted_late[0], pairs_late[:, 0 : 2 * H])
+        part_words(parted_late[1], pairs_late[:, 2 * H : 3 * H])
         res_sb = at("res_sb", [P, 4, J], F32, 4096)
         nc.sync.dma_start(res_sb[:], res.rearrange("(c p) j -> p c j", p=P))
 
@@ -148,7 +149,7 @@ def tile_list_interp_hl_res_kernel(tc, tab_words, tab_scales, w, x, wx, iw0, iw1
                 if h == 0:
                     words = parted[g][:, a, 2 * u * P : 2 * (u + 1) * P]
                 else:
-                    words = parted_late[:, a, 2 * (g * H + u * P) : 2 * (g * H + (u + 1) * P)]
+                    words = parted_late[g // 2][:, a, 2 * (g % 2 * H + u * P) : 2 * (g % 2 * H + (u + 1) * P)]
                 nc.tensor.matmul_mx(
                     out=bank[:],
                     lhsT=words.bitcast(FP4X4),
@@ -213,7 +214,7 @@ def tile_list_interp_hl_res_kernel(tc, tab_words, tab_scales, w, x, wx, iw0, iw1
         x_woven = [at("x_woven%d" % h, [P, H, 4], BF16, 34816 - 2048 * h) for h in range(2)]
         own = sb("own", [P, 4, H], F32)
         early = at("early", [P, 4, H], F32, 44544)
-        early_res = sb("early_res", [P, 4, H], F32)
+        early_res = [sb("early_res%d" % cp, [P, 2, H], F32) for cp in range(2)]
         out_rows = out.rearrange("(c p) j -> p c j", p=P)
 
         def skip(h, cp, b):
@@ -232,15 +233,14 @@ def tile_list_interp_hl_res_kernel(tc, tab_words, tab_scales, w, x, wx, iw0, iw1
                     )
             return bank
 
-        def finish_early(cp, bank):
-            done = at("done_early%d" % cp, [P, 2, H], F32, 54784 + 8192 * cp)
-            nc.vector.tensor_tensor(done[:], bank[:], early_res[:, 2 * cp : 2 * cp + 2, :], ALU.add)
-            nc.sync.dma_start(out_rows[:, 2 * cp : 2 * cp + 2, 0:H], done[:])
+        def finish_early(cp, bank, e0, e1, done):
+            nc.vector.tensor_tensor(done[:], bank[:, e0:e1, :], early_res[cp][:, e0:e1, :], ALU.add)
+            nc.sync.dma_start(out_rows[:, 2 * cp + e0 : 2 * cp + e1, 0:H], done[:])
 
-        def finish_late(u, turned, c0, c1):
-            done = sb("done_late%d_%d" % (u, c0), [P, c1 - c0, P], F32)
-            nc.vector.tensor_tensor(done[:], turned[:, c0:c1, :], own[:, c0:c1, u * P : (u + 1) * P], ALU.add)
-            nc.sync.dma_start(out_rows[:, c0:c1, H + u * P : H + (u + 1) * P], done[:])
+        def finish_late(u, turned):
+            done = sb("done_late%d" % u, [P, 4, P], F32)
+            nc.vector.tensor_tensor(done[:], turned[:], own[:, :, u * P : (u + 1) * P], ALU.add)
+            nc.sync.dma_start(out_rows[:, :, H + u * P : H + (u + 1) * P], done[:])
 
         tops = [top_half(h) for h in range(2)]
         first = [scaled(0, u, u) for u in range(2)]
@@ -259,7 +259,9 @@ def tile_list_interp_hl_res_kernel(tc, tab_words, tab_scales, w, x, wx, iw0, iw1
         for u in range(2):
             cols = slice(u * P, (u + 1) * P)
             nc.scalar.activation(early[:, :, cols], turned[u][:], COPY)
-            nc.gpsimd.tensor_tensor(early_res[:, :, cols], early[:, :, cols], res_sb[:, :, cols], ALU.add)
+        for cp in range(2):
+            rows = slice(2 * cp, 2 * cp + 2)
+            nc.gpsimd.tensor_tensor(early_res[cp][:], early[:, rows, :], res_sb[:, rows, 0:H], ALU.add)
         late.append([scaled(0, 3, 0, 54784), scaled(1, 3, 1, 52736)])
         quantize(splits[0][:], part_codes[0][:], part_plane[0][:])
         quantize(x_woven[1][:], x_codes[1][:], x_plane[1][:])
@@ -270,13 +272,13 @@ def tile_list_interp_hl_res_kernel(tc, tab_words, tab_scales, w, x, wx, iw0, iw1
             bank = skip(1, cp, 2 + cp)
             nc.vector.tensor_tensor(own[:, 2 * cp : 2 * cp + 2, :], bank[:], res_sb[:, 2 * cp : 2 * cp + 2, H:J], ALU.add)
         late[1][0] = added(2, 3, 7, late[1][0])
-        ax_early = [skip(0, cp, 4 + cp) for cp in range(2)]
+        ax_early = [skip(0, cp, 2 + cp) for cp in range(2)]
         for u in range(2):
-            turned.append(bank_tile("turned%d" % (2 + u), [P, 4, P], 6 - 6 * u))
+            turned.append(bank_tile("turned%d" % (2 + u), [P, 4, P], 6 - 2 * u))
             turn(turned[2 + u], late[u][1], True, False)
             turn(turned[2 + u], late[u][0], False, True)
-        finish_late(0, turned[2], 0, 4)
-        for cp in range(2):
-            finish_early(cp, ax_early[cp])
-        finish_late(1, turned[3], 0, 2)
-        finish_late(1, turned[3], 2, 4)
+        finish_late(0, turned[2])
+        finish_early(0, ax_early[0], 0, 2, at("done_early0", [P, 2, H], F32, 54784))
+        finish_late(1, turned[3])
+        for e in range(2):
+            finish_early(1, ax_early[1], e, e + 1, sb("done_early1_%d" % e, [P, 1, H], F32))

@@ -66,7 +66,8 @@ def tile_list_interp_hl_res_kernel(tc, tab_words, tab_scales, w, x, wx, iw0, iw1
         for h in range(2):
             cols = w1_raw[:, h * 4 * H : (h + 1) * 4 * H].rearrange("p (t c) -> p t c", t=4)
             w_raw.append(load_rows(cols, w[512:1024, :], h * H, (h + 1) * H))
-        wx_raw = [load_rows(at("wx_raw0", [P, 4, H], F32, 69632)[:], wx, 0, H)]
+        wx_raw = [load_rows(sb("wx_raw0", [P, 4, H], F32)[:], wx, 0, H)]
+        wx_raw.append(load_rows(sb("wx_raw1", [P, 4, P], F32)[:], wx, H, H + P))
 
         scales_p1 = sb("scales_p1", [P, G * J], U8)
         nc.gpsimd.memset(scales_p1[:].bitcast(I32), 0)
@@ -127,9 +128,9 @@ def tile_list_interp_hl_res_kernel(tc, tab_words, tab_scales, w, x, wx, iw0, iw1
         nc.vector.tensor_copy(*by_lines(w_woven[3][:, P:H, :], w_raw[3][:, :, P:H]))
         part_words(parted[2], pairs[2][:])
         quantize_w(3)
-        wx_raw.append(load_rows(at("wx_raw1", [P, 4, H], F32, 57344)[:], wx, H, N))
+        wx_raw.append(load_rows(at("wx_raw2", [P, 4, P], F32, 57344)[:], wx, H + P, N))
         x_raw = load_rows(at("x_raw", [P, 4, J], F32, 48128)[:], x, 0, J)
-        pairs_late = at("pairs_late", [P, G * H], U32, 36864)
+        pairs_late = at("pairs_late", [P, G * H], U32, 37888)
         for g in range(G):
             pick_words(pairs_late[:, g * H : (g + 1) * H], g, 1)
         parted_late = [sb("parted_late0", [P, 2, 4 * H], U8), sb("parted_late1", [P, 2, 2 * H], U8)]
@@ -181,15 +182,6 @@ def tile_list_interp_hl_res_kernel(tc, tab_words, tab_scales, w, x, wx, iw0, iw1
                     start=(first and c == 0), stop=(last and c == 3), is_transpose=True,
                 )
 
-        def top_half(h):
-            top = sb("top%d" % h, [P, H, 4], BF16)
-            if h == 0:
-                upper = wx_raw[h].bitcast(BF16).rearrange("p t (c i e) -> p c t i e", i=4, e=2)[:, :, :, :, 1]
-                nc.scalar.copy(top[:].rearrange("p (c i) t -> p c t i", i=4), upper)
-            else:
-                nc.gpsimd.tensor_copy(top[:], wx_raw[h].bitcast(BF16).rearrange("p t (c e) -> p c t e", e=2)[:, :, :, 1])
-            return top
-
         def mask_half(h, top):
             split = sb("split%d" % h, [P, 2 * H, 4], BF16)
             nc.vector.tensor_scalar(
@@ -199,19 +191,15 @@ def tile_list_interp_hl_res_kernel(tc, tab_words, tab_scales, w, x, wx, iw0, iw1
             )
             return split
 
-        def rest_half(h, split):
-            nc.vector.tensor_tensor(
-                split[:, H : 2 * H, :].rearrange("p (c i) t -> p c t i", i=4),
-                wx_raw[h].rearrange("p t (c i) -> p c t i", i=4),
-                split[:, 0:H, :].rearrange("p (c i) t -> p c t i", i=4),
-                ALU.subtract,
-            )
+        def rest(split, c0, c1, raw_cols):
+            low, raw_lines = by_lines(split[:, H + c0 : H + c1, :], raw_cols)
+            nc.vector.tensor_tensor(low, raw_lines, split[:, c0:c1, :].rearrange("p (c i) t -> p c t i", i=4), ALU.subtract)
 
         part_codes = [sb("part_codes%d" % h, [P, 2 * H], U32) for h in range(2)]
         part_plane = [sb("part_plane%d" % h, [P, 2 * H], U8) for h in range(2)]
         x_codes = [sb("x_codes%d" % h, [P, H], U32) for h in range(2)]
         x_plane = [sb("x_plane%d" % h, [P, H], U8) for h in range(2)]
-        x_woven = [at("x_woven%d" % h, [P, H, 4], BF16, 34816 - 2048 * h) for h in range(2)]
+        x_woven = [at("x_woven%d" % h, [P, H, 4], BF16, 33792 - 2048 * h) for h in range(2)]
         own = sb("own", [P, 4, H], F32)
         early = at("early", [P, 4, H], F32, 44544)
         early_res = [sb("early_res%d" % cp, [P, 2, H], F32) for cp in range(2)]
@@ -242,13 +230,21 @@ def tile_list_interp_hl_res_kernel(tc, tab_words, tab_scales, w, x, wx, iw0, iw1
             nc.vector.tensor_tensor(done[:], turned[:], own[:, :, u * P : (u + 1) * P], ALU.add)
             nc.sync.dma_start(out_rows[:, :, H + u * P : H + (u + 1) * P], done[:])
 
-        tops = [top_half(h) for h in range(2)]
+        tops = [sb("top0", [P, H, 4], BF16), at("top1", [P, H, 4], BF16, 35840)]
+        nc.scalar.copy(
+            tops[0][:].rearrange("p (c i) t -> p c t i", i=4),
+            wx_raw[0].bitcast(BF16).rearrange("p t (c i e) -> p c t i e", i=4, e=2)[:, :, :, :, 1],
+        )
+        for u in range(2):
+            upper = wx_raw[1 + u].bitcast(BF16).rearrange("p t (c e) -> p c t e", e=2)[:, :, :, 1]
+            nc.gpsimd.tensor_copy(tops[1][:, u * P : (u + 1) * P, :], upper)
         first = [scaled(0, u, u) for u in range(2)]
         second = [scaled(1, u, 2 + u) for u in range(2)]
         third = [scaled(2, u, 6 + u) for u in range(2)]
         splits = [mask_half(h, tops[h]) for h in range(2)]
-        for h in range(2):
-            rest_half(h, splits[h])
+        rest(splits[0], 0, H, wx_raw[0])
+        for u in range(2):
+            rest(splits[1], u * P, (u + 1) * P, wx_raw[1 + u])
         turned = [bank_tile("turned%d" % u, [P, 4, P], 4 + u) for u in range(2)]
         for h in (1, 0):
             weave(x_woven[h][:], x_raw[:, :, h * H : (h + 1) * H])

@@ -20,8 +20,16 @@ COPY = mybir.ActivationFunctionType.Copy
 
 P = 128
 H = 256
+TIP = 32
 HI_MASK = -983056
-MX_BANKS = 4
+
+AT_TABLE = 0
+AT_RAW_A1 = 8192
+AT_RAW_B1 = 12288
+AT_TERMS_A = AT_RAW_B1 + 3072
+AT_WOVEN_B1 = 22528
+AT_RAW_A0 = 24576
+AT_X_WOVEN = 28672
 
 
 def tile_list_interp_hl_res_kernel(tc, tab_words, tab_scales, w, x, wx, iw0, iw1, iw2, res, offs, out):
@@ -31,52 +39,18 @@ def tile_list_interp_hl_res_kernel(tc, tab_words, tab_scales, w, x, wx, iw0, iw1
         placed = ctx.enter_context(tc.tile_pool(name="placed", bufs=1))
         psum = ctx.enter_context(tc.psum_pool(name="psum", bufs=1))
 
-        def sb(name, shape, dtype):
-            return keep.tile(shape, dtype, name=name, align_bytes=64)
-
-        def at(name, shape, dtype, offset):
+        def sb(name, shape, dtype, offset=None):
+            if offset is None:
+                return keep.tile(shape, dtype, name=name, align_bytes=64)
             return placed.tile(shape, dtype, name=name, offset=offset, align_bytes=64)
 
-        def load_rows(raw, rows, c0, c1):
-            nc.sync.dma_start(raw, rows.rearrange("(p t) c -> p t c", t=4)[:, :, c0:c1])
+        def load_cols(name, rows, c0, c1, offset=None):
+            raw = sb(name, [P, 4, c1 - c0], F32, offset)
+            nc.sync.dma_start(raw[:], rows.rearrange("(p t) c -> p t c", t=4)[:, :, c0:c1])
             return raw
 
-        offsets = keep.tile([P, G * J // 16], U16, name="offsets")
-        nc.sync.dma_start(offsets[:], offs)
-        w_head = load_rows(sb("w_head", [P, 4, P], F32)[:], w[0:512, :], 0, P)
-
-        scale_tab = at("scale_tab", [P, T], U8, 55808)
-        nc.gpsimd.memset(scale_tab[:].bitcast(I32), 0)
-        for q in range(4):
-            nc.sync.dma_start(scale_tab[32 * q : 32 * q + 4, :].bitcast(I32), tab_scales[0, 4 * q : 4 * q + 4, :].bitcast(I32))
-        nc.sync.dma_start(scale_tab[8:24, :].bitcast(I32), tab_scales[1].bitcast(I32))
-
-        ident = sb("ident", [P, P], F32)
-        make_identity(nc, ident[:])
-
-        w_raw = [load_rows(sb("w_raw0", [P, 4, P], F32)[:], w[0:512, :], P, H)]
-        word_tab = at("word_tab", [P, T], I32, 4096)
-        nc.sync.dma_start(word_tab[:], tab_words[0].rearrange("p t b -> p (t b)").bitcast(I32))
-        iw_rows = at("iw_rows", [P, P], F32, 12288)
-        nc.vector.memset(iw_rows[:], 0.0)
-        for g, iw in enumerate((iw0, iw1, iw2)):
-            nc.sync.dma_start(iw_rows[4 * g : 4 * g + 4, :], iw.rearrange("(c j) -> c j", c=4))
-        w_raw.append(load_rows(at("w_raw1", [P, 4, H], F32, 16896)[:], w[0:512, :], H, N))
-        w1_raw = at("w1_raw", [P, 8 * H], F32, 20992)
-        for h in range(2):
-            cols = w1_raw[:, h * 4 * H : (h + 1) * 4 * H].rearrange("p (t c) -> p t c", t=4)
-            w_raw.append(load_rows(cols, w[512:1024, :], h * H, (h + 1) * H))
-        wx_raw = [load_rows(sb("wx_raw0", [P, 4, H], F32)[:], wx, 0, H)]
-        wx_raw.append(load_rows(sb("wx_raw1", [P, 4, P], F32)[:], wx, H, H + P))
-
-        scales_p1 = sb("scales_p1", [P, G * J], U8)
-        nc.gpsimd.memset(scales_p1[:].bitcast(I32), 0)
-
-        scales_p0 = at("scales_p0", [P, G * J], U8, 73728)
-        nc.vector.tensor_copy(scales_p0[:], scale_tab[:].indirect(offsets[:]))
-        for q in range(4):
-            nc.sync.dma_start(scales_p1[32 * q : 32 * q + 4, :].bitcast(I32), scales_p0[8 + 4 * q : 12 + 4 * q, :].bitcast(I32))
-        tab_planes = (scales_p0, scales_p1)
+        def bank_tile(name, shape, b):
+            return psum.tile(shape, F32, name=name, tag="bank%d" % b)
 
         def by_lines(woven, raw_cols):
             return woven.rearrange("p (c i) t -> p c t i", i=4), raw_cols.rearrange("p t (c i) -> p c t i", i=4)
@@ -87,122 +61,191 @@ def tile_list_interp_hl_res_kernel(tc, tab_words, tab_scales, w, x, wx, iw0, iw1
         def quantize(woven, codes, plane):
             nc.vector.quantize_mx(out=codes.bitcast(FP8X4), scales=plane, in_=woven.rearrange("p c t -> p (c t)"))
 
-        def pick_words(pairs, g, h):
+        def listed(g, h):
             c0 = (g * J + h * H) // 16
-            nc.vector.tensor_copy(pairs, word_tab[:].bitcast(U32).indirect(offsets[:, c0 : c0 + H // 16]))
+            return offsets[:, c0 : c0 + H // 16]
 
-        def part_words(parted, pairs):
+        offsets = keep.tile([P, G * J // 16], U16, name="offsets")
+        nc.sync.dma_start(offsets[:], offs)
+        w_tip = load_cols("w_tip", w[0:512, :], 0, TIP)
+
+        scale_tab = sb("scale_tab", [P, T], U8)
+        nc.vector.memset(scale_tab[:].bitcast(I32), 0)
+        for q in range(4):
+            nc.sync.dma_start(scale_tab[32 * q : 32 * q + 8, :].bitcast(I32), tab_scales[:, 4 * q : 4 * q + 4, :].bitcast(I32))
+        word_tab = sb("word_tab", [P, T], I32, AT_TABLE)
+        nc.sync.dma_start(word_tab[:], tab_words[0].rearrange("p t b -> p (t b)").bitcast(I32))
+
+        iw_rows = sb("iw_rows", [P, P], F32)
+        nc.gpsimd.memset(iw_rows[:], 0.0)
+        for g, iw in enumerate((iw0, iw1, iw2)):
+            nc.gpsimd.dma_start(iw_rows[4 * g : 4 * g + 4, :], iw.rearrange("(c j) -> c j", c=4))
+        ident = sb("ident", [P, P], F32)
+        make_identity(nc, ident[:])
+        moved = [sb("moved%d" % h, [P, G * H], U8) for h in range(2)]
+        for h in range(2):
+            nc.vector.memset(moved[h][:].bitcast(I32), 0)
+
+        raw_a0 = load_cols("raw_a0", w[0:512, :], TIP, H, AT_RAW_A0)
+        raw_a1 = load_cols("raw_a1", w[512:1024, :], 0, H, AT_RAW_A1)
+
+        def pick_scales(h, offset=None):
+            picked = sb("picked%d" % h, [P, G * H], U8, offset)
+            for g in range(G):
+                nc.vector.tensor_copy(picked[:, g * H : (g + 1) * H], scale_tab[:].indirect(listed(g, h)))
+            return picked
+
+        def move_scales(h):
+            for q in range(4):
+                nc.sync.dma_start(moved[h][32 * q : 32 * q + 4, :].bitcast(I32), picked[h][32 * q + 4 : 32 * q + 8, :].bitcast(I32))
+
+        def pick_words(h, lists, offset=None):
+            pairs = sb("pairs%d_%d" % (h, lists[0]), [P, len(lists) * H], U32, offset)
+            for i, g in enumerate(lists):
+                nc.vector.tensor_copy(pairs[:, i * H : (i + 1) * H], word_tab[:].bitcast(U32).indirect(listed(g, h)))
+            return pairs
+
+        def part_words(name, pairs):
+            parted = sb(name, [P, 2, 2 * pairs.shape[1]], U8)
             nc.vector.tensor_copy(parted[:].bitcast(U16), pairs.bitcast(U16).rearrange("p (j d) -> p d j", d=2))
+            return parted
 
-        def bank_tile(name, shape, b):
-            return psum.tile(shape, F32, name=name, tag="bank%d" % b)
+        picked = [pick_scales(0)]
+        move_scales(0)
+        raw_b0 = load_cols("raw_b0", w[0:512, :], H, N)
+        raw_b1 = load_cols("raw_b1", w[512:1024, :], H, N, AT_RAW_B1)
+        wx_raw = [load_cols("wx_raw%d" % cp, wx, cp * H, (cp + 1) * H) for cp in range(2)]
+        x_raw = load_cols("x_raw", x, 0, J)
+
+        w_codes = [sb("w_codes%d" % a, [P, N], U32) for a in range(2)]
+        w_plane = [sb("w_plane%d" % a, [P, N], U8) for a in range(2)]
+        woven_at = {(0, 1): AT_RAW_A0, (1, 1): AT_WOVEN_B1}
+        woven = {(a, s): sb("woven%d_%d" % (a, s), [P, H, 4], BF16, woven_at.get((a, s))) for a in range(2) for s in range(2)}
+
+        def quantize_w(a, s):
+            quantize(woven[a, s][:], w_codes[a][:, s * H : (s + 1) * H], w_plane[a][:, s * H : (s + 1) * H])
+
+        words = [[part_words("parted0_0", pick_words(0, (0, 1))[:])]]
+        weave(woven[0, 0][:, 0:TIP, :], w_tip[:])
+        weave(woven[0, 0][:, TIP:H, :], raw_a0[:])
+        weave(woven[1, 0][:], raw_a1[:])
+        quantize_w(0, 0)
+        pairs = pick_words(0, (2,), AT_RAW_A0)
+        quantize_w(1, 0)
+        words[0].append(part_words("parted0_1", pairs[:]))
+        picked.append(pick_scales(1, AT_RAW_A1))
+        move_scales(1)
 
         iw_ps = bank_tile("iw_ps", [P, P], 7)
         nc.tensor.transpose(iw_ps[:], iw_rows[:], ident[:])
-        iw_cols = sb("iw_cols", [P, 16], F32)
-
-        w_codes = [sb("w_codes%d" % a, [P, N], U32) for a in range(2)]
-        w_plane = [at("w_plane0", [P, N], U8, 56832), sb("w_plane1", [P, N], U8)]
-        w_woven = [at("w_woven%d" % i, [P, H, 4], BF16, 30720 + 2048 * i) for i in range(4)]
-
-        def quantize_w(i):
-            a, h = divmod(i, 2)
-            quantize(w_woven[i][:], w_codes[a][:, h * H : (h + 1) * H], w_plane[a][:, h * H : (h + 1) * H])
-
-        weave(w_woven[0][:, 0:P, :], w_head)
-        weave(w_woven[0][:, P:H, :], w_raw[0])
-        for i in range(1, 3):
-            weave(w_woven[i][:], w_raw[i])
-        weave(w_woven[3][:, 0:P, :], w_raw[3][:, :, 0:P])
+        iw_cols = sb("iw_cols", [P, 16], F32, AT_RAW_A1 + 1024)
         nc.scalar.activation(iw_cols[:], iw_ps[:, 0:16], COPY)
-        pairs = [sb("pairs0", [P, H], U32), sb("pairs1", [P, H], U32), at("pairs2", [P, H], U32, 33792)]
-        parted = [sb("parted0", [P, 2, 2 * H], U8), at("parted1", [P, 2, 2 * H], U8, 32768), at("parted2", [P, 2, 2 * H], U8, 34816)]
-        quantize_w(0)
-        pick_words(pairs[0][:], 0, 0)
-        pick_words(pairs[1][:], 1, 0)
-        part_words(parted[0], pairs[0][:])
-        quantize_w(1)
-        part_words(parted[1], pairs[1][:])
-        pick_words(pairs[2][:], 2, 0)
-        quantize_w(2)
-        nc.vector.tensor_copy(*by_lines(w_woven[3][:, P:H, :], w_raw[3][:, :, P:H]))
-        part_words(parted[2], pairs[2][:])
-        quantize_w(3)
-        wx_raw.append(load_rows(at("wx_raw2", [P, 4, P], F32, 57344)[:], wx, H + P, N))
-        x_raw = load_rows(at("x_raw", [P, 4, J], F32, 48128)[:], x, 0, J)
-        pairs_late = at("pairs_late", [P, G * H], U32, 37888)
-        for g in range(G):
-            pick_words(pairs_late[:, g * H : (g + 1) * H], g, 1)
-        parted_late = [sb("parted_late0", [P, 2, 4 * H], U8), sb("parted_late1", [P, 2, 2 * H], U8)]
-        part_words(parted_late[0], pairs_late[:, 0 : 2 * H])
-        part_words(parted_late[1], pairs_late[:, 2 * H : 3 * H])
-        res_sb = at("res_sb", [P, 4, J], F32, 4096)
+
+        nc.gpsimd.tensor_copy(woven[0, 1][:], raw_b0[:].rearrange("p t c -> p c t"))
+
+        def iw_col(g, jt):
+            return iw_cols[:, 4 * g + jt : 4 * g + jt + 1]
+
+        def look_up(sums, g, jt, n0, n1, passes=(0, 1)):
+            h, u = divmod(jt, 2)
+            s0 = g * H + u * P
+            c0 = g % 2 * H + u * P
+            for a in passes:
+                nc.tensor.matmul_mx(
+                    out=sums,
+                    lhsT=words[h][g // 2][:, a, 2 * c0 : 2 * (c0 + P)].bitcast(FP4X4),
+                    lhsT_scale=(picked, moved)[a][h][:, s0 : s0 + P],
+                    rhs=w_codes[a][:, n0:n1].bitcast(FP8X4),
+                    rhs_scale=w_plane[a][:, n0:n1],
+                    start=(a == 0),
+                    stop=(a == 1),
+                )
+
+        def turn(turned, term, c0, first, last):
+            blocks = term.shape[1] // P
+            for c in range(blocks):
+                nc.tensor.matmul(
+                    turned[:, c0 + c, :], term[:, c * P : (c + 1) * P], ident[:],
+                    start=(first and c == 0), stop=(last and c == blocks - 1), is_transpose=True,
+                )
+
+        turned = [bank_tile("turned%d" % u, [P, 4, P], 6 + u) for u in range(2)]
+
+        def early_terms(s, sums, lists, offset=None):
+            held = sb("terms%d_%d" % (s, lists[0]), [P, 2 * len(lists) * H], F32, offset)
+            for i, g in enumerate(lists):
+                terms = [held[:, (2 * i + u) * H : (2 * i + u + 1) * H] for u in range(2)]
+                for u in range(2):
+                    nc.scalar.activation(terms[u], sums[g, u], COPY, scale=iw_col(g, u))
+                for u in range(2):
+                    turn(turned[u], terms[u], 2 * s, s == 0 and g == 1, s == 1 and g == 2)
+
+        shared = [bank_tile("first_shared%d" % u, [P, 2, H], u) for u in range(2)]
+        sums_a = {(g, u): shared[u][:, g // 2, :] for g in (0, 2) for u in range(2)}
+        for u in range(2):
+            sums_a[1, u] = bank_tile("first_alone%d" % u, [P, H], 2 + u)[:]
+        for a in range(2):
+            for g in (1, 0):
+                for u in range(2):
+                    look_up(sums_a[g, u], g, u, 0, H, (a,))
+        for u in range(2):
+            look_up(sums_a[2, u], 2, u, 0, H)
+        early_terms(0, sums_a, (1,))
+        weave(woven[1, 1][:], raw_b1[:])
+        early_terms(0, sums_a, (0, 2), AT_TERMS_A)
+        quantize_w(0, 1)
+        quantize_w(1, 1)
+        pairs = pick_words(1, (0, 1, 2), AT_RAW_B1)
+        words.append([part_words("parted1_0", pairs[:, 0 : 2 * H]), part_words("parted1_1", pairs[:, 2 * H : 3 * H])])
+        res_sb = sb("res_sb", [P, 4, J], F32, AT_TABLE)
         nc.sync.dma_start(res_sb[:], res.rearrange("(c p) j -> p c j", p=P))
 
-        iw_col = lambda g, jt: iw_cols[:, 4 * g + jt : 4 * g + jt + 1]
+        tops = [sb("top0", [P, H, 4], BF16, AT_WOVEN_B1), sb("top1", [P, H, 4], BF16)]
+        for u in range(2):
+            upper = wx_raw[0][:, :, u * P : (u + 1) * P].bitcast(BF16).rearrange("p t (c e) -> p c t e", e=2)[:, :, :, 1]
+            nc.gpsimd.tensor_copy(tops[0][:, u * P : (u + 1) * P, :], upper)
+        sums_b = {}
+        for g, b in enumerate((4, 5, 2)):
+            bank = bank_tile("second%d" % g, [P, 2, H], b)
+            for u in range(2):
+                sums_b[g, u] = bank[:, u, :]
+                look_up(sums_b[g, u], g, u, H, N)
+        nc.scalar.copy(
+            tops[1][:].rearrange("p (c i) t -> p c t i", i=4),
+            wx_raw[1][:].bitcast(BF16).rearrange("p t (c i e) -> p c t i e", i=4, e=2)[:, :, :, :, 1],
+        )
+        early_terms(1, sums_b, (0, 1, 2))
 
-        def look_up(g, jt, b):
-            h, u = divmod(jt, 2)
-            bank = bank_tile("a%d_%d" % (g, jt), [P, N], b)
-            s0 = g * J + jt * P
-            passes = (0, 1) if g < 2 and h == 0 else (1, 0)
-            for a in passes:
-                if h == 0:
-                    words = parted[g][:, a, 2 * u * P : 2 * (u + 1) * P]
-                else:
-                    words = parted_late[g // 2][:, a, 2 * (g % 2 * H + u * P) : 2 * (g % 2 * H + (u + 1) * P)]
-                nc.tensor.matmul_mx(
-                    out=bank[:],
-                    lhsT=words.bitcast(FP4X4),
-                    lhsT_scale=tab_planes[a][:, s0 : s0 + P],
-                    rhs=w_codes[a][:].bitcast(FP8X4),
-                    rhs_scale=w_plane[a][:],
-                    start=(a == passes[0]),
-                    stop=(a == passes[1]),
-                )
+        splits = [sb("split%d" % cp, [P, 2 * H, 4], BF16) for cp in range(2)]
+        for cp in range(2):
+            nc.vector.tensor_scalar(
+                splits[cp][:, 0:H, :].rearrange("p c t -> p (c t)").bitcast(I32),
+                tops[cp][:].rearrange("p c t -> p (c t)").bitcast(I32),
+                HI_MASK, None, ALU.bitwise_and,
+            )
+        for cp in range(2):
+            low, raw_lines = by_lines(splits[cp][:, H : 2 * H, :], wx_raw[cp][:])
+            nc.vector.tensor_tensor(low, raw_lines, splits[cp][:, 0:H, :].rearrange("p (c i) t -> p c t i", i=4), ALU.subtract)
+
+        def late_sums(g, jt, b):
+            bank = bank_tile("late%d_%d" % (g, jt), [P, N], b)
+            look_up(bank[:], g, jt, 0, N)
             return bank
 
-        def scaled(g, jt, b, offset=None):
-            bank = look_up(g, jt, b)
-            name = "term%d_%d" % (g, jt)
-            term = sb(name, [P, N], F32) if offset is None else at(name, [P, N], F32, offset)
+        def scaled(g, jt, b):
+            bank = late_sums(g, jt, b)
+            term = sb("late_term%d_%d" % (g, jt), [P, N], F32)
             nc.scalar.activation(term[:], bank[:], COPY, scale=iw_col(g, jt))
             return term
 
-        def added(g, jt, b, earlier):
-            bank = look_up(g, jt, b)
-            term = sb("term%d_%d" % (g, jt), [P, N], F32)
-            nc.vector.scalar_tensor_tensor(term[:], bank[:], iw_col(g, jt), earlier[:], ALU.mult, ALU.add)
-            return term
-
-        def turn(turned, term, first, last):
-            for c in range(4):
-                nc.tensor.matmul(
-                    turned[:, c, :], term[:, c * P : (c + 1) * P], ident[:],
-                    start=(first and c == 0), stop=(last and c == 3), is_transpose=True,
-                )
-
-        def mask_half(h, top):
-            split = sb("split%d" % h, [P, 2 * H, 4], BF16)
-            nc.vector.tensor_scalar(
-                split[:, 0:H, :].rearrange("p c t -> p (c t)").bitcast(I32),
-                top[:].rearrange("p c t -> p (c t)").bitcast(I32),
-                HI_MASK, None, ALU.bitwise_and,
-            )
-            return split
-
-        def rest(split, c0, c1, raw_cols):
-            low, raw_lines = by_lines(split[:, H + c0 : H + c1, :], raw_cols)
-            nc.vector.tensor_tensor(low, raw_lines, split[:, c0:c1, :].rearrange("p (c i) t -> p c t i", i=4), ALU.subtract)
-
-        part_codes = [sb("part_codes%d" % h, [P, 2 * H], U32) for h in range(2)]
-        part_plane = [sb("part_plane%d" % h, [P, 2 * H], U8) for h in range(2)]
+        part_codes = [sb("part_codes%d" % cp, [P, 2 * H], U32) for cp in range(2)]
+        part_plane = [sb("part_plane%d" % cp, [P, 2 * H], U8) for cp in range(2)]
         x_codes = [sb("x_codes%d" % h, [P, H], U32) for h in range(2)]
         x_plane = [sb("x_plane%d" % h, [P, H], U8) for h in range(2)]
-        x_woven = [at("x_woven%d" % h, [P, H, 4], BF16, 33792 - 2048 * h) for h in range(2)]
+        x_woven = [sb("x_woven%d" % h, [P, H, 4], BF16, AT_X_WOVEN + 2048 * h) for h in range(2)]
         own = sb("own", [P, 4, H], F32)
-        early = at("early", [P, 4, H], F32, 44544)
-        early_res = [sb("early_res%d" % cp, [P, 2, H], F32) for cp in range(2)]
+        early = sb("early", [P, 4, H], F32)
+        early_res = sb("early_res", [P, 4, H], F32, AT_X_WOVEN)
         out_rows = out.rearrange("(c p) j -> p c j", p=P)
 
         def skip(h, cp, b):
@@ -221,60 +264,42 @@ def tile_list_interp_hl_res_kernel(tc, tab_words, tab_scales, w, x, wx, iw0, iw1
                     )
             return bank
 
-        def finish_early(cp, bank, e0, e1, done):
-            nc.vector.tensor_tensor(done[:], bank[:, e0:e1, :], early_res[cp][:, e0:e1, :], ALU.add)
+        def finish_early(cp, bank, e0, e1):
+            done = sb("done_early%d_%d" % (cp, e0), [P, e1 - e0, H], F32)
+            nc.vector.tensor_tensor(done[:], bank[:, e0:e1, :], early_res[:, 2 * cp + e0 : 2 * cp + e1, :], ALU.add)
             nc.sync.dma_start(out_rows[:, 2 * cp + e0 : 2 * cp + e1, 0:H], done[:])
 
-        def finish_late(u, turned):
+        def finish_late(u, sums):
             done = sb("done_late%d" % u, [P, 4, P], F32)
-            nc.vector.tensor_tensor(done[:], turned[:], own[:, :, u * P : (u + 1) * P], ALU.add)
+            nc.vector.tensor_tensor(done[:], sums[:], own[:, :, u * P : (u + 1) * P], ALU.add)
             nc.sync.dma_start(out_rows[:, :, H + u * P : H + (u + 1) * P], done[:])
 
-        tops = [sb("top0", [P, H, 4], BF16), at("top1", [P, H, 4], BF16, 35840)]
-        nc.scalar.copy(
-            tops[0][:].rearrange("p (c i) t -> p c t i", i=4),
-            wx_raw[0].bitcast(BF16).rearrange("p t (c i e) -> p c t i e", i=4, e=2)[:, :, :, :, 1],
-        )
+        weave(x_woven[1][:], x_raw[:, :, H:J])
+        late = [[scaled(g, 2, b) for g, b in enumerate((3, 0, 1))]]
+        weave(x_woven[0][:], x_raw[:, :, 0:H])
         for u in range(2):
-            upper = wx_raw[1 + u].bitcast(BF16).rearrange("p t (c e) -> p c t e", e=2)[:, :, :, 1]
-            nc.gpsimd.tensor_copy(tops[1][:, u * P : (u + 1) * P, :], upper)
-        first = [scaled(0, u, u) for u in range(2)]
-        second = [scaled(1, u, 2 + u) for u in range(2)]
-        third = [scaled(2, u, 6 + u) for u in range(2)]
-        splits = [mask_half(h, tops[h]) for h in range(2)]
-        rest(splits[0], 0, H, wx_raw[0])
-        for u in range(2):
-            rest(splits[1], u * P, (u + 1) * P, wx_raw[1 + u])
-        turned = [bank_tile("turned%d" % u, [P, 4, P], 4 + u) for u in range(2)]
-        for h in (1, 0):
-            weave(x_woven[h][:], x_raw[:, :, h * H : (h + 1) * H])
-        late = [[scaled(0, 2, 2, 48640), scaled(1, 2, 3, 50688)]]
-        for i, terms in enumerate((first, second, third)):
-            for u in range(2):
-                turn(turned[u], terms[u], i == 0, i == 2)
-        for u in range(2):
-            cols = slice(u * P, (u + 1) * P)
-            nc.scalar.activation(early[:, :, cols], turned[u][:], COPY)
-        for cp in range(2):
-            rows = slice(2 * cp, 2 * cp + 2)
-            nc.gpsimd.tensor_tensor(early_res[cp][:], early[:, rows, :], res_sb[:, rows, 0:H], ALU.add)
-        late.append([scaled(0, 3, 0, 54784), scaled(1, 3, 1, 52736)])
+            nc.scalar.activation(early[:, :, u * P : (u + 1) * P], turned[u][:], COPY)
+        late.append([scaled(g, 3, b) for g, b in enumerate((4, 5, 2))])
         quantize(splits[0][:], part_codes[0][:], part_plane[0][:])
         quantize(x_woven[1][:], x_codes[1][:], x_plane[1][:])
         quantize(splits[1][:], part_codes[1][:], part_plane[1][:])
         quantize(x_woven[0][:], x_codes[0][:], x_plane[0][:])
-        late[0][0] = added(2, 2, 6, late[0][0])
         for cp in range(2):
-            bank = skip(1, cp, 2 + cp)
+            rows = slice(2 * cp, 2 * cp + 2)
+            nc.gpsimd.tensor_tensor(early_res[:, rows, :], early[:, rows, :], res_sb[:, rows, 0:H], ALU.add)
+
+        def turn_late(u, b):
+            turned.append(bank_tile("turned%d" % (2 + u), [P, 4, P], b))
+            for g in range(G):
+                turn(turned[2 + u], late[u][g][:], 0, g == 0, g == G - 1)
+
+        turn_late(0, 1)
+        for cp in range(2):
+            bank = skip(1, cp, (3, 0)[cp])
             nc.vector.tensor_tensor(own[:, 2 * cp : 2 * cp + 2, :], bank[:], res_sb[:, 2 * cp : 2 * cp + 2, H:J], ALU.add)
-        late[1][0] = added(2, 3, 7, late[1][0])
-        ax_early = [skip(0, cp, 2 + cp) for cp in range(2)]
-        for u in range(2):
-            turned.append(bank_tile("turned%d" % (2 + u), [P, 4, P], 6 - 2 * u))
-            turn(turned[2 + u], late[u][1], True, False)
-            turn(turned[2 + u], late[u][0], False, True)
+        ax_early = [skip(0, cp, (7, 3)[cp]) for cp in range(2)]
+        turn_late(1, 6)
         finish_late(0, turned[2])
-        finish_early(0, ax_early[0], 0, 2, at("done_early0", [P, 2, H], F32, 54784))
+        finish_early(0, ax_early[0], 0, 2)
+        finish_early(1, ax_early[1], 0, 2)
         finish_late(1, turned[3])
-        for e in range(2):
-            finish_early(1, ax_early[1], e, e + 1, sb("done_early1_%d" % e, [P, 1, H], F32))

@@ -20,7 +20,6 @@ COPY = mybir.ActivationFunctionType.Copy
 
 P = 128
 H = 256
-TIP = 32
 HI_MASK = -983056
 
 AT_TABLE = 0
@@ -67,12 +66,11 @@ def tile_list_interp_hl_res_kernel(tc, tab_words, tab_scales, w, x, wx, iw0, iw1
 
         offsets = keep.tile([P, G * J // 16], U16, name="offsets")
         nc.sync.dma_start(offsets[:], offs)
-        w_tip = load_cols("w_tip", w[0:512, :], 0, TIP)
 
         scale_tab = sb("scale_tab", [P, T], U8)
-        nc.vector.memset(scale_tab[:].bitcast(I32), 0)
-        for q in range(4):
-            nc.sync.dma_start(scale_tab[32 * q : 32 * q + 8, :].bitcast(I32), tab_scales[:, 4 * q : 4 * q + 4, :].bitcast(I32))
+        nc.sync.dma_start(scale_tab[0:32, :].bitcast(I32), tab_scales.rearrange("a q t -> q a t").bitcast(I32))
+        for p0, p1 in ((32, 64), (64, 128)):
+            nc.vector.memset(scale_tab[p0:p1, :].bitcast(I32), 0)
         word_tab = sb("word_tab", [P, T], I32, AT_TABLE)
         nc.sync.dma_start(word_tab[:], tab_words[0].rearrange("p t b -> p (t b)").bitcast(I32))
 
@@ -82,11 +80,11 @@ def tile_list_interp_hl_res_kernel(tc, tab_words, tab_scales, w, x, wx, iw0, iw1
             nc.gpsimd.dma_start(iw_rows[4 * g : 4 * g + 4, :], iw.rearrange("(c j) -> c j", c=4))
         ident = sb("ident", [P, P], F32)
         make_identity(nc, ident[:])
-        moved = [sb("moved%d" % h, [P, G * H], U8) for h in range(2)]
-        for h in range(2):
-            nc.vector.memset(moved[h][:].bitcast(I32), 0)
+        moved = [sb("moved%d" % h, [P, 2 * G * H], U8) for h in range(2)]
+        nc.vector.memset(moved[0][:].bitcast(I32), 0)
+        nc.gpsimd.memset(moved[1][:].bitcast(I32), 0)
 
-        raw_a0 = load_cols("raw_a0", w[0:512, :], TIP, H, AT_RAW_A0)
+        raw_a0 = load_cols("raw_a0", w[0:512, :], 0, H, AT_RAW_A0)
         raw_a1 = load_cols("raw_a1", w[512:1024, :], 0, H, AT_RAW_A1)
 
         def pick_scales(h, offset=None):
@@ -97,7 +95,7 @@ def tile_list_interp_hl_res_kernel(tc, tab_words, tab_scales, w, x, wx, iw0, iw1
 
         def move_scales(h):
             for q in range(4):
-                nc.sync.dma_start(moved[h][32 * q : 32 * q + 4, :].bitcast(I32), picked[h][32 * q + 4 : 32 * q + 8, :].bitcast(I32))
+                nc.sync.dma_start(moved[h][32 * q : 32 * q + 4, :].bitcast(I32), picked[h][8 * q : 8 * q + 8, :].bitcast(I32))
 
         def pick_words(h, lists, offset=None):
             pairs = sb("pairs%d_%d" % (h, lists[0]), [P, len(lists) * H], U32, offset)
@@ -115,7 +113,6 @@ def tile_list_interp_hl_res_kernel(tc, tab_words, tab_scales, w, x, wx, iw0, iw1
         raw_b0 = load_cols("raw_b0", w[0:512, :], H, N)
         raw_b1 = load_cols("raw_b1", w[512:1024, :], H, N, AT_RAW_B1)
         wx_raw = [load_cols("wx_raw%d" % cp, wx, cp * H, (cp + 1) * H) for cp in range(2)]
-        x_raw = load_cols("x_raw", x, 0, J)
 
         w_codes = [sb("w_codes%d" % a, [P, N], U32) for a in range(2)]
         w_plane = [sb("w_plane%d" % a, [P, N], U8) for a in range(2)]
@@ -126,14 +123,14 @@ def tile_list_interp_hl_res_kernel(tc, tab_words, tab_scales, w, x, wx, iw0, iw1
             quantize(woven[a, s][:], w_codes[a][:, s * H : (s + 1) * H], w_plane[a][:, s * H : (s + 1) * H])
 
         words = [[part_words("parted0_0", pick_words(0, (0, 1))[:])]]
-        weave(woven[0, 0][:, 0:TIP, :], w_tip[:])
-        weave(woven[0, 0][:, TIP:H, :], raw_a0[:])
+        weave(woven[0, 0][:], raw_a0[:])
         weave(woven[1, 0][:], raw_a1[:])
         quantize_w(0, 0)
         pairs = pick_words(0, (2,), AT_RAW_A0)
         quantize_w(1, 0)
         words[0].append(part_words("parted0_1", pairs[:]))
         picked.append(pick_scales(1, AT_RAW_A1))
+        x_raw = load_cols("x_raw", x, 0, J)
         move_scales(1)
 
         iw_ps = bank_tile("iw_ps", [P, P], 7)
@@ -154,7 +151,7 @@ def tile_list_interp_hl_res_kernel(tc, tab_words, tab_scales, w, x, wx, iw0, iw1
                 nc.tensor.matmul_mx(
                     out=sums,
                     lhsT=words[h][g // 2][:, a, 2 * c0 : 2 * (c0 + P)].bitcast(FP4X4),
-                    lhsT_scale=(picked, moved)[a][h][:, s0 : s0 + P],
+                    lhsT_scale=moved[h][:, a * G * H + s0 : a * G * H + s0 + P],
                     rhs=w_codes[a][:, n0:n1].bitcast(FP8X4),
                     rhs_scale=w_plane[a][:, n0:n1],
                     start=(a == 0),
@@ -238,6 +235,12 @@ def tile_list_interp_hl_res_kernel(tc, tab_words, tab_scales, w, x, wx, iw0, iw1
             nc.scalar.activation(term[:], bank[:], COPY, scale=iw_col(g, jt))
             return term
 
+        def added(g, jt, b, earlier):
+            bank = late_sums(g, jt, b)
+            term = sb("late_term%d_%d" % (g, jt), [P, N], F32)
+            nc.vector.scalar_tensor_tensor(term[:], bank[:], iw_col(g, jt), earlier[:], ALU.mult, ALU.add)
+            return term
+
         part_codes = [sb("part_codes%d" % cp, [P, 2 * H], U32) for cp in range(2)]
         part_plane = [sb("part_plane%d" % cp, [P, 2 * H], U8) for cp in range(2)]
         x_codes = [sb("x_codes%d" % h, [P, H], U32) for h in range(2)]
@@ -275,11 +278,11 @@ def tile_list_interp_hl_res_kernel(tc, tab_words, tab_scales, w, x, wx, iw0, iw1
             nc.sync.dma_start(out_rows[:, :, H + u * P : H + (u + 1) * P], done[:])
 
         weave(x_woven[1][:], x_raw[:, :, H:J])
-        late = [[scaled(g, 2, b) for g, b in enumerate((3, 0, 1))]]
+        late = [[scaled(g, 2, b) for g, b in enumerate((3, 0))]]
         weave(x_woven[0][:], x_raw[:, :, 0:H])
         for u in range(2):
             nc.scalar.activation(early[:, :, u * P : (u + 1) * P], turned[u][:], COPY)
-        late.append([scaled(g, 3, b) for g, b in enumerate((4, 5, 2))])
+        late.append([scaled(g, 3, b) for g, b in enumerate((4, 5))])
         quantize(splits[0][:], part_codes[0][:], part_plane[0][:])
         quantize(x_woven[1][:], x_codes[1][:], x_plane[1][:])
         quantize(splits[1][:], part_codes[1][:], part_plane[1][:])
@@ -290,16 +293,15 @@ def tile_list_interp_hl_res_kernel(tc, tab_words, tab_scales, w, x, wx, iw0, iw1
 
         def turn_late(u, b):
             turned.append(bank_tile("turned%d" % (2 + u), [P, 4, P], b))
-            for g in range(G):
-                turn(turned[2 + u], late[u][g][:], 0, g == 0, g == G - 1)
+            turn(turned[2 + u], late[u][1][:], 0, True, False)
+            turn(turned[2 + u], late[u][0][:], 0, False, True)
 
-        turn_late(0, 1)
         for cp in range(2):
-            bank = skip(1, cp, (3, 0)[cp])
+            bank = skip(1, cp, 6 + cp)
             nc.vector.tensor_tensor(own[:, 2 * cp : 2 * cp + 2, :], bank[:], res_sb[:, 2 * cp : 2 * cp + 2, H:J], ALU.add)
-        ax_early = [skip(0, cp, (7, 3)[cp]) for cp in range(2)]
-        turn_late(1, 6)
-        finish_late(0, turned[2])
-        finish_early(0, ax_early[0], 0, 2)
-        finish_early(1, ax_early[1], 0, 2)
-        finish_late(1, turned[3])
+            late[cp][0] = added(2, 2 + cp, 1 + cp, late[cp][0])
+        for u in range(2):
+            ax_early = skip(0, u, 1 + u)
+            turn_late(u, 3 + u)
+            finish_early(u, ax_early, 0, 2)
+            finish_late(u, turned[2 + u])

@@ -192,8 +192,8 @@ def tile_list_interp_hl_res_kernel(tc, tab_words, tab_scales, w, x, wx, iw0, iw1
         early_terms(0, sums_a, (0, 2), AT_TERMS_A)
         quantize_w(0, 1)
         quantize_w(1, 1)
-        pairs = pick_words(1, (0, 1, 2), AT_RAW_B1)
-        words.append([part_words("parted1_0", pairs[:, 0 : 2 * H]), part_words("parted1_1", pairs[:, 2 * H : 3 * H])])
+        pairs = [pick_words(1, (0, 1), AT_RAW_B1), pick_words(1, (2,), AT_RAW_B1 + 2048)]
+        words.append([part_words("parted1_%d" % i, pairs[i][:]) for i in range(2)])
         res_sb = sb("res_sb", [P, 4, J], F32, AT_TABLE)
         nc.sync.dma_start(res_sb[:], res.rearrange("(c p) j -> p c j", p=P))
 
@@ -229,14 +229,16 @@ def tile_list_interp_hl_res_kernel(tc, tab_words, tab_scales, w, x, wx, iw0, iw1
             look_up(bank[:], g, jt, 0, N)
             return bank
 
-        def scaled(g, jt, b):
-            bank = late_sums(g, jt, b)
+        late_banks = {(g, jt): late_sums(g, jt, b) for (g, jt), b in zip(((0, 2), (1, 2), (0, 3), (1, 3)), (3, 0, 4, 5))}
+
+        def scaled(g, jt):
+            bank = late_banks[g, jt]
             term = sb("late_term%d_%d" % (g, jt), [P, N], F32)
             nc.scalar.activation(term[:], bank[:], COPY, scale=iw_col(g, jt))
             return term
 
-        def added(g, jt, b, earlier):
-            bank = late_sums(g, jt, b)
+        def added(g, jt, earlier):
+            bank = late_banks[g, jt]
             term = sb("late_term%d_%d" % (g, jt), [P, N], F32)
             nc.vector.scalar_tensor_tensor(term[:], bank[:], iw_col(g, jt), earlier[:], ALU.mult, ALU.add)
             return term
@@ -277,12 +279,12 @@ def tile_list_interp_hl_res_kernel(tc, tab_words, tab_scales, w, x, wx, iw0, iw1
             nc.vector.tensor_tensor(done[:], sums[:], own[:, :, u * P : (u + 1) * P], ALU.add)
             nc.sync.dma_start(out_rows[:, :, H + u * P : H + (u + 1) * P], done[:])
 
-        weave(x_woven[1][:], x_raw[:, :, H:J])
-        late = [[scaled(g, 2, b) for g, b in enumerate((3, 0))]]
-        weave(x_woven[0][:], x_raw[:, :, 0:H])
+        for h in (1, 0):
+            weave(x_woven[h][:], x_raw[:, :, h * H : (h + 1) * H])
         for u in range(2):
             nc.scalar.activation(early[:, :, u * P : (u + 1) * P], turned[u][:], COPY)
-        late.append([scaled(g, 3, b) for g, b in enumerate((4, 5))])
+        third = scaled(0, 2)
+        fourth = [scaled(g, 3) for g in range(2)]
         quantize(splits[0][:], part_codes[0][:], part_plane[0][:])
         quantize(x_woven[1][:], x_codes[1][:], x_plane[1][:])
         quantize(splits[1][:], part_codes[1][:], part_plane[1][:])
@@ -291,17 +293,24 @@ def tile_list_interp_hl_res_kernel(tc, tab_words, tab_scales, w, x, wx, iw0, iw1
             rows = slice(2 * cp, 2 * cp + 2)
             nc.gpsimd.tensor_tensor(early_res[:, rows, :], early[:, rows, :], res_sb[:, rows, 0:H], ALU.add)
 
-        def turn_late(u, b):
+        def turn_late(u, b, terms):
             turned.append(bank_tile("turned%d" % (2 + u), [P, 4, P], b))
-            turn(turned[2 + u], late[u][1][:], 0, True, False)
-            turn(turned[2 + u], late[u][0][:], 0, False, True)
+            for i, term in enumerate(terms):
+                turn(turned[2 + u], term[:], 0, i == 0, i == len(terms) - 1)
 
+        third = added(1, 2, third)
         for cp in range(2):
             bank = skip(1, cp, 6 + cp)
+            late_banks[2, 2 + cp] = late_sums(2, 2 + cp, 1 + cp)
             nc.vector.tensor_tensor(own[:, 2 * cp : 2 * cp + 2, :], bank[:], res_sb[:, 2 * cp : 2 * cp + 2, H:J], ALU.add)
-            late[cp][0] = added(2, 2 + cp, 1 + cp, late[cp][0])
-        for u in range(2):
-            ax_early = skip(0, u, 1 + u)
-            turn_late(u, 3 + u)
-            finish_early(u, ax_early, 0, 2)
-            finish_late(u, turned[2 + u])
+            if cp == 0:
+                third = added(2, 2, third)
+        fourth[0] = added(2, 3, fourth[0])
+        ax_early = skip(0, 0, 3)
+        turn_late(0, 0, [third])
+        finish_early(0, ax_early, 0, 2)
+        finish_late(0, turned[2])
+        ax_early = skip(0, 1, 4)
+        turn_late(1, 1, fourth[::-1])
+        finish_early(1, ax_early, 0, 2)
+        finish_late(1, turned[3])

@@ -22,13 +22,16 @@ P = 128
 H = 256
 HI_MASK = -983056
 
-AT_TABLE = 0
-AT_RAW_A1 = 8192
-AT_RAW_B1 = 12288
-AT_TERMS_A = AT_RAW_B1 + 3072
-AT_WOVEN_B1 = 22528
-AT_RAW_A0 = 24576
-AT_X_WOVEN = 28672
+SHARE = 160
+
+AT_WOVEN_A0 = 0
+AT_WOVEN_B0 = 2048
+AT_RAW_A1 = 4096
+AT_RAW_B0 = 8192
+AT_WOVEN_A1 = 14336
+AT_X_RAW = 21504
+AT_X_WOVEN1 = 29696
+AT_X_WOVEN0 = 32768
 
 
 def tile_list_interp_hl_res_kernel(tc, tab_words, tab_scales, w, x, wx, iw0, iw1, iw2, res, offs, out):
@@ -60,9 +63,9 @@ def tile_list_interp_hl_res_kernel(tc, tab_words, tab_scales, w, x, wx, iw0, iw1
         def quantize(woven, codes, plane):
             nc.vector.quantize_mx(out=codes.bitcast(FP8X4), scales=plane, in_=woven.rearrange("p c t -> p (c t)"))
 
-        def listed(g, h):
-            c0 = (g * J + h * H) // 16
-            return offsets[:, c0 : c0 + H // 16]
+        def listed(g, j0, count):
+            c0 = (g * J + j0) // 16
+            return offsets[:, c0 : c0 + count // 16]
 
         offsets = keep.tile([P, G * J // 16], U16, name="offsets")
         nc.sync.dma_start(offsets[:], offs)
@@ -71,186 +74,191 @@ def tile_list_interp_hl_res_kernel(tc, tab_words, tab_scales, w, x, wx, iw0, iw1
         nc.sync.dma_start(scale_tab[0:32, :].bitcast(I32), tab_scales.rearrange("a q t -> q a t").bitcast(I32))
         for p0, p1 in ((32, 64), (64, 128)):
             nc.vector.memset(scale_tab[p0:p1, :].bitcast(I32), 0)
-        word_tab = sb("word_tab", [P, T], I32, AT_TABLE)
+        word_tab = sb("word_tab", [P, T], I32)
         nc.sync.dma_start(word_tab[:], tab_words[0].rearrange("p t b -> p (t b)").bitcast(I32))
 
         iw_rows = sb("iw_rows", [P, P], F32)
         nc.gpsimd.memset(iw_rows[:], 0.0)
         for g, iw in enumerate((iw0, iw1, iw2)):
-            nc.gpsimd.dma_start(iw_rows[4 * g : 4 * g + 4, :], iw.rearrange("(c j) -> c j", c=4))
+            nc.scalar.dma_start(iw_rows[4 * g : 4 * g + 4, :], iw.rearrange("(c j) -> c j", c=4))
         ident = sb("ident", [P, P], F32)
         make_identity(nc, ident[:])
         moved = [sb("moved%d" % h, [P, 2 * G * H], U8) for h in range(2)]
         nc.vector.memset(moved[0][:].bitcast(I32), 0)
         nc.gpsimd.memset(moved[1][:].bitcast(I32), 0)
 
-        raw_a0 = load_cols("raw_a0", w[0:512, :], 0, H, AT_RAW_A0)
+        raw_a0 = load_cols("raw_a0", w[0:512, :], 0, H)
         raw_a1 = load_cols("raw_a1", w[512:1024, :], 0, H, AT_RAW_A1)
 
         def pick_scales(h, offset=None):
             picked = sb("picked%d" % h, [P, G * H], U8, offset)
             for g in range(G):
-                nc.vector.tensor_copy(picked[:, g * H : (g + 1) * H], scale_tab[:].indirect(listed(g, h)))
+                nc.vector.tensor_copy(picked[:, g * H : (g + 1) * H], scale_tab[:].indirect(listed(g, h * H, H)))
             return picked
 
         def move_scales(h):
             for q in range(4):
                 nc.sync.dma_start(moved[h][32 * q : 32 * q + 4, :].bitcast(I32), picked[h][8 * q : 8 * q + 8, :].bitcast(I32))
 
-        def pick_words(h, lists, offset=None):
-            pairs = sb("pairs%d_%d" % (h, lists[0]), [P, len(lists) * H], U32, offset)
+        def pick_words(j0, count, lists, offset=None):
+            pairs = sb("pairs%d_%d" % (j0, lists[0]), [P, len(lists) * count], U32, offset)
             for i, g in enumerate(lists):
-                nc.vector.tensor_copy(pairs[:, i * H : (i + 1) * H], word_tab[:].bitcast(U32).indirect(listed(g, h)))
+                nc.vector.tensor_copy(pairs[:, i * count : (i + 1) * count], word_tab[:].bitcast(U32).indirect(listed(g, j0, count)))
             return pairs
 
-        def part_words(name, pairs):
-            parted = sb(name, [P, 2, 2 * pairs.shape[1]], U8)
-            nc.vector.tensor_copy(parted[:].bitcast(U16), pairs.bitcast(U16).rearrange("p (j d) -> p d j", d=2))
-            return parted
+        words = {}
+
+        def part_words(j0, count, lists, pairs, offset=None):
+            parted = sb("parted%d_%d" % (j0, lists[0]), [P, 2, 2 * len(lists) * count], U8, offset)
+            nc.vector.tensor_copy(parted[:].bitcast(U16), pairs[:].bitcast(U16).rearrange("p (j d) -> p d j", d=2))
+            for i, g in enumerate(lists):
+                for c in range(0, count, P):
+                    words[g, (j0 + c) // P] = parted[:, :, 2 * (i * count + c) : 2 * (i * count + c + P)]
 
         picked = [pick_scales(0)]
         move_scales(0)
-        raw_b0 = load_cols("raw_b0", w[0:512, :], H, N)
-        raw_b1 = load_cols("raw_b1", w[512:1024, :], H, N, AT_RAW_B1)
+        raw_b0 = load_cols("raw_b0", w[0:512, :], H, N, AT_RAW_B0)
+        raw_b1 = load_cols("raw_b1", w[512:1024, :], H, N)
         wx_raw = [load_cols("wx_raw%d" % cp, wx, cp * H, (cp + 1) * H) for cp in range(2)]
 
         w_codes = [sb("w_codes%d" % a, [P, N], U32) for a in range(2)]
         w_plane = [sb("w_plane%d" % a, [P, N], U8) for a in range(2)]
-        woven_at = {(0, 1): AT_RAW_A0, (1, 1): AT_WOVEN_B1}
-        woven = {(a, s): sb("woven%d_%d" % (a, s), [P, H, 4], BF16, woven_at.get((a, s))) for a in range(2) for s in range(2)}
+        woven_a0 = sb("woven_a0", [P, H, 4], BF16, AT_WOVEN_A0)
+        woven_a1 = sb("woven_a1", [P, H, 4], BF16, AT_WOVEN_A1)
+        woven_b0 = sb("woven_b0", [P, H, 4], BF16, AT_WOVEN_B0)
+        woven_b1 = sb("woven_b1", [P, H, 4], BF16, AT_WOVEN_A1 + 1024)
 
-        def quantize_w(a, s):
-            quantize(woven[a, s][:], w_codes[a][:, s * H : (s + 1) * H], w_plane[a][:, s * H : (s + 1) * H])
+        def quantize_w(woven, a, n0):
+            n1 = n0 + woven.shape[1]
+            quantize(woven[:], w_codes[a][:, n0:n1], w_plane[a][:, n0:n1])
 
-        words = [[part_words("parted0_0", pick_words(0, (0, 1))[:])]]
-        weave(woven[0, 0][:], raw_a0[:])
-        weave(woven[1, 0][:], raw_a1[:])
-        quantize_w(0, 0)
-        pairs = pick_words(0, (2,), AT_RAW_A0)
-        quantize_w(1, 0)
-        words[0].append(part_words("parted0_1", pairs[:]))
-        picked.append(pick_scales(1, AT_RAW_A1))
-        x_raw = load_cols("x_raw", x, 0, J)
+        pairs = [pick_words(0, H, (0, 1)), pick_words(0, H, (2,))]
+        part_words(0, H, (0, 1), pairs[0])
+        weave(woven_a0[:], raw_a0[:])
+        weave(woven_a1[:], raw_a1[:])
+        quantize_w(woven_a0, 0, 0)
+        part_words(0, H, (2,), pairs[1])
+        late_last = pick_words(H, H, (2,), AT_WOVEN_A0)
+        quantize_w(woven_a1, 1, 0)
+        weave(woven_b0[:], raw_b0[:])
+        picked.append(pick_scales(1, AT_WOVEN_A1))
         move_scales(1)
+        quantize_w(woven_b0, 0, H)
+        x_raw = load_cols("x_raw", x, 0, J, AT_X_RAW)
+        res_sb = sb("res_sb", [P, 4, J], F32)
+        nc.sync.dma_start(res_sb[:], res.rearrange("(c p) j -> p c j", p=P))
 
         iw_ps = bank_tile("iw_ps", [P, P], 7)
         nc.tensor.transpose(iw_ps[:], iw_rows[:], ident[:])
         iw_cols = sb("iw_cols", [P, 16], F32, AT_RAW_A1 + 1024)
         nc.scalar.activation(iw_cols[:], iw_ps[:, 0:16], COPY)
 
-        nc.gpsimd.tensor_copy(woven[0, 1][:], raw_b0[:].rearrange("p t c -> p c t"))
+        nc.gpsimd.tensor_copy(woven_b1[:, 0:SHARE, :], raw_b1[:, :, 0:SHARE].rearrange("p t c -> p c t"))
+        weave(woven_b1[:, SHARE:H, :], raw_b1[:, :, SHARE:H])
 
         def iw_col(g, jt):
             return iw_cols[:, 4 * g + jt : 4 * g + jt + 1]
 
-        def look_up(sums, g, jt, n0, n1, passes=(0, 1)):
+        def look_up(sums, g, jt, n0, n1, passes=(0, 1), opens=True, closes=True):
             h, u = divmod(jt, 2)
             s0 = g * H + u * P
-            c0 = g % 2 * H + u * P
             for a in passes:
                 nc.tensor.matmul_mx(
                     out=sums,
-                    lhsT=words[h][g // 2][:, a, 2 * c0 : 2 * (c0 + P)].bitcast(FP4X4),
+                    lhsT=words[g, jt][:, a, :].bitcast(FP4X4),
                     lhsT_scale=moved[h][:, a * G * H + s0 : a * G * H + s0 + P],
                     rhs=w_codes[a][:, n0:n1].bitcast(FP8X4),
                     rhs_scale=w_plane[a][:, n0:n1],
-                    start=(a == 0),
-                    stop=(a == 1),
+                    start=(a == 0 and opens),
+                    stop=(a == 1 and closes),
                 )
 
-        def turn(turned, term, c0, first, last):
-            blocks = term.shape[1] // P
-            for c in range(blocks):
+        def turn(blocks, term, first, last):
+            for c, block in enumerate(blocks):
                 nc.tensor.matmul(
-                    turned[:, c0 + c, :], term[:, c * P : (c + 1) * P], ident[:],
-                    start=(first and c == 0), stop=(last and c == blocks - 1), is_transpose=True,
+                    block, term[:, c * P : (c + 1) * P], ident[:],
+                    start=(first and c == 0), stop=(last and c == len(blocks) - 1), is_transpose=True,
                 )
 
-        turned = [bank_tile("turned%d" % u, [P, 4, P], 6 + u) for u in range(2)]
+        turned_early = []
 
-        def early_terms(s, sums, lists, offset=None):
-            held = sb("terms%d_%d" % (s, lists[0]), [P, 2 * len(lists) * H], F32, offset)
-            for i, g in enumerate(lists):
-                terms = [held[:, (2 * i + u) * H : (2 * i + u + 1) * H] for u in range(2)]
+        def early_terms(s, offset=None):
+            held = sb("terms%d" % s, [P, G, 2, H], F32, offset)
+            for g in range(G):
                 for u in range(2):
-                    nc.scalar.activation(terms[u], sums[g, u], COPY, scale=iw_col(g, u))
-                for u in range(2):
-                    turn(turned[u], terms[u], 2 * s, s == 0 and g == 1, s == 1 and g == 2)
+                    nc.scalar.activation(held[:, g, u, :], early_banks[s][g][:, u, :], COPY, scale=iw_col(g, u))
+            return held
 
-        shared = [bank_tile("first_shared%d" % u, [P, 2, H], u) for u in range(2)]
-        sums_a = {(g, u): shared[u][:, g // 2, :] for g in (0, 2) for u in range(2)}
-        for u in range(2):
-            sums_a[1, u] = bank_tile("first_alone%d" % u, [P, H], 2 + u)[:]
-        for a in range(2):
-            for g in (1, 0):
+        def turn_early(held, b):
+            bank = bank_tile("turned_early%d" % len(turned_early), [P, 2, H], b)
+            turned_early.append(bank)
+            for g in range(G):
                 for u in range(2):
-                    look_up(sums_a[g, u], g, u, 0, H, (a,))
-        for u in range(2):
-            look_up(sums_a[2, u], 2, u, 0, H)
-        early_terms(0, sums_a, (1,))
-        weave(woven[1, 1][:], raw_b1[:])
-        early_terms(0, sums_a, (0, 2), AT_TERMS_A)
-        quantize_w(0, 1)
-        quantize_w(1, 1)
-        pairs = [pick_words(1, (0, 1), AT_RAW_B1), pick_words(1, (2,), AT_RAW_B1 + 2048)]
-        words.append([part_words("parted1_%d" % i, pairs[i][:]) for i in range(2)])
-        res_sb = sb("res_sb", [P, 4, J], F32, AT_TABLE)
-        nc.sync.dma_start(res_sb[:], res.rearrange("(c p) j -> p c j", p=P))
+                    blocks = [bank[:, e, u * P : (u + 1) * P] for e in range(2)]
+                    turn(blocks, held[:, g, u, :], g == 0 and u == 0, g == G - 1 and u == 1)
 
-        tops = [sb("top0", [P, H, 4], BF16, AT_WOVEN_B1), sb("top1", [P, H, 4], BF16)]
-        for u in range(2):
-            upper = wx_raw[0][:, :, u * P : (u + 1) * P].bitcast(BF16).rearrange("p t (c e) -> p c t e", e=2)[:, :, :, 1]
-            nc.gpsimd.tensor_copy(tops[0][:, u * P : (u + 1) * P, :], upper)
-        sums_b = {}
-        for g, b in enumerate((4, 5, 2)):
-            bank = bank_tile("second%d" % g, [P, 2, H], b)
-            for u in range(2):
-                sums_b[g, u] = bank[:, u, :]
-                look_up(sums_b[g, u], g, u, H, N)
-        nc.scalar.copy(
-            tops[1][:].rearrange("p (c i) t -> p c t i", i=4),
-            wx_raw[1][:].bitcast(BF16).rearrange("p t (c i e) -> p c t i e", i=4, e=2)[:, :, :, :, 1],
-        )
-        early_terms(1, sums_b, (0, 1, 2))
+        early_banks = [[bank_tile("early%d_%d" % (s, g), [P, 2, H], G * s + g) for g in range(G)] for s in range(2)]
+
+        def early_pass(s, a):
+            for g in range(G):
+                for u in range(2):
+                    look_up(early_banks[s][g][:, u, :], g, u, s * H, (s + 1) * H, (a,), u == 0, u == 1)
+
+        early_pass(0, 0)
+        early_pass(0, 1)
+        early_pass(1, 0)
+        turn_early(early_terms(0, AT_RAW_B0), 6)
+        quantize_w(woven_b1, 1, H)
+        part_words(H, H, (2,), late_last, AT_WOVEN_B0)
+        part_words(H, H, (0, 1), pick_words(H, H, (0, 1), AT_WOVEN_A1 + 2816))
+
+        def upper(cp, c0, c1):
+            return wx_raw[cp][:, :, c0:c1].bitcast(BF16)
+
+        def copy_tops(top, cp, c0, c1):
+            nc.scalar.copy(
+                top[:, c0:c1, :].rearrange("p (c i) t -> p c t i", i=4),
+                upper(cp, c0, c1).rearrange("p t (c i e) -> p c t i e", i=4, e=2)[:, :, :, :, 1],
+            )
+
+        tops = [sb("top0", [P, H, 4], BF16, AT_WOVEN_A1 + 768), sb("top1", [P, H, 4], BF16)]
+        nc.gpsimd.tensor_copy(tops[0][:, 0:P, :], upper(0, 0, P).rearrange("p t (c e) -> p c t e", e=2)[:, :, :, 1])
+        early_pass(1, 1)
+        copy_tops(tops[0], 0, P, H)
+        copy_tops(tops[1], 1, 0, H)
+
+        late_banks = {}
+
+        def late_sums(groups, banks):
+            for (g, jt), b in zip(groups, banks):
+                late_banks[g, jt] = bank_tile("late%d_%d" % (g, jt), [P, N], b)
+                look_up(late_banks[g, jt][:], g, jt, 0, N)
 
         splits = [sb("split%d" % cp, [P, 2 * H, 4], BF16) for cp in range(2)]
-        for cp in range(2):
+
+        def mask(cp):
             nc.vector.tensor_scalar(
                 splits[cp][:, 0:H, :].rearrange("p c t -> p (c t)").bitcast(I32),
                 tops[cp][:].rearrange("p c t -> p (c t)").bitcast(I32),
                 HI_MASK, None, ALU.bitwise_and,
             )
-        for cp in range(2):
+
+        def subtract(cp):
             low, raw_lines = by_lines(splits[cp][:, H : 2 * H, :], wx_raw[cp][:])
             nc.vector.tensor_tensor(low, raw_lines, splits[cp][:, 0:H, :].rearrange("p (c i) t -> p c t i", i=4), ALU.subtract)
 
-        def late_sums(g, jt, b):
-            bank = bank_tile("late%d_%d" % (g, jt), [P, N], b)
-            look_up(bank[:], g, jt, 0, N)
-            return bank
+        second_terms = early_terms(1)
+        late_sums(((2, 2), (2, 3), (0, 2), (1, 2), (0, 3), (1, 3)), (0, 1, 2, 7, 3, 4))
+        mask(0)
+        mask(1)
+        subtract(0)
+        subtract(1)
 
-        late_banks = {(g, jt): late_sums(g, jt, b) for (g, jt), b in zip(((0, 2), (1, 2), (0, 3), (1, 3)), (3, 0, 4, 5))}
-
-        def scaled(g, jt):
-            bank = late_banks[g, jt]
-            term = sb("late_term%d_%d" % (g, jt), [P, N], F32)
-            nc.scalar.activation(term[:], bank[:], COPY, scale=iw_col(g, jt))
-            return term
-
-        def added(g, jt, earlier):
-            bank = late_banks[g, jt]
-            term = sb("late_term%d_%d" % (g, jt), [P, N], F32)
-            nc.vector.scalar_tensor_tensor(term[:], bank[:], iw_col(g, jt), earlier[:], ALU.mult, ALU.add)
-            return term
-
-        part_codes = [sb("part_codes%d" % cp, [P, 2 * H], U32) for cp in range(2)]
+        part_codes = [sb("part_codes0", [P, 2 * H], U32), sb("part_codes1", [P, 2 * H], U32, AT_X_WOVEN1)]
         part_plane = [sb("part_plane%d" % cp, [P, 2 * H], U8) for cp in range(2)]
         x_codes = [sb("x_codes%d" % h, [P, H], U32) for h in range(2)]
         x_plane = [sb("x_plane%d" % h, [P, H], U8) for h in range(2)]
-        x_woven = [sb("x_woven%d" % h, [P, H, 4], BF16, AT_X_WOVEN + 2048 * h) for h in range(2)]
-        own = sb("own", [P, 4, H], F32)
-        early = sb("early", [P, 4, H], F32)
-        early_res = sb("early_res", [P, 4, H], F32, AT_X_WOVEN)
+        x_woven = [sb("x_woven%d" % h, [P, H, 4], BF16, (AT_X_WOVEN0, AT_X_WOVEN1)[h]) for h in range(2)]
         out_rows = out.rearrange("(c p) j -> p c j", p=P)
 
         def skip(h, cp, b):
@@ -269,48 +277,74 @@ def tile_list_interp_hl_res_kernel(tc, tab_words, tab_scales, w, x, wx, iw0, iw1
                     )
             return bank
 
-        def finish_early(cp, bank, e0, e1):
-            done = sb("done_early%d_%d" % (cp, e0), [P, e1 - e0, H], F32)
-            nc.vector.tensor_tensor(done[:], bank[:, e0:e1, :], early_res[:, 2 * cp + e0 : 2 * cp + e1, :], ALU.add)
-            nc.sync.dma_start(out_rows[:, 2 * cp + e0 : 2 * cp + e1, 0:H], done[:])
+        def scaled(g, jt, offset=None):
+            term = sb("late_term%d_%d" % (g, jt), [P, N], F32, offset)
+            nc.scalar.activation(term[:], late_banks[g, jt][:], COPY, scale=iw_col(g, jt))
+            return term
 
-        def finish_late(u, sums):
-            done = sb("done_late%d" % u, [P, 4, P], F32)
+        def added(g, jt, earlier, offset=None):
+            term = sb("late_term%d_%d" % (g, jt), [P, N], F32, offset)
+            nc.vector.scalar_tensor_tensor(term[:], late_banks[g, jt][:], iw_col(g, jt), earlier[:], ALU.mult, ALU.add)
+            return term
+
+        def copy_early(cp, offset=None):
+            early = sb("early%d" % cp, [P, 2, H], F32, offset)
+            nc.scalar.activation(early[:], turned_early[cp][:], COPY)
+            return early
+
+        def add_res(cp, early, offset=None):
+            early_res = sb("early_res%d" % cp, [P, 2, H], F32, offset)
+            nc.gpsimd.tensor_tensor(early_res[:], early[:], res_sb[:, 2 * cp : 2 * cp + 2, 0:H], ALU.add)
+            return early_res
+
+        def finish_early(cp):
+            done = sb("done_early%d" % cp, [P, 2, H], F32)
+            nc.vector.tensor_tensor(done[:], ax_early[cp][:], early_res[cp][:], ALU.add)
+            nc.sync.dma_start(out_rows[:, 2 * cp : 2 * cp + 2, 0:H], done[:])
+
+        def finish_late(u, sums, offset=None):
+            done = sb("done_late%d" % u, [P, 4, P], F32, offset)
             nc.vector.tensor_tensor(done[:], sums[:], own[:, :, u * P : (u + 1) * P], ALU.add)
             nc.sync.dma_start(out_rows[:, :, H + u * P : H + (u + 1) * P], done[:])
 
+        third = [scaled(2, 2)]
+        turn_early(second_terms, 0)
+        early = [copy_early(0)]
         for h in (1, 0):
             weave(x_woven[h][:], x_raw[:, :, h * H : (h + 1) * H])
-        for u in range(2):
-            nc.scalar.activation(early[:, :, u * P : (u + 1) * P], turned[u][:], COPY)
-        third = scaled(0, 2)
-        fourth = [scaled(g, 3) for g in range(2)]
         quantize(splits[0][:], part_codes[0][:], part_plane[0][:])
         quantize(x_woven[1][:], x_codes[1][:], x_plane[1][:])
         quantize(splits[1][:], part_codes[1][:], part_plane[1][:])
         quantize(x_woven[0][:], x_codes[0][:], x_plane[0][:])
-        for cp in range(2):
-            rows = slice(2 * cp, 2 * cp + 2)
-            nc.gpsimd.tensor_tensor(early_res[:, rows, :], early[:, rows, :], res_sb[:, rows, 0:H], ALU.add)
 
-        def turn_late(u, b, terms):
-            turned.append(bank_tile("turned%d" % (2 + u), [P, 4, P], b))
-            for i, term in enumerate(terms):
-                turn(turned[2 + u], term[:], 0, i == 0, i == len(terms) - 1)
+        fourth = [scaled(2, 3, AT_X_RAW + 4096)]
+        third.append(scaled(1, 2, AT_X_RAW))
+        early.append(copy_early(1, AT_X_RAW + 2048))
+        fourth.append(scaled(0, 3, AT_X_RAW + 6144))
+        early_res = [add_res(0, early[0], AT_X_WOVEN0), add_res(1, early[1])]
 
-        third = added(1, 2, third)
-        for cp in range(2):
-            bank = skip(1, cp, 6 + cp)
-            late_banks[2, 2 + cp] = late_sums(2, 2 + cp, 1 + cp)
-            nc.vector.tensor_tensor(own[:, 2 * cp : 2 * cp + 2, :], bank[:], res_sb[:, 2 * cp : 2 * cp + 2, H:J], ALU.add)
-            if cp == 0:
-                third = added(2, 2, third)
-        fourth[0] = added(2, 3, fourth[0])
-        ax_early = skip(0, 0, 3)
-        turn_late(0, 0, [third])
-        finish_early(0, ax_early, 0, 2)
-        finish_late(0, turned[2])
-        ax_early = skip(0, 1, 4)
-        turn_late(1, 1, fourth[::-1])
-        finish_early(1, ax_early, 0, 2)
-        finish_late(1, turned[3])
+        def turn_late(turned, term, first, last):
+            turn([turned[:, c, :] for c in range(4)], term[:], first, last)
+
+        third[0] = added(0, 2, third[0])
+        turned_third = bank_tile("turned_third", [P, 4, P], 2)
+        turn_late(turned_third, third[0], True, False)
+        ax_late = [skip(1, 0, 6), skip(1, 1, 5)]
+        ax_early = [skip(0, 0, 7)]
+        turn_late(turned_third, third[1], False, True)
+        own = sb("own", [P, 4, H], F32)
+
+        def add_own(cp):
+            nc.vector.tensor_tensor(own[:, 2 * cp : 2 * cp + 2, :], ax_late[cp][:], res_sb[:, 2 * cp : 2 * cp + 2, H:J], ALU.add)
+
+        add_own(0)
+        fourth[0] = added(1, 3, fourth[0])
+        add_own(1)
+        turned_fourth = bank_tile("turned_fourth", [P, 4, P], 6)
+        turn_late(turned_fourth, fourth[0], True, False)
+        turn_late(turned_fourth, fourth[1], False, True)
+        ax_early.append(skip(0, 1, 3))
+        finish_early(0)
+        finish_late(0, turned_third)
+        finish_late(1, turned_fourth)
+        finish_early(1)

@@ -80,7 +80,7 @@ def tile_list_interp_hl_res_kernel(tc, tab_words, tab_scales, w, x, wx, iw0, iw1
         iw_rows = sb("iw_rows", [P, P], F32)
         nc.gpsimd.memset(iw_rows[:], 0.0)
         for g, iw in enumerate((iw0, iw1, iw2)):
-            nc.scalar.dma_start(iw_rows[4 * g : 4 * g + 4, :], iw.rearrange("(c j) -> c j", c=4))
+            nc.gpsimd.dma_start(iw_rows[4 * g : 4 * g + 4, :], iw.rearrange("(c j) -> c j", c=4))
         ident = sb("ident", [P, P], F32)
         make_identity(nc, ident[:])
         moved = [sb("moved%d" % h, [P, 2 * G * H], U8) for h in range(2)]
@@ -119,7 +119,11 @@ def tile_list_interp_hl_res_kernel(tc, tab_words, tab_scales, w, x, wx, iw0, iw1
         move_scales(0)
         raw_b0 = load_cols("raw_b0", w[0:512, :], H, N, AT_RAW_B0)
         raw_b1 = load_cols("raw_b1", w[512:1024, :], H, N)
-        wx_raw = [load_cols("wx_raw%d" % cp, wx, cp * H, (cp + 1) * H) for cp in range(2)]
+        wx_all = load_cols("wx_all", wx, 0, N)
+        wx_raw = [wx_all[:, :, cp * H : (cp + 1) * H] for cp in range(2)]
+        x_raw = sb("x_raw", [P, 4, J], F32, AT_X_RAW)
+        x_rows = x.rearrange("(p t) c -> p t c", t=4)
+        nc.sync.dma_start(x_raw[:, 0:2, :], x_rows[:, 0:2, :])
 
         w_codes = [sb("w_codes%d" % a, [P, N], U32) for a in range(2)]
         w_plane = [sb("w_plane%d" % a, [P, N], U8) for a in range(2)]
@@ -144,7 +148,7 @@ def tile_list_interp_hl_res_kernel(tc, tab_words, tab_scales, w, x, wx, iw0, iw1
         picked.append(pick_scales(1, AT_WOVEN_A1))
         move_scales(1)
         quantize_w(woven_b0, 0, H)
-        x_raw = load_cols("x_raw", x, 0, J, AT_X_RAW)
+        nc.sync.dma_start(x_raw[:, 2:4, :], x_rows[:, 2:4, :])
         res_sb = sb("res_sb", [P, 4, J], F32)
         nc.sync.dma_start(res_sb[:], res.rearrange("(c p) j -> p c j", p=P))
 
@@ -244,7 +248,7 @@ def tile_list_interp_hl_res_kernel(tc, tab_words, tab_scales, w, x, wx, iw0, iw1
             )
 
         def subtract(cp):
-            low, raw_lines = by_lines(splits[cp][:, H : 2 * H, :], wx_raw[cp][:])
+            low, raw_lines = by_lines(splits[cp][:, H : 2 * H, :], wx_raw[cp])
             nc.vector.tensor_tensor(low, raw_lines, splits[cp][:, 0:H, :].rearrange("p (c i) t -> p c t i", i=4), ALU.subtract)
 
         second_terms = early_terms(1)

@@ -29,6 +29,7 @@ AT_WOVEN_B0 = 2048
 AT_RAW_A1 = 4096
 AT_RAW_B0 = 8192
 AT_WOVEN_A1 = 14336
+AT_RAW_B1 = 36864
 AT_X_RAW = 21504
 AT_X_WOVEN1 = 29696
 AT_X_WOVEN0 = 32768
@@ -118,7 +119,7 @@ def tile_list_interp_hl_res_kernel(tc, tab_words, tab_scales, w, x, wx, iw0, iw1
         picked = [pick_scales(0)]
         move_scales(0)
         raw_b0 = load_cols("raw_b0", w[0:512, :], H, N, AT_RAW_B0)
-        raw_b1 = load_cols("raw_b1", w[512:1024, :], H, N)
+        raw_b1 = load_cols("raw_b1", w[512:1024, :], H, N, AT_RAW_B1)
         wx_all = load_cols("wx_all", wx, 0, N)
         wx_raw = [wx_all[:, :, cp * H : (cp + 1) * H] for cp in range(2)]
         x_raw = sb("x_raw", [P, 4, J], F32, AT_X_RAW)
@@ -186,20 +187,26 @@ def tile_list_interp_hl_res_kernel(tc, tab_words, tab_scales, w, x, wx, iw0, iw1
 
         turned_early = []
 
-        def early_terms(s, offset=None):
-            held = sb("terms%d" % s, [P, G, 2, H], F32, offset)
-            for g in range(G):
+        def early_terms(s, lists, offset=None):
+            held = sb("terms%d" % s, [P, len(lists), 2, H], F32, offset)
+            for g in lists:
                 for u in range(2):
                     nc.scalar.activation(held[:, g, u, :], early_banks[s][g][:, u, :], COPY, scale=iw_col(g, u))
-            return held
+            return [held[:, g, :, :] for g in lists]
+
+        def early_added(s, g, earlier, offset):
+            terms = sb("added%d" % s, [P, 2, H], F32, offset)
+            for u in range(2):
+                nc.vector.scalar_tensor_tensor(terms[:, u, :], early_banks[s][g][:, u, :], iw_col(g, u), earlier[:, u, :], ALU.mult, ALU.add)
+            return terms[:]
 
         def turn_early(held, b):
             bank = bank_tile("turned_early%d" % len(turned_early), [P, 2, H], b)
             turned_early.append(bank)
-            for g in range(G):
+            for i, terms in enumerate(held):
                 for u in range(2):
                     blocks = [bank[:, e, u * P : (u + 1) * P] for e in range(2)]
-                    turn(blocks, held[:, g, u, :], g == 0 and u == 0, g == G - 1 and u == 1)
+                    turn(blocks, terms[:, u, :], i == 0 and u == 0, i == len(held) - 1 and u == 1)
 
         early_banks = [[bank_tile("early%d_%d" % (s, g), [P, 2, H], G * s + g) for g in range(G)] for s in range(2)]
 
@@ -211,10 +218,12 @@ def tile_list_interp_hl_res_kernel(tc, tab_words, tab_scales, w, x, wx, iw0, iw1
         early_pass(0, 0)
         early_pass(0, 1)
         early_pass(1, 0)
-        turn_early(early_terms(0, AT_RAW_B0), 6)
+        first_terms = early_terms(0, (0, 1), AT_RAW_B0)
         quantize_w(woven_b1, 1, H)
         part_words(H, H, (2,), late_last, AT_WOVEN_B0)
-        part_words(H, H, (0, 1), pick_words(H, H, (0, 1), AT_WOVEN_A1 + 2816))
+        late_first = pick_words(H, H, (0, 1), AT_RAW_B1)
+        turn_early([first_terms[1], early_added(0, 2, first_terms[0], AT_WOVEN_A1 + 2816)], 6)
+        part_words(H, H, (0, 1), late_first)
 
         def upper(cp, c0, c1):
             return wx_raw[cp][:, :, c0:c1].bitcast(BF16)
@@ -226,9 +235,9 @@ def tile_list_interp_hl_res_kernel(tc, tab_words, tab_scales, w, x, wx, iw0, iw1
             )
 
         tops = [sb("top0", [P, H, 4], BF16, AT_WOVEN_A1 + 768), sb("top1", [P, H, 4], BF16)]
-        nc.gpsimd.tensor_copy(tops[0][:, 0:P, :], upper(0, 0, P).rearrange("p t (c e) -> p c t e", e=2)[:, :, :, 1])
+        for c0 in (0, P):
+            nc.gpsimd.tensor_copy(tops[0][:, c0 : c0 + P, :], upper(0, c0, c0 + P).rearrange("p t (c e) -> p c t e", e=2)[:, :, :, 1])
         early_pass(1, 1)
-        copy_tops(tops[0], 0, P, H)
         copy_tops(tops[1], 1, 0, H)
 
         late_banks = {}
@@ -251,7 +260,7 @@ def tile_list_interp_hl_res_kernel(tc, tab_words, tab_scales, w, x, wx, iw0, iw1
             low, raw_lines = by_lines(splits[cp][:, H : 2 * H, :], wx_raw[cp])
             nc.vector.tensor_tensor(low, raw_lines, splits[cp][:, 0:H, :].rearrange("p (c i) t -> p c t i", i=4), ALU.subtract)
 
-        second_terms = early_terms(1)
+        second_terms = early_terms(1, (0, 1, 2))
         late_sums(((2, 2), (2, 3), (0, 2), (1, 2), (0, 3), (1, 3)), (0, 1, 2, 7, 3, 4))
         mask(0)
         mask(1)

@@ -310,15 +310,16 @@ def tile_list_interp_hl_res_kernel(tc, tab_words, tab_scales, w, x, wx, iw0, iw1
             nc.gpsimd.tensor_tensor(early_res[:], early[:], res_sb[:, 2 * cp : 2 * cp + 2, 0:H], ALU.add)
             return early_res
 
-        def finish_early(cp):
-            done = sb("done_early%d" % cp, [P, 2, H], F32)
-            nc.vector.tensor_tensor(done[:], ax_early[cp][:], early_res[cp][:], ALU.add)
-            nc.sync.dma_start(out_rows[:, 2 * cp : 2 * cp + 2, 0:H], done[:])
+        def finish_early(c0, c1):
+            cp, e = divmod(c0, 2)
+            done = sb("done_early%d" % c0, [P, c1 - c0, H], F32)
+            nc.vector.tensor_tensor(done[:], ax_early[cp][:, e : e + c1 - c0, :], early_res[cp][:, e : e + c1 - c0, :], ALU.add)
+            nc.sync.dma_start(out_rows[:, c0:c1, 0:H], done[:])
 
-        def finish_late(u, sums, offset=None):
-            done = sb("done_late%d" % u, [P, 4, P], F32, offset)
-            nc.vector.tensor_tensor(done[:], sums[:], own[:, :, u * P : (u + 1) * P], ALU.add)
-            nc.sync.dma_start(out_rows[:, :, H + u * P : H + (u + 1) * P], done[:])
+        def finish_late(cp):
+            done = sb("done_late%d" % cp, [P, 2, H], F32)
+            nc.vector.tensor_tensor(done[:], turned_late[cp][:], own[:, 2 * cp : 2 * cp + 2, :], ALU.add)
+            nc.sync.dma_start(out_rows[:, 2 * cp : 2 * cp + 2, H:J], done[:])
 
         third = [scaled(2, 2)]
         turn_early(second_terms, 0)
@@ -336,15 +337,18 @@ def tile_list_interp_hl_res_kernel(tc, tab_words, tab_scales, w, x, wx, iw0, iw1
         fourth.append(scaled(0, 3, AT_X_RAW + 6144))
         early_res = [add_res(0, early[0], AT_X_WOVEN0), add_res(1, early[1])]
 
-        def turn_late(turned, term, first, last):
-            turn([turned[:, c, :] for c in range(4)], term[:], first, last)
-
         third[0] = added(0, 2, third[0])
-        turned_third = bank_tile("turned_third", [P, 4, P], 2)
-        turn_late(turned_third, third[0], True, False)
-        ax_late = [skip(1, 0, 6), skip(1, 1, 5)]
+        turned_late = [bank_tile("turned_late%d" % cp, [P, 2, H], b) for cp, b in enumerate((2, 5))]
+
+        def turn_late(u, term, first, last):
+            for cp in range(2):
+                blocks = [turned_late[cp][:, e, u * P : (u + 1) * P] for e in range(2)]
+                turn(blocks, term[:, cp * H : (cp + 1) * H], first, last)
+
+        turn_late(0, third[0], True, False)
+        ax_late = [skip(1, 0, 6), skip(1, 1, 1)]
         ax_early = [skip(0, 0, 7)]
-        turn_late(turned_third, third[1], False, True)
+        turn_late(0, third[1], False, False)
         own = sb("own", [P, 4, H], F32)
 
         def add_own(cp):
@@ -353,11 +357,11 @@ def tile_list_interp_hl_res_kernel(tc, tab_words, tab_scales, w, x, wx, iw0, iw1
         add_own(0)
         fourth[0] = added(1, 3, fourth[0])
         add_own(1)
-        turned_fourth = bank_tile("turned_fourth", [P, 4, P], 6)
-        turn_late(turned_fourth, fourth[0], True, False)
-        turn_late(turned_fourth, fourth[1], False, True)
+        turn_late(1, fourth[0], False, False)
+        turn_late(1, fourth[1], False, True)
         ax_early.append(skip(0, 1, 3))
-        finish_early(0)
-        finish_late(0, turned_third)
-        finish_late(1, turned_fourth)
-        finish_early(1)
+        finish_early(0, 2)
+        finish_late(0)
+        finish_late(1)
+        finish_early(2, 3)
+        finish_early(3, 4)

@@ -29,7 +29,6 @@ AT_WOVEN_B0 = 2048
 AT_RAW_A1 = 4096
 AT_RAW_B0 = 8192
 AT_WOVEN_A1 = 14336
-AT_RAW_B1 = 36864
 AT_X_RAW = 21504
 AT_X_WOVEN1 = 29696
 AT_X_WOVEN0 = 32768
@@ -119,7 +118,7 @@ def tile_list_interp_hl_res_kernel(tc, tab_words, tab_scales, w, x, wx, iw0, iw1
         picked = [pick_scales(0)]
         move_scales(0)
         raw_b0 = load_cols("raw_b0", w[0:512, :], H, N, AT_RAW_B0)
-        raw_b1 = load_cols("raw_b1", w[512:1024, :], H, N, AT_RAW_B1)
+        raw_b1 = load_cols("raw_b1", w[512:1024, :], H, N)
         wx_all = load_cols("wx_all", wx, 0, N)
         wx_raw = [wx_all[:, :, cp * H : (cp + 1) * H] for cp in range(2)]
         x_raw = sb("x_raw", [P, 4, J], F32, AT_X_RAW)
@@ -187,18 +186,12 @@ def tile_list_interp_hl_res_kernel(tc, tab_words, tab_scales, w, x, wx, iw0, iw1
 
         turned_early = []
 
-        def early_terms(s, lists, offset=None):
-            held = sb("terms%d" % s, [P, len(lists), 2, H], F32, offset)
-            for g in lists:
+        def early_terms(s, offset=None):
+            held = sb("terms%d" % s, [P, G, 2, H], F32, offset)
+            for g in range(G):
                 for u in range(2):
                     nc.scalar.activation(held[:, g, u, :], early_banks[s][g][:, u, :], COPY, scale=iw_col(g, u))
-            return [held[:, g, :, :] for g in lists]
-
-        def early_added(s, g, earlier, offset):
-            terms = sb("added%d" % s, [P, 2, H], F32, offset)
-            for u in range(2):
-                nc.vector.scalar_tensor_tensor(terms[:, u, :], early_banks[s][g][:, u, :], iw_col(g, u), earlier[:, u, :], ALU.mult, ALU.add)
-            return terms[:]
+            return [held[:, g, :, :] for g in range(G)]
 
         def turn_early(held, b):
             bank = bank_tile("turned_early%d" % len(turned_early), [P, 2, H], b)
@@ -218,12 +211,10 @@ def tile_list_interp_hl_res_kernel(tc, tab_words, tab_scales, w, x, wx, iw0, iw1
         early_pass(0, 0)
         early_pass(0, 1)
         early_pass(1, 0)
-        first_terms = early_terms(0, (0, 1), AT_RAW_B0)
+        turn_early(early_terms(0, AT_RAW_B0), 6)
         quantize_w(woven_b1, 1, H)
         part_words(H, H, (2,), late_last, AT_WOVEN_B0)
-        late_first = pick_words(H, H, (0, 1), AT_RAW_B1)
-        turn_early([first_terms[1], early_added(0, 2, first_terms[0], AT_WOVEN_A1 + 2816)], 6)
-        part_words(H, H, (0, 1), late_first)
+        part_words(H, H, (0, 1), pick_words(H, H, (0, 1), AT_WOVEN_A1 + 2816))
 
         def upper(cp, c0, c1):
             return wx_raw[cp][:, :, c0:c1].bitcast(BF16)
@@ -260,7 +251,7 @@ def tile_list_interp_hl_res_kernel(tc, tab_words, tab_scales, w, x, wx, iw0, iw1
             low, raw_lines = by_lines(splits[cp][:, H : 2 * H, :], wx_raw[cp])
             nc.vector.tensor_tensor(low, raw_lines, splits[cp][:, 0:H, :].rearrange("p (c i) t -> p c t i", i=4), ALU.subtract)
 
-        second_terms = early_terms(1, (0, 1, 2))
+        second_terms = early_terms(1)
         late_sums(((2, 2), (2, 3), (0, 2), (1, 2), (0, 3), (1, 3)), (0, 1, 2, 7, 3, 4))
         mask(0)
         mask(1)

from contextlib import ExitStack

import concourse.mybir as mybir
from concourse.masks import make_identity

K, L, N, T, J = 1024, 512, 512, 2048, 512
G = 3
FLOPS = 2 * N * J * (G * K + 2 * L)

F32 = mybir.dt.float32
BF16 = mybir.dt.bfloat16
I32 = mybir.dt.int32
U32 = mybir.dt.uint32
U16 = mybir.dt.uint16
U8 = mybir.dt.uint8
FP8X4 = mybir.dt.float8_e4m3fn_x4
FP4X4 = mybir.dt.float4_e2m1fn_x4
ALU = mybir.AluOpType
COPY = mybir.ActivationFunctionType.Copy

P = 128
H = 256
HI_MASK = -983056

SHARE = 160

AT_WOVEN_A0 = 0
AT_WOVEN_B0 = 2048
AT_RAW_A1 = 4096
AT_RAW_B0 = 8192
AT_WOVEN_A1 = 14336
AT_X_RAW = 21504
AT_X_WOVEN1 = 29696
AT_X_WOVEN0 = 32768


def tile_list_interp_hl_res_kernel(tc, tab_words, tab_scales, w, x, wx, iw0, iw1, iw2, res, offs, out):
    nc = tc.nc
    with ExitStack() as ctx:
        keep = ctx.enter_context(tc.tile_pool(name="keep", bufs=1))
        placed = ctx.enter_context(tc.tile_pool(name="placed", bufs=1))
        psum = ctx.enter_context(tc.psum_pool(name="psum", bufs=1))

        def sb(name, shape, dtype, offset=None):
            if offset is None:
                return keep.tile(shape, dtype, name=name, align_bytes=64)
            return placed.tile(shape, dtype, name=name, offset=offset, align_bytes=64)

        def load_cols(name, rows, c0, c1, offset=None):
            raw = sb(name, [P, 4, c1 - c0], F32, offset)
            nc.sync.dma_start(raw[:], rows.rearrange("(p t) c -> p t c", t=4)[:, :, c0:c1])
            return raw

        def bank_tile(name, shape, b):
            return psum.tile(shape, F32, name=name, tag="bank%d" % b)

        def by_lines(woven, raw_cols):
            return woven.rearrange("p (c i) t -> p c t i", i=4), raw_cols.rearrange("p t (c i) -> p c t i", i=4)

        def weave(woven, raw_cols):
            nc.scalar.activation(*by_lines(woven, raw_cols), COPY)

        def quantize(woven, codes, plane):
            nc.vector.quantize_mx(out=codes.bitcast(FP8X4), scales=plane, in_=woven.rearrange("p c t -> p (c t)"))

        def listed(g, j0, count):
            c0 = (g * J + j0) // 16
            return offsets[:, c0 : c0 + count // 16]

        offsets = keep.tile([P, G * J // 16], U16, name="offsets")
        nc.sync.dma_start(offsets[:], offs)

        scale_tab = sb("scale_tab", [P, T], U8)
        nc.sync.dma_start(scale_tab[0:32, :].bitcast(I32), tab_scales.rearrange("a q t -> q a t").bitcast(I32))
        for p0, p1 in ((32, 64), (64, 128)):
            nc.vector.memset(scale_tab[p0:p1, :].bitcast(I32), 0)
        word_tab = sb("word_tab", [P, T], I32)
        nc.sync.dma_start(word_tab[:], tab_words[0].rearrange("p t b -> p (t b)").bitcast(I32))

        iw_rows = sb("iw_rows", [P, P], F32)
        nc.gpsimd.memset(iw_rows[:], 0.0)
        for g, iw in enumerate((iw0, iw1, iw2)):
            nc.gpsimd.dma_start(iw_rows[4 * g : 4 * g + 4, :], iw.rearrange("(c j) -> c j", c=4))
        ident = sb("ident", [P, P], F32)
        make_identity(nc, ident[:])
        moved = [sb("moved%d" % h, [P, 2 * G * H], U8) for h in range(2)]
        nc.vector.memset(moved[0][:].bitcast(I32), 0)
        nc.gpsimd.memset(moved[1][:].bitcast(I32), 0)

        raw_a0 = load_cols("raw_a0", w[0:512, :], 0, H)
        raw_a1 = load_cols("raw_a1", w[512:1024, :], 0, H, AT_RAW_A1)

        def pick_scales(h, offset=None):
            picked = sb("picked%d" % h, [P, G * H], U8, offset)
            for g in range(G):
                nc.vector.tensor_copy(picked[:, g * H : (g + 1) * H], scale_tab[:].indirect(listed(g, h * H, H)))
            return picked

        def move_scales(h):
            for q in range(4):
                nc.sync.dma_start(moved[h][32 * q : 32 * q + 4, :].bitcast(I32), picked[h][8 * q : 8 * q + 8, :].bitcast(I32))

        def pick_words(j0, count, lists, offset=None):
            pairs = sb("pairs%d_%d" % (j0, lists[0]), [P, len(lists) * count], U32, offset)
            for i, g in enumerate(lists):
                nc.vector.tensor_copy(pairs[:, i * count : (i + 1) * count], word_tab[:].bitcast(U32).indirect(listed(g, j0, count)))
            return pairs

        words = {}

        def part_words(j0, count, lists, pairs, offset=None):
            parted = sb("parted%d_%d" % (j0, lists[0]), [P, 2, 2 * len(lists) * count], U8, offset)
            nc.vector.tensor_copy(parted[:].bitcast(U16), pairs[:].bitcast(U16).rearrange("p (j d) -> p d j", d=2))
            for i, g in enumerate(lists):
                for c in range(0, count, P):
                    words[g, (j0 + c) // P] = parted[:, :, 2 * (i * count + c) : 2 * (i * count + c + P)]

        picked = [pick_scales(0)]
        move_scales(0)
        raw_b0 = load_cols("raw_b0", w[0:512, :], H, N, AT_RAW_B0)
        raw_b1 = load_cols("raw_b1", w[512:1024, :], H, N)
        wx_all = load_cols("wx_all", wx, 0, N)
        wx_raw = [wx_all[:, :, cp * H : (cp + 1) * H] for cp in range(2)]
        x_raw = sb("x_raw", [P, 4, J], F32, AT_X_RAW)
        x_rows = x.rearrange("(p t) c -> p t c", t=4)
        nc.sync.dma_start(x_raw[:, 0:2, :], x_rows[:, 0:2, :])

        w_codes = [sb("w_codes%d" % a, [P, N], U32) for a in range(2)]
        w_plane = [sb("w_plane%d" % a, [P, N], U8) for a in range(2)]
        woven_a0 = sb("woven_a0", [P, H, 4], BF16, AT_WOVEN_A0)
        woven_a1 = sb("woven_a1", [P, H, 4], BF16, AT_WOVEN_A1)
        woven_b0 = sb("woven_b0", [P, H, 4], BF16, AT_WOVEN_B0)
        woven_b1 = sb("woven_b1", [P, H, 4], BF16, AT_WOVEN_A1 + 1024)

        def quantize_w(woven, a, n0):
            n1 = n0 + woven.shape[1]
            quantize(woven[:], w_codes[a][:, n0:n1], w_plane[a][:, n0:n1])

        pairs = [pick_words(0, H, (0, 1)), pick_words(0, H, (2,))]
        part_words(0, H, (0, 1), pairs[0])
        weave(woven_a0[:], raw_a0[:])
        weave(woven_a1[:], raw_a1[:])
        quantize_w(woven_a0, 0, 0)
        part_words(0, H, (2,), pairs[1])
        late_last = pick_words(H, H, (2,), AT_WOVEN_A0)
        quantize_w(woven_a1, 1, 0)
        weave(woven_b0[:], raw_b0[:])
        picked.append(pick_scales(1, AT_WOVEN_A1))
        move_scales(1)
        quantize_w(woven_b0, 0, H)
        nc.sync.dma_start(x_raw[:, 2:4, :], x_rows[:, 2:4, :])
        res_sb = sb("res_sb", [P, 4, J], F32)
        nc.sync.dma_start(res_sb[:], res.rearrange("(c p) j -> p c j", p=P))

        iw_ps = bank_tile("iw_ps", [P, P], 7)
        nc.tensor.transpose(iw_ps[:], iw_rows[:], ident[:])
        iw_cols = sb("iw_cols", [P, 16], F32, AT_RAW_A1 + 1024)
        nc.scalar.activation(iw_cols[:], iw_ps[:, 0:16], COPY)

        nc.gpsimd.tensor_copy(woven_b1[:, 0:SHARE, :], raw_b1[:, :, 0:SHARE].rearrange("p t c -> p c t"))
        weave(woven_b1[:, SHARE:H, :], raw_b1[:, :, SHARE:H])

        def iw_col(g, jt):
            return iw_cols[:, 4 * g + jt : 4 * g + jt + 1]

        def look_up(sums, g, jt, n0, n1, passes=(0, 1), opens=True, closes=True):
            h, u = divmod(jt, 2)
            s0 = g * H + u * P
            for a in passes:
                nc.tensor.matmul_mx(
                    out=sums,
                    lhsT=words[g, jt][:, a, :].bitcast(FP4X4),
                    lhsT_scale=moved[h][:, a * G * H + s0 : a * G * H + s0 + P],
                    rhs=w_codes[a][:, n0:n1].bitcast(FP8X4),
                    rhs_scale=w_plane[a][:, n0:n1],
                    start=(a == 0 and opens),
                    stop=(a == 1 and closes),
                )

        def turn(blocks, term, first, last):
            for c, block in enumerate(blocks):
                nc.tensor.matmul(
                    block, term[:, c * P : (c + 1) * P], ident[:],
                    start=(first and c == 0), stop=(last and c == len(blocks) - 1), is_transpose=True,
                )

        turned_early = []

        def early_terms(s, offset=None):
            held = sb("terms%d" % s, [P, G, 2, H], F32, offset)
            for g in range(G):
                for u in range(2):
                    nc.scalar.activation(held[:, g, u, :], early_banks[s][g][:, u, :], COPY, scale=iw_col(g, u))
            return [held[:, g, :, :] for g in range(G)]

        def turn_early(held, b):
            bank = bank_tile("turned_early%d" % len(turned_early), [P, 2, H], b)
            turned_early.append(bank)
            for i, terms in enumerate(held):
                for u in range(2):
                    blocks = [bank[:, e, u * P : (u + 1) * P] for e in range(2)]
                    turn(blocks, terms[:, u, :], i == 0 and u == 0, i == len(held) - 1 and u == 1)

        early_banks = [[bank_tile("early%d_%d" % (s, g), [P, 2, H], G * s + g) for g in range(G)] for s in range(2)]

        def early_pass(s, a):
            for g in range(G):
                for u in range(2):
                    look_up(early_banks[s][g][:, u, :], g, u, s * H, (s + 1) * H, (a,), u == 0, u == 1)

        early_pass(0, 0)
        early_pass(0, 1)
        early_pass(1, 0)
        turn_early(early_terms(0, AT_RAW_B0), 6)
        quantize_w(woven_b1, 1, H)
        part_words(H, H, (2,), late_last, AT_WOVEN_B0)
        part_words(H, H, (0, 1), pick_words(H, H, (0, 1), AT_WOVEN_A1 + 2816))

        def upper(cp, c0, c1):
            return wx_raw[cp][:, :, c0:c1].bitcast(BF16)

        def copy_tops(top, cp, c0, c1):
            nc.scalar.copy(
                top[:, c0:c1, :].rearrange("p (c i) t -> p c t i", i=4),
                upper(cp, c0, c1).rearrange("p t (c i e) -> p c t i e", i=4, e=2)[:, :, :, :, 1],
            )

        tops = [sb("top0", [P, H, 4], BF16, AT_WOVEN_A1 + 768), sb("top1", [P, H, 4], BF16)]
        for c0 in (0, P):
            nc.gpsimd.tensor_copy(tops[0][:, c0 : c0 + P, :], upper(0, c0, c0 + P).rearrange("p t (c e) -> p c t e", e=2)[:, :, :, 1])
        early_pass(1, 1)
        copy_tops(tops[1], 1, 0, H)

        late_banks = {}

        def late_sums(groups, banks):
            for (g, jt), b in zip(groups, banks):
                late_banks[g, jt] = bank_tile("late%d_%d" % (g, jt), [P, N], b)
                look_up(late_banks[g, jt][:], g, jt, 0, N)

        splits = [sb("split%d" % cp, [P, 2 * H, 4], BF16) for cp in range(2)]

        def mask(cp):
            nc.vector.tensor_scalar(
                splits[cp][:, 0:H, :].rearrange("p c t -> p (c t)").bitcast(I32),
                tops[cp][:].rearrange("p c t -> p (c t)").bitcast(I32),
                HI_MASK, None, ALU.bitwise_and,
            )

        def subtract(cp):
            low, raw_lines = by_lines(splits[cp][:, H : 2 * H, :], wx_raw[cp])
            nc.vector.tensor_tensor(low, raw_lines, splits[cp][:, 0:H, :].rearrange("p (c i) t -> p c t i", i=4), ALU.subtract)

        second_terms = early_terms(1)
        late_sums(((2, 2), (2, 3), (0, 2), (1, 2), (0, 3), (1, 3)), (0, 1, 2, 7, 3, 4))
        mask(0)
        mask(1)
        subtract(0)
        subtract(1)

        part_codes = [sb("part_codes0", [P, 2 * H], U32), sb("part_codes1", [P, 2 * H], U32, AT_X_WOVEN1)]
        part_plane = [sb("part_plane%d" % cp, [P, 2 * H], U8) for cp in range(2)]
        x_codes = [sb("x_codes%d" % h, [P, H], U32) for h in range(2)]
        x_plane = [sb("x_plane%d" % h, [P, H], U8) for h in range(2)]
        x_woven = [sb("x_woven%d" % h, [P, H, 4], BF16, (AT_X_WOVEN0, AT_X_WOVEN1)[h]) for h in range(2)]
        out_rows = out.rearrange("(c p) j -> p c j", p=P)

        def skip(h, cp, b):
            bank = bank_tile("ax%d_%d" % (h, cp), [P, 2, H], b)
            for e in range(2):
                for s in range(2):
                    c0 = s * H + e * P
                    nc.tensor.matmul_mx(
                        out=bank[:, e, :],
                        lhsT=part_codes[cp][:, c0 : c0 + P].bitcast(FP8X4),
                        lhsT_scale=part_plane[cp][:, c0 : c0 + P],
                        rhs=x_codes[h][:].bitcast(FP8X4),
                        rhs_scale=x_plane[h][:],
                        start=(s == 0),
                        stop=(s == 1),
                    )
            return bank

        def scaled(g, jt, offset=None):
            term = sb("late_term%d_%d" % (g, jt), [P, N], F32, offset)
            nc.scalar.activation(term[:], late_banks[g, jt][:], COPY, scale=iw_col(g, jt))
            return term

        def added(g, jt, earlier, offset=None):
            term = sb("late_term%d_%d" % (g, jt), [P, N], F32, offset)
            nc.vector.scalar_tensor_tensor(term[:], late_banks[g, jt][:], iw_col(g, jt), earlier[:], ALU.mult, ALU.add)
            return term

        def copy_early(cp, offset=None):
            early = sb("early%d" % cp, [P, 2, H], F32, offset)
            nc.scalar.activation(early[:], turned_early[cp][:], COPY)
            return early

        def add_res(cp, early, offset=None):
            early_res = sb("early_res%d" % cp, [P, 2, H], F32, offset)
            nc.gpsimd.tensor_tensor(early_res[:], early[:], res_sb[:, 2 * cp : 2 * cp + 2, 0:H], ALU.add)
            return early_res

        def finish_early(c0, c1):
            cp, e = divmod(c0, 2)
            done = sb("done_early%d" % c0, [P, c1 - c0, H], F32)
            nc.vector.tensor_tensor(done[:], ax_early[cp][:, e : e + c1 - c0, :], early_res[cp][:, e : e + c1 - c0, :], ALU.add)
            nc.sync.dma_start(out_rows[:, c0:c1, 0:H], done[:])

        def finish_late(cp):
            done = sb("done_late%d" % cp, [P, 2, H], F32)
            nc.vector.tensor_tensor(done[:], turned_late[cp][:], own[:, 2 * cp : 2 * cp + 2, :], ALU.add)
            nc.sync.dma_start(out_rows[:, 2 * cp : 2 * cp + 2, H:J], done[:])

        third = [scaled(2, 2)]
        turn_early(second_terms, 0)
        early = [copy_early(0)]
        for h in (1, 0):
            weave(x_woven[h][:], x_raw[:, :, h * H : (h + 1) * H])
        quantize(splits[0][:], part_codes[0][:], part_plane[0][:])
        quantize(x_woven[1][:], x_codes[1][:], x_plane[1][:])
        quantize(splits[1][:], part_codes[1][:], part_plane[1][:])
        quantize(x_woven[0][:], x_codes[0][:], x_plane[0][:])

        fourth = [scaled(2, 3, AT_X_RAW + 4096)]
        third.append(scaled(1, 2, AT_X_RAW))
        early.append(copy_early(1, AT_X_RAW + 2048))
        fourth.append(scaled(0, 3, AT_X_RAW + 6144))
        early_res = [add_res(0, early[0], AT_X_WOVEN0), add_res(1, early[1])]

        third[0] = added(0, 2, third[0])
        turned_late = [bank_tile("turned_late%d" % cp, [P, 2, H], b) for cp, b in enumerate((2, 5))]

        def turn_late(u, term, first, last):
            for cp in range(2):
                blocks = [turned_late[cp][:, e, u * P : (u + 1) * P] for e in range(2)]
                turn(blocks, term[:, cp * H : (cp + 1) * H], first, last)

        turn_late(0, third[0], True, False)
        ax_late = [skip(1, 0, 6), skip(1, 1, 1)]
        ax_early = [skip(0, 0, 7)]
        turn_late(0, third[1], False, False)
        own = sb("own", [P, 4, H], F32)

        def add_own(cp):
            nc.vector.tensor_tensor(own[:, 2 * cp : 2 * cp + 2, :], ax_late[cp][:], res_sb[:, 2 * cp : 2 * cp + 2, H:J], ALU.add)

        add_own(0)
        fourth[0] = added(1, 3, fourth[0])
        add_own(1)
        turn_late(1, fourth[0], False, False)
        turn_late(1, fourth[1], False, True)
        ax_early.append(skip(0, 1, 3))
        finish_early(0, 2)
        finish_late(0)
        finish_late(1)
        finish_early(2, 3)
        finish_early(3, 4)
